import numpy as np, ml_dtypes
CORES = [3,7,11,15,131,135,139,143]
N = 8
import mx_ref
BF = ml_dtypes.bfloat16
def gentries(a):
    return np.ascontiguousarray(a.reshape(8, 16, -1).transpose(0, 2, 1)).reshape(8, -1)
def gtable(e):
    e = np.asarray(e); return np.ascontiguousarray(e.reshape(8, -1, 16).transpose(0, 2, 1)).reshape(128, -1).astype(np.int32)
def gcols(t, e):
    v = np.concatenate([t.reshape(8, 16, -1, 4), np.zeros((8, 16, 1, 4), BF)], axis=2)
    return np.ascontiguousarray(np.stack([v[g][:, e[g]] for g in range(8)])).reshape(128, -1)
def tile(rs):
    return np.stack(rs, axis=2).reshape(128, -1).astype(BF)
def pick(q, e):
    c = np.concatenate([q[0].reshape(128, -1, 4), np.zeros((128, 1, 4), np.uint8)], axis=1); s = np.concatenate([q[1], np.ones((16, 1), np.uint8)], axis=1)
    return (np.ascontiguousarray(c[:, e].reshape(128, -1)), np.ascontiguousarray(s[:, e]))
def join(*qs):
    return (np.concatenate([q[0] for q in qs], axis=1), np.concatenate([q[1] for q in qs], axis=1))
def put(q, e, v):
    c, s = q[0].reshape(128, -1, 4).copy(), q[1].copy(); c[:, e] = v[0].reshape(128, -1, 4); s[:, e] = v[1]
    return (c.reshape(128, -1), s)
def pk(c, s):
    return (np.ascontiguousarray(c), mx_ref.live(s))
def emit(q):
    return q[0], q[1]
def packed(v, rng):
    q = [mx_ref.quantize(np.ascontiguousarray(v[r])) for r in range(N)]
    return np.stack([a for a, b in q]), np.stack([mx_ref.plane(b, rng) for a, b in q])
def values_of_codes():
    e, c = np.zeros((128, 128, 4), np.float32), np.zeros((128, 2, 4), np.uint8)
    e[np.arange(128), np.arange(128), 0] = 1
    c[:127, :, 0] = np.arange(256).reshape(2, 128).T[:127]
    return mx_ref.matmul(mx_ref.quantize(e.reshape(128, 512).astype(BF)), (c.reshape(128, 8), np.full((16, 2), 127, np.uint8))).T.reshape(-1).astype(np.float64)
CODE_VALUE, SCALE_VALUE = values_of_codes(), 2.0 ** (np.arange(256) - 127.0)
def decode(q):
    return (CODE_VALUE[q[0]].reshape(16, 8, -1, 4) * SCALE_VALUE[q[1]][:, None, :, None] + 0.0).reshape(128, -1).astype(np.float32)
def f(rng, *shape):
    return mx_ref.flush((rng.standard_normal(shape, dtype=np.float32) * np.exp2(rng.integers(-2, 3, shape[:-1] + (1,)))).astype(BF))
def wide(rng, *shape, cols=0):
    v = rng.standard_normal(shape, dtype=np.float32) * np.exp2(rng.integers(-12, 13, shape)).astype(np.float32)
    if cols: v *= np.repeat(np.exp2(rng.integers(-cols, cols + 1, shape[:-2] + (1, shape[-1] // 4))) * (rng.random(shape[:-2] + (1, shape[-1] // 4)) > 0.0625), 4, axis=-1).astype(np.float32)
    return mx_ref.flush(v.astype(BF))
C = 288
STEP = [2, 4, 1]
GAPS = [[2, 4, 5, 6, 7, 8], [3, 4, 5, 6, 7, 8]]
def numbers_of(rng):
    return {"x": np.array(f(rng, N, 128, 4 * C)), "u": np.array(f(rng, N, 128, 512)), "v": np.array(f(rng, N, 128, 512))}
def full(rng, k):
    h = 128 + rng.permutation(128)[:k]
    low = rng.permutation(np.concatenate([2 * h, 2 * h + 1]))[:C - 127 - k]
    return np.sort(np.concatenate([np.arange(1, 128), h, low]))
def below(h):
    return np.concatenate([np.arange(h << n, (h + 1) << n) for n in range(10 - h.bit_length())])
def lean(side, slot):
    c = 3 - side
    return np.sort(np.concatenate([[1], below(2 + side), np.concatenate([[c], below(2 * c + slot)])[:C - 256]]))
def ragged(rng, first):
    cuts, left = [], 511 - C
    for n, most in [(n, 1) for n in first] + [(n, 9) for n in range(3, 9)]:
        size = 2 ** (9 - n) - 1
        k = min(most, left // size)
        cuts += [n] * k
        left -= k * size
    keep = np.arange(512) > 0
    for n in sorted(cuts):
        h = np.arange(2 ** n, 2 ** (n + 1))
        h = int(rng.choice(h[keep[h] & keep[h ^ 1]]))
        keep[below(h)] = False
    return np.flatnonzero(keep)
def grown(h, places):
    at = np.zeros(512, np.int64)
    at[h] = places
    e = np.zeros(C, np.int64)
    e[places[1:]] = 2 * at[h[1:] >> 1] + (h[1:] & 1)
    return e
def shuffled(rng):
    return np.concatenate([[0], 1 + rng.permutation(C - 1)])
def trees(rng):
    t = np.stack([np.stack([grown(full(rng, int(rng.integers(112, 129))), shuffled(rng)) for g in range(8)]) for r in range(N)])
    o = rng.permutation(8)
    for r in range(N):
        for n in range(2): t[r, o[(r + 4 * n) % 8]] = grown(ragged(rng, GAPS[n]), shuffled(rng))
    return t
def stored(t):
    return {"se": np.stack([gtable(t[r]) for r in range(N)])}
def weights(rng, w):
    c, s = packed(np.ascontiguousarray(w).reshape(N, 128, 2048), rng)
    return {"wc": c, "ws": s}
def layers(rng, still=[], pairs=False):
    w = np.array(f(rng, N, 128, 2048)).reshape(N, 8, 16, 4, 8, 16, 4)
    for i in still:
        w[:, :, i] = 0
        w[:, :, :, :, :, i] = 0
    if pairs:
        w[:, :, :, :, :, 8:] = 0
        for g in range(8):
            w[:, g, 8, 0, g, 8, 0] = -28.0
            for b in range(4): w[:, g, 10, b, g, 9, 0] = -2.0 ** (b - 5)
    return weights(rng, w)
def setup_inputs(rng):
    return {**numbers_of(rng), **stored(trees(rng)), **layers(rng)}
def setup_inputs_ties(rng):
    d = numbers_of(rng)
    o = rng.permutation(N)
    k = rng.integers(-1, 2, (N, 8, C)).astype(np.float32)
    k[o[1]] = -1
    x = d["x"].reshape(N, 8, 16, C, 4)
    x[:, :, 0] = 0
    x[:, :, 0, :, 0] = k.astype(BF)
    a = np.exp2(rng.integers(-3, 4, (1, 8, 1)).astype(np.float32))
    x[:, :, 8:] = 0
    x[:, :, 8, :, 0] = (-1.125 * a).astype(BF)
    x[:, :, 10, :, 0] = (-0.0703125 * a).astype(BF)
    c = np.ones(N, np.float32)
    c[o[0]] = 0
    c[o[2]] = -1
    u = d["u"].reshape(N, 128, 128, 4)
    u[:, :, ::16] = 0
    for h in range(0, 128, 16): u[:, h, h, 0] = c.astype(BF)
    return {"x": x.reshape(N, 128, 4 * C), "u": u.reshape(N, 128, 512), "v": d["v"], **stored(trees(rng)), **layers(rng, [0], True)}
def setup_inputs_near(rng):
    d = numbers_of(rng)
    o = rng.permutation(N) % 2
    k = np.where(o == 0, 2.0 ** -30, 1.0).astype(np.float32)
    x = np.zeros((N, 8, 16, C, 4), np.float32)
    s = rng.integers(-1, 2, (N, 8, C)) * k[:, None, None]
    x[:, :, 0, :, 0] = 1.125 * s
    x[:, :, 1, :, 0] = -1.25 * s
    s = rng.choice([-1.0, 1.0], (N, 8, C)) * 2.0 ** -30
    x[:, :, 8, :, 0] = 1.125 * s
    x[:, :, 9, :, 0] = -1.25 * s
    x[:, :, 2, :, 0] = 2.0 ** -28
    x[:, :, 10, :, 0] = 2.0 ** -28
    for r in range(N):
        at = [0, C - 1, int(rng.integers(C)), int(rng.integers(C))]
        for g, j in zip(rng.permutation(8)[:4], at): x[r, g, 0, j, 0] = 2.0 ** 30 * rng.choice([-1.0, 1.0])
    u = d["u"].astype(np.float32).reshape(N, 128, 128, 4)
    u[:, :, ::16] = 0
    w = np.zeros((N, 128, 4, 128, 4), np.float32)
    for h in range(0, 128, 16):
        u[:, h, h, 0] = 1.125 * k
        u[:, h + 1, h, 0] = k
        w[:, h + 8, 0, h, 0] = 0.5
        w[:, h + 9, 0, h + 1, 0] = 0.5
        w[:, h + 10, 0, h + 2, 0] = 32.0
        w[:, h + 10, 0, h + 10, 0] = 32.0
    return {"x": x.reshape(N, 128, 4 * C).astype(BF), "u": u.reshape(N, 128, 512).astype(BF), "v": d["v"], **stored(trees(rng)), **weights(rng, w.astype(BF))}
def setup_inputs_odd(rng):
    d = numbers_of(rng)
    x = (1.0 + (2 * rng.integers(0, 64, (N, 16, 8, C, 4)) + 1) * 2.0 ** -7) * np.exp2(-rng.integers(0, 7, (N, 16, 8, C, 4)).astype(np.float64)) * rng.choice([-1.0, 1.0], (N, 16, 8, C, 4))
    x[:, :, 0, :, 0] = 1.96875 * 2.0 ** 8 * rng.choice([-1.0, 1.0], (N, 16, C))
    e = rng.choice([-1.0, 1.0], (N, 8, C)) * 2.0 ** -5
    x[:, ::2, 1, :, 0] = 1.125 * e
    x[:, ::2, 2, :, 0] = -e
    u = d["u"].reshape(N, 128, 128, 4)
    u[:, :, ::16] = 0
    for h in range(0, 128, 16): u[:, h + 1:h + 3, h, 0] = 1
    return {"x": x.astype(np.float32).reshape(N, 128, 4 * C).astype(BF), "u": u.reshape(N, 128, 512), "v": d["v"], **stored(trees(rng)), **layers(rng, [0, 8])}
def setup_inputs_ends(rng):
    d = numbers_of(rng)
    o, e = rng.permutation(N) % 4, rng.permutation(N) % 4
    x = np.zeros((N, 128, C, 4))
    u = d["u"].astype(np.float32).reshape(N, 128, 128, 4)
    v = d["v"].astype(np.float32)
    w = np.zeros((N, 128, 4, 128, 4), np.float32)
    t = np.zeros((N, 8, C), np.int64)
    i = np.arange(128)
    last = i % 16 == 15
    for r in range(N):
        h = rng.permutation(8)
        c = np.where(h < 2, 0.0, h % 2 * 2.0 - 1.0)[None, :, None]
        a = -(0.9 + 0.1 * rng.random((128, C, 4))) * 2.0 ** 30
        if o[r] == 1: a = a * rng.choice([-1.0, 1.0], (C, 1))
        if o[r] == 2: a = -(1.0 + 0.125 * rng.integers(0, 8, (128, C, 4))) * 2.0 ** -30
        if o[r] == 3: a = d["x"][r].astype(np.float32).reshape(128, C, 4)[:, :1]
        x[r] = a
        if o[r] < 2:
            x[r, last] = 2.0 ** -30
            u[r, :, ::16] = c * (0.9 + 0.1 * rng.random((128, 8, 4))) * 2.0 ** 30
            v[r] = rng.choice([-1.0, 1.0], (128, 512)) * (0.9 + 0.1 * rng.random((128, 512))) * 2.0 ** 30
        if o[r] == 2:
            u[r, :, ::16] = c * (1.0 + 0.125 * rng.integers(0, 8, (128, 8, 4))) * 2.0 ** -30
            v[r] = rng.choice([-1.0, 1.0], (128, 512)) * (1.0 + 0.125 * rng.integers(0, 8, (128, 512))) * 2.0 ** -30
        if o[r] == 3: u[r, :, ::16] *= np.abs(c).astype(np.float32)
        k = np.where(last, [32.0, 32.0, 256.0, 2.0 ** -8][o[r]], 32.0)
        for b in range(4): w[r, i, b, i, b] = k
        for g in range(8):
            if e[r] == 0: t[r, g] = grown(lean(0, g % 2), np.arange(C))
            if e[r] == 1: t[r, g] = grown(lean(1, g % 2), np.concatenate([[0], np.arange(C - 1, 0, -1)]))
            if e[r] >= 2: t[r, g] = grown(ragged(rng, GAPS[g - 6]) if g >= 6 else full(rng, 128 if e[r] == 2 else (C - 125) // 3), shuffled(rng))
    return {"x": x.astype(np.float32).reshape(N, 128, 4 * C).astype(BF), "u": u.reshape(N, 128, 512).astype(BF), "v": v.astype(BF), **stored(t), **weights(rng, w.astype(BF))}
def setup_inputs_spread(rng):
    d = setup_inputs(rng)
    d["x"] = wide(rng, N, 128, 4 * C, cols=6)
    return d
def check_inputs(d):
    b = []
    for k in ("x", "u", "v"):
        a = np.abs(d[k].astype(np.float32))
        if not (np.isfinite(a).all() and ((a == 0) | (a >= 2.0 ** -30) & (a <= 2.0 ** 30)).all()): b.append("a value of " + k)
    e = np.stack([gentries(d["se"][r]) for r in range(N)])
    if not ((e >= 0) & (e < 2 * C)).all(): b.append("an entry of se")
    else:
        if e[:, :, 0].any(): b.append("se: entry 0")
        if (np.diff(np.sort(e[:, :, 1:], axis=2), axis=2) == 0).any(): b.append("se: equal seats")
        a = e >> 1
        for n in range(7): a = np.take_along_axis(e >> 1, a, 2)
        if a.any(): b.append("se: a place from which eight steps don't lead to place 0")
    none, least, most = [emit(mx_ref.quantize(np.full((128, 16), k, np.float32).astype(BF)))[1][0, 0] for k in (0.0, 2.0 ** -8, 2.0 ** 8)]
    for r in range(N):
        if ((d["wc"][r] == 0x7F) | (d["wc"][r] == 0xFF)).any(): b.append("wc: a code that is no number")
        s = mx_ref.live(d["ws"][r])
        if ((s != none) & ((s < least) | (s > most))).any(): b.append("ws: a scale out of range")
        if (((d["wc"][r].reshape(16, 8, 512, 4) & 0x7F) != 0) & (s == none)[:, None, :, None]).any(): b.append("wc: a code other than zero under the scale of zeros")
    return b
def reference(x, u, v, se, wc, ws):
    qu = [mx_ref.quantize(u[r]) for r in range(N)]
    lay = [pk(wc[r], ws[r]) for r in range(N)]
    seat = [gentries(se[r]).astype(np.int64) for r in range(N)]
    par = [seat[r] >> 1 for r in range(N)]
    now = [x[r] for r in range(N)]
    y, im = np.zeros((N, 128, C), np.float32), np.zeros((N, 8, C), np.float32)
    oc, osc = np.zeros((N, 128, 4 * C), np.uint8), np.zeros((N, 16, C), np.uint8)
    for step in STEP:
        q = [mx_ref.quantize(now[r]) for r in range(N)]
        layered, child = [], []
        for r in range(N):
            layered.append(tile([mx_ref.matmul(pick(lay[r], np.arange(128 * b, 128 * b + 128)), q[r]) * np.float32(0.03125) for b in range(4)]))
            turn = (mx_ref.matmul(qu[r], q[r])[::16] < 0).astype(np.int64)
            seat[r] = seat[r] ^ np.take_along_axis(turn, par[r], 1)
            c = np.full((8, 2 * C), -1, np.int64)
            np.put_along_axis(c, seat[r][:, 1:], np.tile(np.arange(1, C), (8, 1)), 1)
            child.append(c)
        for r in range(N):
            p = r ^ step
            m = np.zeros((8, C), np.int64)
            for depth in range(8):
                at = np.take_along_axis(m, par[r], 1)
                c = np.take_along_axis(child[p], 2 * at + (seat[r] & 1), 1)
                m = np.where(c < 0, at, c)
                m[:, 0] = 0
            e = mx_ref.quantize(gcols(layered[p], m))
            above = gcols(decode(q[r]).astype(BF), par[r]).astype(np.float32)
            now[r] = ((decode(e) + above) * np.float32(0.5)).astype(BF)
            im[r] = m
    for r in range(N):
        z = mx_ref.quantize(now[r])
        y[r] = mx_ref.matmul(mx_ref.quantize(v[r]), z)
        oc[r], osc[r] = emit(z)
    return {"y": y, "im": im, "oc": oc, "osc": osc}

@@ -1,0 +1,490 @@
+from concourse.bass import IndirectOffsetOnAxis
+from concourse.mybir import dt, AluOpType, AxisListType, ActivationFunctionType
+
+N, C, R = 8, 288, 3
+STEP = [2, 4, 1]
+A, F = AluOpType, ActivationFunctionType
+BF, F32, I32, U16, FP8, U8 = "bfloat16", "float32", "int32", "uint16", "float8_e4m3fn_x4", "uint8"
+
+
+def _sb(n, d):
+    return ("sbuf", [128, n], d)
+
+
+SCRATCH = {
+    "xin": _sb(4 * C, BF), "uin": _sb(512, BF), "vin": _sb(512, BF), "sei": _sb(18, I32),
+    "wq": _sb(512, FP8), "wp": _sb(512, U8),
+    "uq": _sb(128, FP8), "up": _sb(128, U8), "ur": _sb(128, FP8), "urp": _sb(128, U8),
+    "vq": _sb(128, FP8), "vp": _sb(128, U8), "eq": _sb(512, FP8), "ep": _sb(512, U8),
+    "xq": _sb(4 * C, FP8), "xp": _sb(4 * C, U8), "hq": _sb(R * C, FP8), "hp": _sb(R * C, U8),
+    "lq": _sb(R * C, FP8), "lp": _sb(R * C, U8),
+    "half": _sb(512, BF), "et": _sb(2048, BF), "xt": _sb(R * 4 * C, BF), "ht": _sb(R * 4 * C, BF),
+    "fb": _sb(R * 4 * C, BF), "fp": _sb(R * 4 * C, BF), "db": _sb(R * 4 * C, BF),
+    "pi": _sb(1, I32), "qi": _sb(1, I32), "gi": _sb(1, I32), "qf": _sb(1, F32), "ad": _sb(1, F32),
+    "bi": _sb(4, I32), "bf": _sb(4, F32), "bc": _sb(4, F32),
+    "cl": _sb(4, F32), "cb": _sb(4, F32), "cc": _sb(4, F32), "ini": _sb(1, F32),
+    "t16": _sb(C, BF), "ij": _sb(C, BF), "ix": _sb(512, BF), "mask": _sb(C, BF), "mask2": _sb(256, BF), "rst": _sb(C, BF),
+    "pm": _sb(2, F32), "c2": _sb(2, F32), "icx": _sb(32, F32), "icy": _sb(32, F32), "lui": _sb(8, I32), "lu": _sb(8, U16),
+    "seu": _sb(18, U16), "paru": _sb(18, U16),
+    "ch": _sb(4 * C, F32), "cw": _sb(4 * C, BF), "loff": _sb(40, U16), "gm": _sb(64, F32), "red": _sb(6, F32),
+    "gl": _sb(480, F32), "gs": _sb(480, F32), "v0f": _sb(32, F32), "v0": _sb(512, BF), "ol": _sb(18, U16),
+    "top": _sb(16, F32), "pv": _sb(32, F32), "pf": _sb(16, F32), "pg": _sb(16, F32),
+    "n1": _sb(32, F32), "n2": _sb(32, F32), "n3": _sb(32, F32), "n4": _sb(32, F32), "nu": _sb(32, U16),
+    "now": _sb(800, BF), "nm": _sb(C, BF), "ns": _sb(C, BF), "no": _sb(18, U16),
+    "tau": _sb(R * C, BF), "ox": _sb((R + 1) * 272, BF), "sc": _sb(R * 272, BF), "ks": _sb(R * 32, BF),
+    "kl": _sb(R * 32, BF), "k8": _sb(R * 16, BF), "ku": _sb(R * 32, U16), "k9": _sb(R * 16, BF), "kv": _sb(R * 32, U16),
+    "vp0": _sb(512, BF), "vp1": _sb(512, BF), "vp2": _sb(512, BF), "v1": _sb(R * 512, BF), "v2": _sb(R * 512, BF),
+    "mm": _sb(R * C, BF), "ms": _sb(R * C, BF), "mo": _sb(R * 18, U16),
+    "ims": _sb(C, F32), "ys": _sb(C, F32),
+    "dv": ("dram", [128, 32], BF), "dl1": ("dram", [128, 32], BF), "dl2": ("dram", [128, 32], BF),
+    "dt1": ("dram", [8, 512], BF), "dt2": ("dram", [8, 512], BF),
+    "ps": ("psum", [128, 4096], F32),
+}
+NDMA = 24
+SEMAPHORES = (["cv", "cs", "ct", "cg", "loc", "va", "vb1", "vb2"] + ["ha%d" % r for r in range(R)]
+              + ["ka%d" % r for r in range(R)] + ["d%d" % i for i in range(NDMA)])
+
+
+def tracker(g, T):
+    qs = {"v": g.vector, "s": g.scalar, "t": g.tensor, "g": g, "y": g.sync}
+    own = {"v": "cv", "s": "cs", "t": "ct", "g": "cg"}
+    total, waited = {}, {q: {} for q in qs}
+    wrote, read = {}, {}
+    nd = [0]
+
+    def wait(q, sem, val):
+        if waited[q].get(sem, 0) < val:
+            qs[q].wait_ge(T.sem[sem], val)
+            waited[q][sem] = val
+
+    def before(q, reads, writes):
+        need = {}
+        for k in list(reads) + list(writes):
+            if k in wrote:
+                s, v = wrote[k]
+                need[s] = max(need.get(s, 0), v)
+        for k in writes:
+            for s, v in read.get(k, []):
+                need[s] = max(need.get(s, 0), v)
+        for s in sorted(need):
+            wait(q, s, need[s])
+
+    def after(reads, writes, mark):
+        for k in writes:
+            wrote[k] = mark
+            read[k] = []
+        for k in reads:
+            if k not in writes:
+                read.setdefault(k, []).append(mark)
+
+    def op(q, fn, reads, writes):
+        before(q, reads, writes)
+        s = own[q]
+        total[s] = total.get(s, 0) + 1
+        fn(qs[q]).then_inc(T.sem[s], 1)
+        after(reads, writes, (s, total[s]))
+
+    def dma(q, fn, reads, writes):
+        before(q, reads, writes)
+        s = "d%d" % nd[0]
+        nd[0] += 1
+        total[s] = 16
+        fn(qs[q]).then_inc(T.sem[s], 16)
+        after(reads, writes, (s, 16))
+
+    def send(fn, reads, count):
+        before("g", reads, [])
+        fn()
+        total["loc"] = total.get("loc", 0) + count
+
+    def arrive(sem, val, keys):
+        total[sem] = val
+        for k in keys:
+            wrote[k] = (sem, val)
+            read[k] = []
+
+    def finish():
+        for s in sorted(total):
+            if max(waited[q].get(s, 0) for q in qs) < total[s]:
+                wait("g", s, total[s])
+
+    return op, dma, send, arrive, finish
+
+
+def rank_program(g, core, T, topo):
+    rank = T.rank_of(core)
+    if rank is None:
+        return
+    op, dma, send, arrive, finish = tracker(g, T)
+    mate = [T.cores[rank ^ s] for s in STEP]
+
+    def remote(r, dst, src, sem):
+        d = mate[r]
+        rid, pid = topo.addr(d, core)
+        g.remote_dma(dst, src, T.sem[sem], T.sem.loc, pid, rid, topo.mask(core, d))
+
+    def eng(r):
+        return len(topo.engines(core, mate[r]))
+
+    def ts(out, in0, s1, s2, o0, o1, reads, writes):
+        if s2 is None:
+            op("v", lambda q: q.tensor_scalar(out, in0, s1, None, o0), reads, writes)
+        else:
+            op("v", lambda q: q.tensor_scalar(out, in0, s1, s2, o0, o1), reads, writes)
+
+    def tt(out, a, b, o, reads, writes):
+        op("v", lambda q: q.tensor_tensor(out, a, b, o), reads, writes)
+
+    def cp(out, in_, reads, writes):
+        op("v", lambda q: q.tensor_copy(out, in_), reads, writes)
+
+    def fill(ap, c, writes):
+        op("v", lambda q: q.memset(ap, c), [], writes)
+
+    def act(out, in_, reads, writes, func=F.Copy, **kw):
+        op("s", lambda q: q.activation(out, in_, func, **kw), reads, writes)
+
+    def iota(out, pattern, base, cm, writes):
+        op("g", lambda q: q.iota(out, pattern, base, cm, allow_small_or_imprecise_dtypes=True), [], writes)
+
+    def scan(out, d1, n, reads, writes, init=0.0):
+        op("v", lambda q: q.tensor_tensor_scan(out, T.rst[:, 0:n], d1, init, A.mult, A.add), ["rst0", "rst1"] + reads, writes)
+
+    def mm(bank, w, wp, a, x, xp, b, reads):
+        op("t", lambda q: q.matmul_mx(T.ps[:, 512 * bank:512 * bank + C], w[:, a:a + 128], wp[:, a:a + 128],
+                                      x[:, b:b + C], xp[:, b:b + C], True, True), reads, ["b%d" % bank])
+
+    def psum(bank):
+        return T.ps[:, 512 * bank:512 * bank + C]
+
+    def quant(src, a, q_, p_, c, n, reads, writes):
+        op("v", lambda q: q.quantize_mx(q_[:, c:c + n], p_[:, c:c + n], src[:, a:a + 4 * n]), reads, writes)
+
+    def signs(r):
+        mm(0, T.ur, T.urp, 0, T.xq, T.xp, C * r, ["ur", "urp", "xq%d" % r])
+
+    def h_products(r):
+        for b in range(4):
+            mm(1 + b, T.wq, T.wp, 128 * b, T.xq, T.xp, C * r, ["wq", "wp", "xq%d" % r])
+
+    def tau(r):
+        act(T.tau[:, C * r:C * r + C], psum(0), ["b0"], ["tau%d" % r], F.Sign, bias=2.0 ** -100)
+
+    def h_tile(r):
+        for b in range(4):
+            act(T.ht[:, 4 * C * r + b:4 * C * (r + 1):4], psum(1 + b), ["b%d" % (1 + b)], ["ht%d%d" % (r, b)], scale=0.03125)
+
+    def h_quant(r):
+        quant(T.ht, 4 * C * r, T.hq, T.hp, C * r, C, ["ht%d%d" % (r, b) for b in range(4)], ["hq%d" % r])
+
+    def h_send(r):
+        n, a, b = eng(r), C * r, C * r + C
+        send(lambda: remote(r, T.lq[:, a:b].bitcast(dt.uint8), T.hq[:, a:b].bitcast(dt.uint8), "ha%d" % r), ["hq%d" % r], n)
+        send(lambda: remote(r, T.lp[:, a:b], T.hp[:, a:b], "ha%d" % r), ["hq%d" % r], n)
+        arrive("ha%d" % r, 2 * n, ["lq%d" % r])
+
+    def key_part(r):
+        o, s, k = 272 * r, 272 * r, 32 * r
+        ox, sc, ks = "ox%d" % (r + 1), "sc%d" % r, "ks%d" % r
+        tt(T.ox[:, o + 272:o + 544], T.tau[:, C * r:C * r + C].indirect(T.ol[:, 0:17]), T.ox[:, o:o + 272], A.mult,
+           ["tau%d" % r, "ol0", "ol1"] + (OX if r == 0 else ["ox%d" % r]), [ox])
+        scan(T.sc[:, s:s + 272], T.ox[:, o + 272:o + 544], 272, [ox, "ini"], [sc], T.ini[:, 0:1])
+        ts(T.ks[:, k + 2:k + 4], T.pm[:, :], T.sc[:, s + 31:s + 32], T.sc[:, s + 271:s + 272], A.mult, A.add, [sc, "pm"], [ks + "b"])
+        cp(T.ks[:, k:k + 2], T.sc[:, s + 15:s + 272:256], [sc], [ks + "a"])
+        for n, x, y in [(2, ["b"], "c"), (4, ["c0", "c1"], "d")]:
+            v, x = T.sc[:, s + 16 * n + 15:s + 32 * n:16], [sc] + [ks + z for z in x]
+            tt(T.ks[:, k + 2 * n:k + 3 * n], T.ks[:, k + n:k + 2 * n], v, A.subtract, x, [ks + y + "0"])
+            tt(T.ks[:, k + 3 * n:k + 4 * n], T.ks[:, k + n:k + 2 * n], v, A.add, x, [ks + y + "1"])
+            if n == 2:
+                cp(T.ks[:, k + 16:k + 24], T.sc[:, s + 143:s + 256:16], [sc], [ks + "e"])
+
+    def key_send(r):
+        n = eng(r)
+        send(lambda: remote(r, T.kl[:, 32 * r:32 * r + 24], T.ks[:, 32 * r:32 * r + 24], "ka%d" % r),
+             ["ks%d%s" % (r, z) for z in ("a", "b", "c0", "c1", "d0", "d1", "e")], n)
+        arrive("ka%d" % r, n, ["kl%d" % r])
+
+    def key_list(r, src, last, lst, deps, out):
+        k, e = 32 * r, 16 * r
+        tt(last[:, e:e + 8], src[:, k + 8:k + 16], src[:, k + 16:k + 24], A.subtract, deps, [out + "x"])
+        tt(last[:, e + 8:e + 16], src[:, k + 8:k + 16], src[:, k + 16:k + 24], A.add, deps, [out + "y"])
+        ts(lst[:, k:k + 16], src[:, k:k + 16], 256.0, None, A.add, None, deps, [out + "a"])
+        ts(lst[:, k + 16:k + 32], last[:, e:e + 16], 256.0, None, A.add, None, [out + "x", out + "y"], [out + "b"])
+
+    def own_list(r):
+        key_list(r, T.ks, T.k9, T.kv, ["ks%d%s" % (r, z) for z in ("a", "b", "c0", "c1", "d0", "d1", "e")], "kv%d" % r)
+
+    def f_products(r):
+        for b in range(4):
+            mm([5, 6, 7, 0][b], T.eq, T.ep, 128 * b, T.xq, T.xp, C * r, ["eq", "xq%d" % r])
+
+    def f_copies(r):
+        for b in range(4):
+            k, a = [5, 6, 7, 0][b], 4 * C * r + C * b
+            act(T.fb[:, a:a + C], psum(k), ["b%d" % k], ["fb%d%d" % (r, b)])
+
+    def f_picks(r):
+        for b in range(4):
+            a = 4 * C * r + C * b
+            act(T.fp[:, a:a + C], T.fb[:, a:a + C].indirect(T.paru[:, 0:18]), ["fb%d%d" % (r, b), "paru"], ["fp%d%d" % (r, b)])
+
+    def mapping(r):
+        k, a, b, z = 32 * r, C * r, C * r + C, "%d" % r
+        key_list(r, T.kl, T.k8, T.ku, ["kl" + z], "ku" + z)
+        v1, v2 = T.v1[:, 512 * r:512 * r + 512], T.v2[:, 512 * r:512 * r + 512]
+        cp(v1.indirect(T.ku[:, k:k + 32]), T["vp" + z][:, 0:512], ["ku" + z + "a", "ku" + z + "b", "vp" + z], ["v1" + z])
+        cp(v2, v1.indirect(T.kv[:, k:k + 32]), ["v1" + z, "kv" + z + "a", "kv" + z + "b"], ["v2" + z])
+        tt(T.mm[:, a:b], v2.indirect(T.no[:, 0:18]), T.mask[:, :], A.mult, ["v2" + z, "no", "mask"], ["mm" + z])
+        scan(T.ms[:, a:b], T.mm[:, a:b], C, ["mm" + z], ["ms" + z])
+        ts(T.mo[:, 18 * r:18 * r + 18], T.ms[:, a + 15:b:16], 144.0, None, A.add, None, ["ms" + z], ["mo" + z])
+
+    def unpack(r):
+        for b in range(4):
+            mm(1 + b, T.eq, T.ep, 128 * b, T.lq, T.lp, C * r, ["eq", "lq%d" % r])
+        for b in range(4):
+            a = 4 * C * r + C * b
+            act(T.db[:, a:a + C], psum(1 + b), ["b%d" % (1 + b)], ["db%d%d" % (r, b)])
+
+    def new_state(r):
+        for b in range(4):
+            a = 4 * C * r + C * b
+            tt(T.xt[:, 4 * C * r + b:4 * C * (r + 1):4], T.db[:, a:a + C].indirect(T.mo[:, 18 * r:18 * r + 18]), T.fp[:, a:a + C],
+               A.add, ["db%d%d" % (r, b), "mo%d" % r, "fp%d%d" % (r, b)], ["xt%d%d" % (r, b)])
+        quant(T.xt, 4 * C * r, T.xq, T.xp, C * (r + 1), C, ["xt%d%d" % (r, b) for b in range(4)], ["xq%d" % (r + 1)])
+
+    dma("y", lambda q: q.dma_start(T.sei[:, :], T.se[:, :]), [], ["sei"])
+    dma("s", lambda q: q.dma_start(T.xin[:, :], T.x[:, :]), [], ["xin"])
+    dma("y", lambda q: q.dma_start(T.uin[:, :], T.u[:, :]), [], ["uin"])
+    dma("s", lambda q: q.dma_start(T.wq[:, :].bitcast(dt.uint8), T.wc[:, :]), [], ["wq"])
+    dma("y", lambda q: q.dma_start(T.wp[:, :], T.ws[:, :]), [], ["wp"])
+    dma("y", lambda q: q.dma_start(T.vin[:, :], T.v[:, :]), [], ["vin"])
+
+    op("g", lambda q: q.iota(T.pi[:, :], [[0, 1]], 0, 1), [], ["pi"])
+    iota(T.ij[:, :], [[1, C]], -144, 0, ["ij"])
+    iota(T.t16[:, :], [[0, 18], [1, 16]], 0, 0, ["t16"])
+    iota(T.c2[:, :], [[1, 2]], 288, 0, ["c2"])
+    op("g", lambda q: q.iota(T.lui[:, :], [[16, 8]], 0, 0), [], ["lui"])
+    iota(T.pm[:, :], [[2, 2]], -1, 0, ["pm"])
+    iota(T.icx[:, :], [[16, 32]], 144, 0, ["icx"])
+    fill(T.half[:, :], 0.5, ["half"])
+    for b in range(4):
+        op("g", lambda q: q.affine_select(T.et[:, 512 * b:512 * b + 512], T.half[:, :], [[1, 512]], A.is_equal, 0.0, -b, -4),
+           ["half"], ["et%d" % b])
+    iota(T.ix[:, :], [[1, 512]], -256, 0, ["ix"])
+    ts(T.qi[:, :], T.pi[:, :], 15, None, A.bitwise_and, None, ["pi"], ["qi"])
+    BI = ["bi%d" % d for d in range(4)]
+    for d in range(4):
+        ts(T.bi[:, d:d + 1], T.pi[:, :], d, 1, A.arith_shift_right, A.bitwise_and, ["pi"], [BI[d]])
+    cp(T.qf[:, :], T.qi[:, :], ["qi"], ["qf"])
+    cp(T.bf[:, :], T.bi[:, :], BI, ["bf"])
+    ts(T.ad[:, :], T.qf[:, :], 0.0, 576.0, A.is_equal, A.mult, ["qf"], ["ad"])
+    for i in range(2):
+        ts(T.ch[:, i:2 * C:2], T.ij[:, :], 288.0, None, A.add, None, ["ij"], ["ch%d" % i])
+        cp(T.cw[:, i:2 * C:2], T.ij[:, :], ["ij"], ["cw%d" % i])
+    ts(T.bc[:, :], T.bf[:, :], 288.0, None, A.add, None, ["bf"], ["bc"])
+    cp(T.loff[:, 0:1], T.bf[:, 0:1], ["bf"], ["lo1"])
+    ts(T.mask2[:, 0:256], T.t16[:, 0:256], T.qf[:, 0:1], 2.0, A.is_equal, A.mult, ["t16", "qf"], ["mask2"])
+    ts(T.rst[:, 1:C], T.t16[:, 1:C], 0.0, None, A.not_equal, None, ["t16"], ["rst1"])
+    for d in range(4):
+        act(T.cb[:, d:d + 1], T.bf[:, d:d + 1], ["bf"], ["cb%d" % d], F.Identity, scale=2.0 ** (8 - d), bias=-2.0 ** (7 - d))
+
+    ts(T.seu[:, 0:1], T.sei[:, 0:1], T.ad[:, 0:1], None, A.add, None, ["sei", "ad"], ["seu0"])
+    cp(T.seu[:, 1:18], T.sei[:, 1:18], ["sei"], ["seu1"])
+    cp(T.lu[:, :], T.lui[:, :], ["lui"], ["lu"])
+    cp(T.ch[:, 0:592].indirect(T.seu[:, 0:18]), T.ij[:, :], ["seu0", "seu1", "ij", "ch0", "ch1"], ["ch"])
+    cp(T.cw[:, 0:592].indirect(T.seu[:, 0:18]), T.ij[:, :], ["seu0", "seu1", "ij", "cw0", "cw1"], ["cw"])
+    act(T.ch[:, 2 * C:4 * C], T.cw[:, 0:2 * C], ["cw", "ch"], ["cht"], F.Identity, bias=288.0)
+    act(T.cw[:, 2 * C:4 * C], T.cw[:, 0:2 * C], ["cw"], ["cwt"])
+
+    OX = []
+    todo = []
+
+    def later(fn, *a):
+        todo.append((fn, a))
+
+    def some(n=1):
+        for i in range(n):
+            if todo:
+                fn, a = todo.pop(0)
+                fn(*a)
+
+    def ox(fn, *a):
+        k = "ox0_%d" % len(OX)
+        OX.append(k)
+        later(fn, *(a + ([k],)))
+
+    later(fill, T.v0f[:, 0:1], 200.0, ["v0i"])
+    later(fill, T.v0f[:, 1:2], -144.0, ["v0j"])
+    later(fill, T.v0[:, 0:2], -144.0, ["v0k"])
+    later(fill, T.rst[:, 0:1], 1.0, ["rst0"])
+    later(ts, T.cl[:, 2:3], T.bf[:, 1:2], 2.0, T.bf[:, 0:1], A.mult, A.add, ["bf"], ["cl2"])
+    for d in range(3):
+        later(ts, T.cc[:, d:d + 1], T.qf[:, :], 2.0 ** (d + 1), T.cb[:, d:d + 1], A.is_ge, A.mult, ["qf", "cb%d" % d], ["cc%d" % d])
+    later(ts, T.cl[:, 3:4], T.bf[:, 2:3], 4.0, T.cl[:, 2:3], A.mult, A.add, ["bf", "cl2"], ["cl3"])
+    ox(fill, T.ox[:, 0:1], 0.0)
+    ox(fill, T.ox[:, 256:257], 0.0)
+    ox(fill, T.ox[:, 8:16], 0.0)
+    for d in range(4):
+        ox(ts, T.ox[:, 16 * 2 ** d:32 * 2 ** d], T.t16[:, 0:16 * 2 ** d], T.qf[:, 0:1], 2.0 ** (3 - d), A.is_equal, A.mult, ["t16", "qf"])
+    for c, z, m in ((0, "cc", 3), (256, "cb", 4)):
+        for d in range(m):
+            if d == 0:
+                ox(cp, T.ox[:, c + 1:c + 2], T[z][:, 0:1], [z + "0"])
+            else:
+                low = T.bf[:, 0:1] if d == 1 else T.cl[:, d:d + 1]
+                ox(ts, T.ox[:, c + 2 ** d:c + 2 ** (d + 1)], T.t16[:, 0:2 ** d], low, T[z][:, d:d + 1], A.is_equal, A.mult,
+                   ["t16", "bf" if d == 1 else "cl%d" % d, z + "%d" % d])
+    later(ts, T.ini[:, :], T.qf[:, :], 0.0, -256.0, A.is_equal, A.mult, ["qf"], ["ini"])
+    later(ts, T.paru[:, :], T.sei[:, :], 0.5, 0.25, A.mult, A.subtract, ["sei"], ["paru"])
+
+    LO = {1: 0, 2: 2, 3: 4, 4: 6, 5: 8, 6: 10, 7: 14, 8: 22}
+
+    def child(t, name="ch"):
+        n = max(1, 2 ** t // 16)
+        deps = [name] + ([name + "t"] if t > 1 else []) + (["lo%da" % t, "lo%db" % t] if t > 4 else ["lo%d" % t])
+        return T[name][:, 0:(4 if t > 1 else 2) * C].indirect(T.loff[:, LO[t]:LO[t] + n]), deps
+
+    def lanes(t):
+        kid, deps = child(t)
+        if t < 5:
+            gm, red = T.gm[:, 16 * t - 16:16 * t], T.red[:, t - 1:t]
+            tt(gm, kid, T.mask2[:, 0:16], A.mult, deps + ["mask2"], ["gm%d" % t])
+            some()
+            op("v", lambda q: q.tensor_reduce(red, gm, AxisListType.X, A.add), ["gm%d" % t], ["red%d" % t])
+            some()
+            if t < 4:
+                ts(T.loff[:, LO[t + 1]:LO[t + 1] + 1], red, T.bc[:, t:t + 1], None, A.add, None, ["red%d" % t, "bc"], ["lo%d" % (t + 1)])
+                some()
+            else:
+                ts(T.loff[:, 8:9], red, T.c2[:, 0:1], None, A.add, None, ["red4", "c2"], ["lo5a"])
+                ts(T.loff[:, 9:10], red, T.c2[:, 1:2], None, A.add, None, ["red4", "c2"], ["lo5b"])
+                ts(T.pv[:, 1:2], red, 0.5, None, A.mult, None, ["red4"], ["pv4"])
+            return
+        n = 2 ** t
+        o, w = n - 32, n // 16
+        tt(T.gl[:, o:o + n], kid, T.mask2[:, 0:n], A.mult, deps + ["mask2"], ["gl%d" % t])
+        some()
+        scan(T.gs[:, o:o + n], T.gl[:, o:o + n], n, ["gl%d" % t], ["gs%d" % t])
+        some()
+        e = T.gs[:, o + 15:o + n:16]
+        if t < 8:
+            b = LO[t + 1]
+            ts(T.loff[:, b:b + w], e, 288.0, None, A.add, None, ["gs%d" % t], ["lo%da" % (t + 1)])
+            ts(T.loff[:, b + w:b + 2 * w], e, 289.0, None, A.add, None, ["gs%d" % t], ["lo%db" % (t + 1)])
+        ts(T.pv[:, w:2 * w], e, 0.5, None, A.mult, None, ["gs%d" % t], ["pv%d" % t])
+
+    def whole(t):
+        kid, deps = child(t, "cw")
+        n = max(16, 2 ** t)
+        act(T.v0[:, 2 ** t:2 ** t + n], kid, deps, ["v0t" if t < 5 else "v0%d" % t])
+        if t < 4:
+            kid, deps = child(t)
+            act(T.v0f[:, 2 ** t:2 ** t + 16], kid, deps, ["v0s"])
+
+    lanes(1)
+    quant(T.xin, 0, T.xq, T.xp, 0, C, ["xin"], ["xq0"])
+    h_products(0)
+    lanes(2)
+    quant(T.uin, 0, T.uq, T.up, 0, 128, ["uin"], ["uq"])
+    act(T.urp[:, :], T.up[:, 0:128].indirect(T.lu[:, 0:8]), ["uq", "lu"], ["urp"])
+    lanes(3)
+    cp(T.ur[:, :].bitcast(dt.uint32), T.uq[:, 0:128].bitcast(dt.uint32).indirect(T.lu[:, 0:8]), ["uq", "lu"], ["ur"])
+    signs(0)
+    h_tile(0)
+    for t in range(1, 4):
+        whole(t)
+    lanes(4)
+    whole(4)
+    tau(0)
+    lanes(5)
+    whole(5)
+    lanes(6)
+    whole(6)
+    h_quant(0)
+    h_send(0)
+    tt(T.top[:, :], T.v0f[:, 0:16], T.mask2[:, 0:16], A.mult, ["v0i", "v0j", "v0s", "mask2"], ["top"])
+    lanes(7)
+    op("v", lambda q: q.tensor_reduce(T.red[:, 4:5], T.top[:, :], AxisListType.X, A.add), ["top"], ["red5"])
+    some()
+    ts(T.pv[:, 0:1], T.red[:, 4:5], 0.5, None, A.mult, None, ["red5"], ["pv0"])
+    some(2)
+    PV = ["pv0", "pv4", "pv5", "pv6", "pv7"]
+    ts(T.pf[:, 0:16], T.pv[:, 0:16], 144.0, -288.0, A.is_ge, A.mult, PV, ["pf"])
+    some(2)
+    tt(T.pg[:, 0:16], T.pf[:, 0:16], T.pv[:, 0:16], A.add, PV + ["pf"], ["pg"])
+    some(2)
+    ts(T.ol[:, 0:16], T.pg[:, 0:16], 144.0, None, A.add, None, ["pg"], ["ol0"])
+    ts(T.ol[:, 16:17], T.pg[:, 0:1], 144.0, None, A.add, None, ["pg"], ["ol1"])
+    some(99)
+    whole(7)
+    whole(8)
+    key_part(0)
+    key_send(0)
+    V0 = ["v0k", "v0t", "v05", "v06", "v07", "v08"]
+    send(lambda: remote(0, T.vp0[:, :], T.v0[:, :], "va"), V0, eng(0))
+    arrive("va", eng(0), ["vp0"])
+    dma("y", lambda q: q.dma_start(T.dv[:, :], T.v0[0:128:16, 0:512]), V0, ["dv"])
+    later(ts, T.icy[:, :], T.icx[:, :], T.qf[:, 0:1], None, A.add, None, ["icx", "qf"], ["icy"])
+    lanes(8)
+    quant(T.et, 0, T.eq, T.ep, 0, 512, ["et%d" % b for b in range(4)], ["eq"])
+    PV = PV + ["pv8"]
+    ts(T.n1[:, :], T.pv[:, :], 144.0, None, A.is_ge, None, PV, ["n1"])
+    tt(T.n2[:, :], T.icy[:, :], T.pv[:, :], A.subtract, PV + ["icy"], ["n2"])
+    ts(T.mask[:, :], T.t16[:, :], T.qf[:, 0:1], None, A.is_equal, None, ["t16", "qf"], ["mask"])
+    ksk = ["ks0%s" % z for z in ("a", "b", "c0", "c1", "d0", "d1", "e")]
+    tt(T.k9[:, 0:8], T.ks[:, 8:16], T.ks[:, 16:24], A.subtract, ksk, ["kv0x"])
+    tt(T.n3[:, :], T.n1[:, :], T.n2[:, :], A.mult, ["n1", "n2"], ["n3"])
+    tt(T.k9[:, 8:16], T.ks[:, 8:16], T.ks[:, 16:24], A.add, ksk, ["kv0y"])
+    tt(T.n4[:, :], T.n3[:, :], T.pv[:, :], A.add, PV + ["n3"], ["n4"])
+    ts(T.kv[:, 0:16], T.ks[:, 0:16], 256.0, None, A.add, None, ksk, ["kv0a"])
+    ts(T.nu[:, :], T.n4[:, :], 144.0, None, A.add, None, ["n4"], ["nu"])
+    ts(T.kv[:, 16:32], T.k9[:, 0:16], 256.0, None, A.add, None, ["kv0x", "kv0y"], ["kv0b"])
+    cp(T.now[:, 0:800].indirect(T.nu[:, 0:32]), T.ix[:, :], ["nu", "ix"], ["now"])
+    tt(T.nm[:, :], T.now[:, 0:C], T.mask[:, :], A.mult, ["now", "mask"], ["nm"])
+    scan(T.ns[:, :], T.nm[:, :], C, ["nm"], ["ns"])
+    ts(T.no[:, :], T.ns[:, 15:C:16], 256.0, None, A.add, None, ["ns"], ["no"])
+    f_products(0)
+    f_copies(0)
+    f_picks(0)
+    for r in (1, 2):
+        send(lambda: remote(r, T["dl%d" % r][:, :], T.dv[:, :], "vb%d" % r), ["dv"], eng(r))
+        arrive("vb%d" % r, eng(r), ["dl%d" % r])
+        dma("y", lambda q: q.dma_start(T["dt%d" % r][:, :], T["dl%d" % r][:, :]), ["dl%d" % r], ["dt%d" % r])
+    unpack(0)
+    ts(T.gi[:, :], T.pi[:, :], 4, None, A.arith_shift_right, None, ["pi"], ["gi"])
+    mapping(0)
+    for r in (1, 2):
+        dma("g", lambda q: q.indirect_dma_start(T["vp%d" % r][:, :], None, T["dt%d" % r][:], IndirectOffsetOnAxis(ap=T.gi[:, 0:1], axis=0),
+                                                bounds_check=7), ["gi", "dt%d" % r], ["vp%d" % r])
+    new_state(0)
+
+    for r in (1, 2):
+        signs(r)
+        h_products(r)
+        tau(r)
+        h_tile(r)
+        key_part(r)
+        key_send(r)
+        h_quant(r)
+        h_send(r)
+        f_products(r)
+        f_copies(r)
+        f_picks(r)
+        own_list(r)
+        if r == 1:
+            quant(T.vin, 0, T.vq, T.vp, 0, 128, ["vin"], ["vq"])
+        unpack(r)
+        mapping(r)
+        if r == R - 1:
+            act(T.ims[:, :], T.v2[:, 512 * r:512 * r + 512].indirect(T.no[:, 0:18]), ["v2%d" % r, "no"], ["ims"], F.Identity, bias=144.0)
+            dma("y", lambda q: q.dma_start(T.im[:, :], T.ims[0:128:16, :]), ["ims"], [])
+        new_state(r)
+
+    a, b = R * C, R * C + C
+    mm(5, T.vq, T.vp, 0, T.xq, T.xp, a, ["vq", "xq%d" % R])
+    dma("y", lambda q: q.dma_start(T.oc[:, :], T.xq[:, a:b].bitcast(dt.uint8)), ["xq%d" % R], [])
+    for k in range(4):
+        dma("y" if k < 2 else "s", lambda q: q.dma_start(T.osc[4 * k:4 * k + 4, :], T.xp[32 * k:32 * k + 4, a:b]), ["xq%d" % R], [])
+    act(T.ys[:, :], psum(5), ["b5"], ["ys"])
+    dma("s", lambda q: q.dma_start(T.y[:, :], T.ys[:, :]), ["ys"], [])
+    finish()

@@ -1,8 +1,8 @@
-from concourse.bass import IndirectOffsetOnAxis
-from concourse.mybir import dt, AluOpType, AxisListType, ActivationFunctionType
+from concourse.mybir import dt, AluOpType, ActivationFunctionType
 
 N, C, R = 8, 288, 3
 STEP = [2, 4, 1]
+PART = [(0, 160), (160, 128)]
 A, F = AluOpType, ActivationFunctionType
 BF, F32, I32, U16, FP8, U8 = "bfloat16", "float32", "int32", "uint16", "float8_e4m3fn_x4", "uint8"
 
@@ -12,37 +12,38 @@ def _sb(n, d):
 
 
 SCRATCH = {
-    "xin": _sb(4 * C, BF), "uin": _sb(512, BF), "vin": _sb(512, BF), "sei": _sb(18, I32),
+    "xin": _sb(4 * C, BF), "uin": _sb(512, BF), "vin": _sb(512, BF), "sei": _sb(20, I32), "pa": _sb(36, I32), "pb": _sb(36, I32),
     "wq": _sb(512, FP8), "wp": _sb(512, U8),
     "uq": _sb(128, FP8), "up": _sb(128, U8), "ur": _sb(128, FP8), "urp": _sb(128, U8),
-    "vq": _sb(128, FP8), "vp": _sb(128, U8), "eq": _sb(512, FP8), "ep": _sb(512, U8),
-    "xq": _sb(4 * C, FP8), "xp": _sb(4 * C, U8), "hq": _sb(R * C, FP8), "hp": _sb(R * C, U8),
-    "lq": _sb(R * C, FP8), "lp": _sb(R * C, U8),
-    "half": _sb(512, BF), "et": _sb(2048, BF), "xt": _sb(R * 4 * C, BF), "ht": _sb(R * 4 * C, BF),
-    "fb": _sb(R * 4 * C, BF), "fp": _sb(R * 4 * C, BF), "db": _sb(R * 4 * C, BF),
-    "pi": _sb(1, I32), "qi": _sb(1, I32), "gi": _sb(1, I32), "qf": _sb(1, F32), "ad": _sb(1, F32),
-    "bi": _sb(4, I32), "bf": _sb(4, F32), "bc": _sb(4, F32),
-    "cl": _sb(4, F32), "cb": _sb(4, F32), "cc": _sb(4, F32), "ini": _sb(1, F32),
-    "t16": _sb(C, BF), "ij": _sb(C, BF), "ix": _sb(512, BF), "mask": _sb(C, BF), "mask2": _sb(256, BF), "rst": _sb(C, BF),
-    "pm": _sb(2, F32), "c2": _sb(2, F32), "icx": _sb(32, F32), "icy": _sb(32, F32), "lui": _sb(8, I32), "lu": _sb(8, U16),
-    "seu": _sb(18, U16), "paru": _sb(18, U16),
-    "ch": _sb(4 * C, F32), "cw": _sb(4 * C, BF), "loff": _sb(40, U16), "gm": _sb(64, F32), "red": _sb(6, F32),
-    "gl": _sb(480, F32), "gs": _sb(480, F32), "v0f": _sb(32, F32), "v0": _sb(512, BF), "ol": _sb(18, U16),
-    "top": _sb(16, F32), "pv": _sb(32, F32), "pf": _sb(16, F32), "pg": _sb(16, F32),
-    "n1": _sb(32, F32), "n2": _sb(32, F32), "n3": _sb(32, F32), "n4": _sb(32, F32), "nu": _sb(32, U16),
-    "now": _sb(800, BF), "nm": _sb(C, BF), "ns": _sb(C, BF), "no": _sb(18, U16),
-    "tau": _sb(R * C, BF), "ox": _sb((R + 1) * 272, BF), "sc": _sb(R * 272, BF), "ks": _sb(R * 32, BF),
-    "kl": _sb(R * 32, BF), "k8": _sb(R * 16, BF), "ku": _sb(R * 32, U16), "k9": _sb(R * 16, BF), "kv": _sb(R * 32, U16),
-    "vp0": _sb(512, BF), "vp1": _sb(512, BF), "vp2": _sb(512, BF), "v1": _sb(R * 512, BF), "v2": _sb(R * 512, BF),
-    "mm": _sb(R * C, BF), "ms": _sb(R * C, BF), "mo": _sb(R * 18, U16),
-    "ims": _sb(C, F32), "ys": _sb(C, F32),
-    "dv": ("dram", [128, 32], BF), "dl1": ("dram", [128, 32], BF), "dl2": ("dram", [128, 32], BF),
-    "dt1": ("dram", [8, 512], BF), "dt2": ("dram", [8, 512], BF),
+    "vq": _sb(128, FP8), "vp": _sb(128, U8), "eq": _sb(1024, FP8), "ep": _sb(1024, U8),
+    "off": _sb(520, BF), "be": _sb(520, BF), "bo": _sb(520, BF),
+    "xt": _sb(R * 4 * C, BF), "ht": _sb(R * 4 * C, BF),
+    "pi": _sb(1, I32), "bi": _sb(6, I32), "bf": _sb(5, F32), "k": _sb(40, F32), "bc": _sb(4, F32),
+    "ij": _sb(C, BF), "t16": _sb(304, BF), "diag": _sb(304, BF), "rst": _sb(304, BF), "r18": _sb(144, BF), "eg": _sb(144, BF),
+    "kg": _sb(20, F32), "bg": _sb(16, F32), "tg": _sb(128, BF), "wh": _sb(128, BF), "xf": _sb(144, BF), "xm": _sb(144, BF),
+    "xs": _sb(144, BF), "ls": _sb(56, U16), "xi": _sb(16, I32), "cm": _sb(16, BF), "c2": _sb(2, F32),
+    "dum": _sb(18, F32), "pk": _sb(C, F32),
+    "seu": _sb(18, U16), "cw": _sb(592, BF), "lo": _sb(24, U16), "gm": _sb(272, BF), "rb": _sb(304, BF), "v0": _sb(256, BF),
+    "lm": _sb(272, BF), "lsc": _sb(272, BF), "lst": _sb(18, U16), "wd": _sb(C, BF), "wt": _sb(C, BF),
+    "xx": _sb(256, BF), "yy": _sb(256, BF), "yg": _sb(128, BF),
+    "same": _sb(20, F32), "nr": _sb(20, F32), "nn": _sb(54, F32), "nu": _sb(18, U16),
+    "now": _sb(592, F32), "pn": _sb(20, U16), "nm": _sb(304, F32), "ns": _sb(304, F32), "si": _sb(20, I32), "sm": _sb(20, F32),
+    "dl": _sb(20, I32), "dw": _sb(20, F32), "cd": _sb(20, I32), "ni": _sb(20, I32), "no": _sb(20, U16), "cl": _sb(20, U16),
+    "mask": _sb(304, BF), "pp": _sb(108, F32), "par": _sb(36, U16),
+    "tau": _sb(R * C, BF), "ta2": _sb(R * C, BF), "ox": _sb((R + 1) * 144, BF), "sc": _sb(R * 144, BF), "key": _sb(R * 8, U16),
+    "src": _sb((R + 1) * 128, BF), "cum": _sb(R * 128, BF), "tb": _sb(R * 128, BF), "tl": _sb(R * 128, BF), "t1": _sb(R * 128, BF),
+    "gg": _sb(R * 304, BF), "zz": _sb(R * 576, BF), "zs": _sb(R * 576, BF), "mo": _sb(R * 64, U16),
+    "ims": _sb(2 * C, F32), "ys": _sb(C, F32),
     "ps": ("psum", [128, 4096], F32),
 }
-NDMA = 24
-SEMAPHORES = (["cv", "cs", "ct", "cg", "loc", "va", "vb1", "vb2"] + ["ha%d" % r for r in range(R)]
-              + ["ka%d" % r for r in range(R)] + ["d%d" % i for i in range(NDMA)])
+for _r in range(R + 1):
+    SCRATCH["xq%d" % _r], SCRATCH["xp%d" % _r] = _sb(C, FP8), _sb(C, U8)
+for _r in range(R):
+    for _n, _w in (("h", C), ("l", C), ("f", 2 * C), ("p", 2 * C)):
+        SCRATCH["%sq%d" % (_n, _r)], SCRATCH["%sp%d" % (_n, _r)] = _sb(_w, FP8), _sb(_w, U8)
+NDMA = 36
+SEMAPHORES = (["cv", "cs", "ct", "cg", "loc"] + ["ha%d" % r for r in range(R)] + ["ka%d" % r for r in range(R)]
+              + ["d%d" % i for i in range(NDMA)])
 
 
 def tracker(g, T):
@@ -74,11 +75,12 @@ def tracker(g, T):
             wrote[k] = mark
             read[k] = []
         for k in reads:
+            assert k in wrote, k
             if k not in writes:
                 read.setdefault(k, []).append(mark)
 
-    def op(q, fn, reads, writes):
-        before(q, reads, writes)
+    def op(q, fn, reads, writes, adds=False):
+        before(q, reads, [] if adds else writes)
         s = own[q]
         total[s] = total.get(s, 0) + 1
         fn(qs[q]).then_inc(T.sem[s], 1)
@@ -144,159 +146,237 @@ def rank_program(g, core, T, topo):
     def act(out, in_, reads, writes, func=F.Copy, **kw):
         op("s", lambda q: q.activation(out, in_, func, **kw), reads, writes)
 
-    def iota(out, pattern, base, cm, writes):
-        op("g", lambda q: q.iota(out, pattern, base, cm, allow_small_or_imprecise_dtypes=True), [], writes)
+    def iota(out, pattern, base, cm, writes, reads=()):
+        op("g", lambda q: q.iota(out, pattern, base, cm, allow_small_or_imprecise_dtypes=True), list(reads), writes)
 
-    def scan(out, d1, n, reads, writes, init=0.0):
-        op("v", lambda q: q.tensor_tensor_scan(out, T.rst[:, 0:n], d1, init, A.mult, A.add), ["rst0", "rst1"] + reads, writes)
+    def scan(out, d1, n, reads, writes):
+        op("v", lambda q: q.tensor_tensor_scan(out, T.rst[:, 0:n], d1, 0.0, A.mult, A.add), ["rst"] + reads, writes)
 
-    def mm(bank, w, wp, a, x, xp, b, reads):
-        op("t", lambda q: q.matmul_mx(T.ps[:, 512 * bank:512 * bank + C], w[:, a:a + 128], wp[:, a:a + 128],
-                                      x[:, b:b + C], xp[:, b:b + C], True, True), reads, ["b%d" % bank])
+    def turn(out, in_, reads, writes):
+        op("v", lambda q: q.transpose(out, in_), reads, writes)
 
-    def psum(bank):
-        return T.ps[:, 512 * bank:512 * bank + C]
+    def mm(bank, w, wp, a, x, xp, b, n, reads, start=True, stop=True):
+        op("t", lambda q: q.matmul_mx(T.ps[:, 512 * bank:512 * bank + n], w[:, a:a + 128], wp[:, a:a + 128],
+                                      x[:, b:b + n], xp[:, b:b + n], start, stop), reads, ["b%d" % bank], not start)
+
+    def psum(bank, n=C):
+        return T.ps[:, 512 * bank:512 * bank + n]
 
     def quant(src, a, q_, p_, c, n, reads, writes):
         op("v", lambda q: q.quantize_mx(q_[:, c:c + n], p_[:, c:c + n], src[:, a:a + 4 * n]), reads, writes)
 
-    def signs(r):
-        mm(0, T.ur, T.urp, 0, T.xq, T.xp, C * r, ["ur", "urp", "xq%d" % r])
+    KN = ["q", "ad", "lo", "a2", "a3", "a3b", "w0", "w1", "w2", "w3", "i7", "y1", "y2", "al1", "al", "m1", "m2", "ma",
+          "ys", "sp", "sp2", "bp", "u", "w", "x", "y", "z", "eh", "dq", "lo2", "hi2", "ae"]
+
+    def k(name):
+        i = KN.index(name)
+        return T.k[:, i:i + 1]
+
+    def b(d):
+        return T.bf[:, d:d + 1]
+
+    def e(i):
+        return T.diag[:, i:i + 1]
+
+    def lin(name, in_, scale, bias, reads):
+        act(k(name), in_, reads, [name], F.Identity, scale=scale, bias=bias)
+
+    def xkeys(r):
+        return ["xq%d%d" % (r, j) for j in range(2)]
 
     def h_products(r):
-        for b in range(4):
-            mm(1 + b, T.wq, T.wp, 128 * b, T.xq, T.xp, C * r, ["wq", "wp", "xq%d" % r])
-
-    def tau(r):
-        act(T.tau[:, C * r:C * r + C], psum(0), ["b0"], ["tau%d" % r], F.Sign, bias=2.0 ** -100)
+        for i in range(4):
+            mm(4 + i, T.wq, T.wp, 128 * i, T["xq%d" % r], T["xp%d" % r], 0, C, ["wq", "wp"] + xkeys(r))
 
     def h_tile(r):
-        for b in range(4):
-            act(T.ht[:, 4 * C * r + b:4 * C * (r + 1):4], psum(1 + b), ["b%d" % (1 + b)], ["ht%d%d" % (r, b)], scale=0.03125)
+        for i in range(4):
+            act(T.ht[:, 4 * C * r + i:4 * C * (r + 1):4], psum(4 + i), ["b%d" % (4 + i)], ["ht%d%d" % (r, i)], scale=0.03125)
 
     def h_quant(r):
-        quant(T.ht, 4 * C * r, T.hq, T.hp, C * r, C, ["ht%d%d" % (r, b) for b in range(4)], ["hq%d" % r])
+        quant(T.ht, 4 * C * r, T["hq%d" % r], T["hp%d" % r], 0, C, ["ht%d%d" % (r, i) for i in range(4)], ["hq%d" % r])
 
     def h_send(r):
-        n, a, b = eng(r), C * r, C * r + C
-        send(lambda: remote(r, T.lq[:, a:b].bitcast(dt.uint8), T.hq[:, a:b].bitcast(dt.uint8), "ha%d" % r), ["hq%d" % r], n)
-        send(lambda: remote(r, T.lp[:, a:b], T.hp[:, a:b], "ha%d" % r), ["hq%d" % r], n)
+        n = eng(r)
+        send(lambda: remote(r, T["lq%d" % r][:, :].bitcast(dt.uint8), T["hq%d" % r][:, :].bitcast(dt.uint8), "ha%d" % r), ["hq%d" % r], n)
+        send(lambda: remote(r, T["lp%d" % r][:, :], T["hp%d" % r][:, :], "ha%d" % r), ["hq%d" % r], n)
         arrive("ha%d" % r, 2 * n, ["lq%d" % r])
 
-    def key_part(r):
-        o, s, k = 272 * r, 272 * r, 32 * r
-        ox, sc, ks = "ox%d" % (r + 1), "sc%d" % r, "ks%d" % r
-        tt(T.ox[:, o + 272:o + 544], T.tau[:, C * r:C * r + C].indirect(T.ol[:, 0:17]), T.ox[:, o:o + 272], A.mult,
-           ["tau%d" % r, "ol0", "ol1"] + (OX if r == 0 else ["ox%d" % r]), [ox])
-        scan(T.sc[:, s:s + 272], T.ox[:, o + 272:o + 544], 272, [ox, "ini"], [sc], T.ini[:, 0:1])
-        ts(T.ks[:, k + 2:k + 4], T.pm[:, :], T.sc[:, s + 31:s + 32], T.sc[:, s + 271:s + 272], A.mult, A.add, [sc, "pm"], [ks + "b"])
-        cp(T.ks[:, k:k + 2], T.sc[:, s + 15:s + 272:256], [sc], [ks + "a"])
-        for n, x, y in [(2, ["b"], "c"), (4, ["c0", "c1"], "d")]:
-            v, x = T.sc[:, s + 16 * n + 15:s + 32 * n:16], [sc] + [ks + z for z in x]
-            tt(T.ks[:, k + 2 * n:k + 3 * n], T.ks[:, k + n:k + 2 * n], v, A.subtract, x, [ks + y + "0"])
-            tt(T.ks[:, k + 3 * n:k + 4 * n], T.ks[:, k + n:k + 2 * n], v, A.add, x, [ks + y + "1"])
-            if n == 2:
-                cp(T.ks[:, k + 16:k + 24], T.sc[:, s + 143:s + 256:16], [sc], [ks + "e"])
+    def tau(r):
+        return T.tau[:, C * r:C * r + C]
 
-    def key_send(r):
+    def ta2(r):
+        return T.ta2[:, C * r:C * r + C]
+
+    def table(r, between):
+        z, o, s = "%d" % r, 144 * r, 128 * r
+        tt(T.ox[:, o + 144:o + 288], tau(r).indirect(T.lst[:, 8:17]), T.ox[:, o:o + 144], A.mult,
+           ["tau%d0" % r, "tau%d1" % r, "lst"] + (["ox0", "oxa", "oxb", "oxc"] if r == 0 else ["ox" + z]), ["ox%d" % (r + 1)])
+        between()
+        op("v", lambda q: q.tensor_tensor_scan(T.sc[:, o:o + 144], T.r18[:, :], T.ox[:, o + 144:o + 288], 0.0, A.mult, A.add),
+           ["r18", "ox%d" % (r + 1)], ["sc" + z])
+        tt(T.src[:, s + 128:s + 256], ta2(r).indirect(T.lst[:, 0:8]), T.src[:, s:s + 128], A.mult,
+           ["ta2" + z, "lst", "src" + z], ["src%d" % (r + 1)])
+        ts(T.key[:, 8 * r:8 * r + 8], T.sc[:, o + 17:o + 144:18], 2.0 ** (r - 1), 63.5, A.mult, A.add, ["sc" + z], ["key" + z])
+        cp(T.tb[:, s:s + 128].indirect(T.key[:, 8 * r:8 * r + 8]), T.src[:, s + 128:s + 256], ["key" + z, "src%d" % (r + 1)], ["tb" + z])
         n = eng(r)
-        send(lambda: remote(r, T.kl[:, 32 * r:32 * r + 24], T.ks[:, 32 * r:32 * r + 24], "ka%d" % r),
-             ["ks%d%s" % (r, z) for z in ("a", "b", "c0", "c1", "d0", "d1", "e")], n)
-        arrive("ka%d" % r, n, ["kl%d" % r])
+        send(lambda: remote(r, T.tl[:, s:s + 128], T.tb[:, s:s + 128], "ka" + z), ["tb" + z], n)
+        arrive("ka" + z, n, ["tl" + z])
 
-    def key_list(r, src, last, lst, deps, out):
-        k, e = 32 * r, 16 * r
-        tt(last[:, e:e + 8], src[:, k + 8:k + 16], src[:, k + 16:k + 24], A.subtract, deps, [out + "x"])
-        tt(last[:, e + 8:e + 16], src[:, k + 8:k + 16], src[:, k + 16:k + 24], A.add, deps, [out + "y"])
-        ts(lst[:, k:k + 16], src[:, k:k + 16], 256.0, None, A.add, None, deps, [out + "a"])
-        ts(lst[:, k + 16:k + 32], last[:, e:e + 16], 256.0, None, A.add, None, [out + "x", out + "y"], [out + "b"])
+    def own_signs(r):
+        z, s = "%d" % r, 128 * r
+        if r == 0:
+            act(T.cum[:, 0:128], ta2(0).indirect(T.lst[:, 0:8]), ["ta20", "lst"], ["cum0"])
+        else:
+            tt(T.cum[:, s:s + 128], ta2(r).indirect(T.lst[:, 0:8]), T.cum[:, s - 128:s], A.mult,
+               ["ta2" + z, "lst", "cum%d" % (r - 1)], ["cum" + z])
 
-    def own_list(r):
-        key_list(r, T.ks, T.k9, T.kv, ["ks%d%s" % (r, z) for z in ("a", "b", "c0", "c1", "d0", "d1", "e")], "kv%d" % r)
+    def pick(out, a, src, lst, n, reads, writes):
+        cp(T[out % "q"][:, a:a + n].bitcast(dt.uint32), T[src % "q"][:, 0:C].bitcast(dt.uint32).indirect(lst), reads, [writes + "q"])
+        act(T[out % "p"][:, a:a + n], T[src % "p"][:, 0:C].indirect(lst), reads, [writes + "p"])
 
-    def f_products(r):
-        for b in range(4):
-            mm([5, 6, 7, 0][b], T.eq, T.ep, 128 * b, T.xq, T.xp, C * r, ["eq", "xq%d" % r])
-
-    def f_copies(r):
-        for b in range(4):
-            k, a = [5, 6, 7, 0][b], 4 * C * r + C * b
-            act(T.fb[:, a:a + C], psum(k), ["b%d" % k], ["fb%d%d" % (r, b)])
-
-    def f_picks(r):
-        for b in range(4):
-            a = 4 * C * r + C * b
-            act(T.fp[:, a:a + C], T.fb[:, a:a + C].indirect(T.paru[:, 0:18]), ["fb%d%d" % (r, b), "paru"], ["fp%d%d" % (r, b)])
+    def f_part(r):
+        z = "%d" % r
+        pick("f%s" + z, 0, "x%s" + z, T.par[:, 0:36], 2 * C, ["par"] + xkeys(r), "f" + z)
+        for j, (c, n) in enumerate(PART):
+            for h in range(2):
+                for i in range(4):
+                    mm(4 * j + i, T.eq, T.ep, 512 * h + 128 * i, T["fq" + z], T["fp" + z], C * h + c, n,
+                       ["eq%d%d" % (h, i), "f" + z + "q", "f" + z + "p"], h == 0, False)
 
     def mapping(r):
-        k, a, b, z = 32 * r, C * r, C * r + C, "%d" % r
-        key_list(r, T.kl, T.k8, T.ku, ["kl" + z], "ku" + z)
-        v1, v2 = T.v1[:, 512 * r:512 * r + 512], T.v2[:, 512 * r:512 * r + 512]
-        cp(v1.indirect(T.ku[:, k:k + 32]), T["vp" + z][:, 0:512], ["ku" + z + "a", "ku" + z + "b", "vp" + z], ["v1" + z])
-        cp(v2, v1.indirect(T.kv[:, k:k + 32]), ["v1" + z, "kv" + z + "a", "kv" + z + "b"], ["v2" + z])
-        tt(T.mm[:, a:b], v2.indirect(T.no[:, 0:18]), T.mask[:, :], A.mult, ["v2" + z, "no", "mask"], ["mm" + z])
-        scan(T.ms[:, a:b], T.mm[:, a:b], C, ["mm" + z], ["ms" + z])
-        ts(T.mo[:, 18 * r:18 * r + 18], T.ms[:, a + 15:b:16], 144.0, None, A.add, None, ["ms" + z], ["mo" + z])
+        z, s, a, c = "%d" % r, 128 * r, 304 * r, 576 * r
+        tt(T.t1[:, s:s + 128], T.tl[:, s:s + 128].indirect(T.key[:, 8 * r:8 * r + 8]), T.cum[:, s:s + 128], A.mult,
+           ["tl" + z, "key" + z, "cum" + z], ["t1" + z])
+        tt(T.gg[:, a:a + 304], T.t1[:, s:s + 128].indirect(T.no[:, 0:19]), T.mask[:, :], A.mult, ["t1" + z, "no", "mask"], ["gg" + z])
+        for h in range(2):
+            turn(T.zz[:, c + C * h:c + C * h + C], T.gg[:, a + 16 * h:a + 16 * h + C], ["gg" + z], ["zz%d%d" % (r, h)])
+        for h in range(2):
+            scan(T.zs[:, c + C * h:c + C * h + C], T.zz[:, c + C * h:c + C * h + C], C, ["zz%d%d" % (r, h)], ["zs%d%d" % (r, h)])
+        ts(T.mo[:, 64 * r:64 * r + 64], T.zs[:, c:c + 576].indirect(T.ls[:, 50:54]), 144.0, None, A.add, None,
+           ["zs%d0" % r, "zs%d1" % r, "lsf"], ["mo" + z])
 
-    def unpack(r):
-        for b in range(4):
-            mm(1 + b, T.eq, T.ep, 128 * b, T.lq, T.lp, C * r, ["eq", "lq%d" % r])
-        for b in range(4):
-            a = 4 * C * r + C * b
-            act(T.db[:, a:a + C], psum(1 + b), ["b%d" % (1 + b)], ["db%d%d" % (r, b)])
+    def mo(r, h, c=0, n=C):
+        a = 64 * r + 32 * h + c // 16
+        return T.mo[:, a:a + n // 16]
 
     def new_state(r):
-        for b in range(4):
-            a = 4 * C * r + C * b
-            tt(T.xt[:, 4 * C * r + b:4 * C * (r + 1):4], T.db[:, a:a + C].indirect(T.mo[:, 18 * r:18 * r + 18]), T.fp[:, a:a + C],
-               A.add, ["db%d%d" % (r, b), "mo%d" % r, "fp%d%d" % (r, b)], ["xt%d%d" % (r, b)])
-        quant(T.xt, 4 * C * r, T.xq, T.xp, C * (r + 1), C, ["xt%d%d" % (r, b) for b in range(4)], ["xq%d" % (r + 1)])
+        z, x = "%d" % r, 4 * C * r
+        for j, (c, n) in enumerate(PART):
+            for h in range(2):
+                pick("p%s" + z, C * h + c, "l%s" + z, mo(r, h, c, n), n, ["mo" + z, "lq" + z], "p%d%d%d" % (r, j, h))
+        for j, (c, n) in enumerate(PART):
+            for h in range(2):
+                for i in range(4):
+                    mm(4 * j + i, T.eq, T.ep, 512 * h + 128 * i, T["pq" + z], T["pp" + z], C * h + c, n,
+                       ["p%d%d%dq" % (r, j, h), "p%d%d%dp" % (r, j, h)], False, h == 1)
+        for j, (c, n) in enumerate(PART):
+            for i in range(4):
+                out, key, bank = T.xt[:, x + 4 * c + i:x + 4 * (c + n):4], "xt%d%d%d" % (r, j, i), 4 * j + i
+                if i % 2 == j:
+                    ts(out, psum(bank, n), 0.5, None, A.mult, None, ["b%d" % bank], [key])
+                else:
+                    act(out, psum(bank, n), ["b%d" % bank], [key], scale=0.5)
+            quant(T.xt, x + 4 * c, T["xq%d" % (r + 1)], T["xp%d" % (r + 1)], c, n, ["xt%d%d%d" % (r, j, i) for i in range(4)],
+                  ["xq%d%d" % (r + 1, j)])
 
-    dma("y", lambda q: q.dma_start(T.sei[:, :], T.se[:, :]), [], ["sei"])
+    dma("y", lambda q: q.dma_start(T.sei[:, 0:18], T.se[:, :]), [], ["sei"])
     dma("s", lambda q: q.dma_start(T.xin[:, :], T.x[:, :]), [], ["xin"])
-    dma("y", lambda q: q.dma_start(T.uin[:, :], T.u[:, :]), [], ["uin"])
-    dma("s", lambda q: q.dma_start(T.wq[:, :].bitcast(dt.uint8), T.wc[:, :]), [], ["wq"])
+    dma("y", lambda q: q.dma_start(T.wq[:, :].bitcast(dt.uint8), T.wc[:, :]), [], ["wq"])
     dma("y", lambda q: q.dma_start(T.wp[:, :], T.ws[:, :]), [], ["wp"])
+    dma("y", lambda q: q.dma_start(T.uin[:, :], T.u[:, :]), [], ["uin"])
+    dma("y", lambda q: q.dma_start(T.sei[:, 18:20], T.se[:, 0:2]), [], ["sej"])
+    PA = []
+    for i, (buf, c, p0, p1, s0) in enumerate([("pa", 0, 0, 128, 0), ("pa", 18, 0, 112, 16), ("pa", 18, 112, 128, 0),
+                                              ("pb", 0, 16, 128, 0), ("pb", 0, 0, 16, 112), ("pb", 18, 0, 128, 0)]):
+        dma("y", lambda q: q.dma_start(T[buf][p0:p1, c:c + 18], T.se[s0:s0 + p1 - p0, :]), [], ["pa%d" % i])
+        PA.append("pa%d" % i)
     dma("y", lambda q: q.dma_start(T.vin[:, :], T.v[:, :]), [], ["vin"])
 
     op("g", lambda q: q.iota(T.pi[:, :], [[0, 1]], 0, 1), [], ["pi"])
-    iota(T.ij[:, :], [[1, C]], -144, 0, ["ij"])
-    iota(T.t16[:, :], [[0, 18], [1, 16]], 0, 0, ["t16"])
-    iota(T.c2[:, :], [[1, 2]], 288, 0, ["c2"])
-    op("g", lambda q: q.iota(T.lui[:, :], [[16, 8]], 0, 0), [], ["lui"])
-    iota(T.pm[:, :], [[2, 2]], -1, 0, ["pm"])
-    iota(T.icx[:, :], [[16, 32]], 144, 0, ["icx"])
-    fill(T.half[:, :], 0.5, ["half"])
-    for b in range(4):
-        op("g", lambda q: q.affine_select(T.et[:, 512 * b:512 * b + 512], T.half[:, :], [[1, 512]], A.is_equal, 0.0, -b, -4),
-           ["half"], ["et%d" % b])
-    iota(T.ix[:, :], [[1, 512]], -256, 0, ["ix"])
-    ts(T.qi[:, :], T.pi[:, :], 15, None, A.bitwise_and, None, ["pi"], ["qi"])
-    BI = ["bi%d" % d for d in range(4)]
-    for d in range(4):
+    iota(T.ij[:, :], [[2, C]], -C, 0, ["ij"])
+    iota(T.t16[:, :], [[0, 19], [1, 16]], 0, 0, ["t16"])
+    iota(T.kg[:, :], [[1, 20]], 0, 0, ["kg"])
+    iota(T.c2[:, :], [[1, 2]], C, 0, ["c2"])
+    iota(T.xf[:, :], [[1, 8], [8, 18]], -16, 0, ["xf"])
+    iota(T.tg[:, :], [[1, 16], [0, 8]], 0, 0, ["tg"])
+    iota(T.xf[:, 0:144:18], [[0, 8]], 1, 0, ["xfa"], ["xf"])
+    iota(T.xf[:, 1:144:18], [[0, 4], [1, 2]], 2, 0, ["xfb"], ["xf"])
+    iota(T.xf[:, 2:144:18], [[0, 2], [1, 4]], 4, 0, ["xfc"], ["xf"])
+    iota(T.bg[:, :], [[1, 8], [0, 2]], 0, 0, ["bg"])
+    iota(T.eg[:, :], [[0, 8], [1, 18]], 0, 0, ["eg"])
+    iota(T.off[:, :], [[1, 520]], -3, -4, ["io"])
+    iota(T.now[:, :], [[0, 592]], 0, 0, ["nw0"])
+    W = [16, 32, 64, 1, 8, 4, 2, 128]
+
+    def handed(d):
+        n = max(1, 2 ** (d - 4))
+        c = 16 * (d - 1) if d < 5 else 16 * (n + 2)
+        iota(T.pk[:, c:c + 16 * n], [[16 // n, n], [1, 2], [16, 8]], 128 * (d + 1) + 2048 * W[d], 0, ["pk%d" % d])
+
+    for d in (7, 6, 5):
+        handed(d)
+
+    fill(T.rb[:, 0:16], -float(C), ["rb0"])
+    fill(T.v0[:, 0:2], -float(C), ["v00"])
+    ts(T.bi[:, 5:6], T.pi[:, :], 15, None, A.bitwise_and, None, ["pi"], ["qi"])
+    BI = ["bi%d" % d for d in range(5)]
+    for d in range(5):
         ts(T.bi[:, d:d + 1], T.pi[:, :], d, 1, A.arith_shift_right, A.bitwise_and, ["pi"], [BI[d]])
-    cp(T.qf[:, :], T.qi[:, :], ["qi"], ["qf"])
-    cp(T.bf[:, :], T.bi[:, :], BI, ["bf"])
-    ts(T.ad[:, :], T.qf[:, :], 0.0, 576.0, A.is_equal, A.mult, ["qf"], ["ad"])
+    cp(k("q"), T.bi[:, 5:6], ["qi"], ["q"])
+    cp(T.bf[:, :], T.bi[:, 0:5], BI, ["bf"])
+    ts(k("ad"), k("q"), 0.0, 576.0, A.is_equal, A.mult, ["q"], ["ad"])
+    for d in range(3):
+        ts(T.k[:, 36 + d:37 + d], k("q"), 2.0 ** (d + 1), None, A.is_ge, None, ["q"], ["gq%d" % d])
+    ts(T.bc[:, :], T.bf[:, 0:4], float(C), None, A.add, None, ["bf"], ["bc"])
     for i in range(2):
-        ts(T.ch[:, i:2 * C:2], T.ij[:, :], 288.0, None, A.add, None, ["ij"], ["ch%d" % i])
-        cp(T.cw[:, i:2 * C:2], T.ij[:, :], ["ij"], ["cw%d" % i])
-    ts(T.bc[:, :], T.bf[:, :], 288.0, None, A.add, None, ["bf"], ["bc"])
-    cp(T.loff[:, 0:1], T.bf[:, 0:1], ["bf"], ["lo1"])
-    ts(T.mask2[:, 0:256], T.t16[:, 0:256], T.qf[:, 0:1], 2.0, A.is_equal, A.mult, ["t16", "qf"], ["mask2"])
-    ts(T.rst[:, 1:C], T.t16[:, 1:C], 0.0, None, A.not_equal, None, ["t16"], ["rst1"])
-    for d in range(4):
-        act(T.cb[:, d:d + 1], T.bf[:, d:d + 1], ["bf"], ["cb%d" % d], F.Identity, scale=2.0 ** (8 - d), bias=-2.0 ** (7 - d))
+        act(T.cw[:, i:2 * C:2], T.ij[:, :], ["ij"], ["cw%d" % i])
+    ts(k("a2"), b(3), 2.0, b(0), A.mult, A.add, ["bf"], ["a2"])
+    ts(k("a3b"), b(3), 2.0, b(2), A.mult, A.add, ["bf"], ["a3b"])
+    ts(k("x"), b(0), b(4), 272.0, A.not_equal, A.mult, ["bf"], ["x"])
+    ts(k("y"), k("q"), b(4), 16.0, A.subtract, A.mult, ["q", "bf"], ["y"])
+    ts(k("eh"), k("ad"), b(4), 0.5, A.mult, A.mult, ["ad", "bf"], ["eh"])
+    ts(k("y1"), k("q"), b(4), 16.0, A.add, A.mult, ["q", "bf"], ["y1"])
+    ts(k("z"), k("x"), k("y"), 15.0, A.add, A.add, ["x", "y"], ["z"])
+    ts(k("a3"), k("a3b"), 2.0, b(0), A.mult, A.add, ["bf", "a3b"], ["a3"])
+    ts(k("y2"), b(0), -8.0, k("y1"), A.mult, A.add, ["bf", "y1"], ["y2"])
+    ts(T.diag[:, :], T.t16[:, :], k("q"), None, A.is_equal, None, ["t16", "q"], ["diag"])
+    ts(T.k[:, 34:35], k("z"), k("eh"), None, A.add, None, ["z", "eh"], ["fl0"])
+    ts(T.k[:, 35:36], k("z"), 256.0, 559.0, A.add, A.min, ["z"], ["fl1"])
+    act(T.rst[:, :], T.t16[:, :], ["t16"], ["rst"], F.Sign)
+    for d, s in enumerate((0, 3, 2, 1)):
+        lin("w%d" % d, b(s), 2.0 ** (4 - d), -2.0 ** (3 - d), ["bf"])
+    lin("i7", k("q"), 8.0, 128.0, ["q"])
+    ts(k("ma"), e(8), e(10), 0.5, A.add, A.mult, ["diag"], ["ma"])
+    ts(k("sp"), e(10), e(11), None, A.add, None, ["diag"], ["sp"])
+    ts(k("al1"), e(6), 0.5, e(7), A.mult, A.add, ["diag"], ["al1"])
+    ts(k("m1"), e(7), 4.0, e(6), A.mult, A.add, ["diag"], ["m1"])
+    ts(T.ls[:, 0:8], T.kg[:, 0:8], 16.0, None, A.mult, None, ["kg"], ["lsu"])
+    ts(k("u"), e(8), e(9), 0.5, A.add, A.mult, ["diag"], ["u"])
+    ts(k("w"), e(10), e(11), 0.5, A.subtract, A.mult, ["diag"], ["w"])
+    ts(k("al"), e(5), 0.25, k("al1"), A.mult, A.add, ["diag", "al1"], ["al"])
+    ts(k("m2"), k("m1"), k("q"), 0.375, A.add, A.subtract, ["m1", "q"], ["m2"])
 
-    ts(T.seu[:, 0:1], T.sei[:, 0:1], T.ad[:, 0:1], None, A.add, None, ["sei", "ad"], ["seu0"])
+    ts(T.seu[:, 0:1], T.sei[:, 0:1], k("ad"), None, A.add, None, ["sei", "ad"], ["seu0"])
     cp(T.seu[:, 1:18], T.sei[:, 1:18], ["sei"], ["seu1"])
-    cp(T.lu[:, :], T.lui[:, :], ["lui"], ["lu"])
-    cp(T.ch[:, 0:592].indirect(T.seu[:, 0:18]), T.ij[:, :], ["seu0", "seu1", "ij", "ch0", "ch1"], ["ch"])
-    cp(T.cw[:, 0:592].indirect(T.seu[:, 0:18]), T.ij[:, :], ["seu0", "seu1", "ij", "cw0", "cw1"], ["cw"])
-    act(T.ch[:, 2 * C:4 * C], T.cw[:, 0:2 * C], ["cw", "ch"], ["cht"], F.Identity, bias=288.0)
-    act(T.cw[:, 2 * C:4 * C], T.cw[:, 0:2 * C], ["cw"], ["cwt"])
+    cp(T.ls[:, 50:52], T.k[:, 34:36], ["fl0", "fl1"], ["lse"])
+    ts(T.ls[:, 52:54], T.k[:, 34:36], 16.0, None, A.add, None, ["fl0", "fl1"], ["lsf"])
+    cp(T.cw[:, 0:592].indirect(T.seu[:, 0:18]), T.ij[:, :], ["seu0", "seu1", "ij", "cw0", "cw1", "lse"], ["cw"])
 
-    OX = []
+    act(T.cm[:, 10:11], b(0), ["bf"], ["cm3"])
+    lin("lo", b(4), -1.0, 1.0, ["bf"])
+    lin("ys", b(3), -0.5, 0.5, ["bf"])
+    lin("bp", k("sp"), -1.0, 1.0, ["sp"])
+    lin("sp2", k("sp"), 2.0, 0.0, ["sp"])
+    lin("dq", k("q"), 2.0, 688.0, ["q"])
+    lin("ae", k("ad"), 1.0, -0.25, ["ad"])
+    lin("lo2", b(4), -0.5, 0.5, ["bf"])
+    lin("hi2", b(4), 0.5, 0.0, ["bf"])
+    act(T.cm[:, 0:8], T.diag[:, 0:8], ["diag"], ["cm0"])
+    act(T.cm[:, 8:9], k("w"), ["u", "w"], ["cm1"], F.Identity, bias=k("u"))
+    act(T.cm[:, 9:10], k("w"), ["u", "w"], ["cm2"], F.Identity, scale=-1.0, bias=k("u"))
+    act(T.dum[:, :], T.kg[:, 0:18], ["kg", "dq"], ["dum"], F.Identity, scale=32.0, bias=k("dq"))
+    act(T.r18[:, :], T.eg[:, :], ["eg"], ["r18"], F.Sign)
+
     todo = []
 
     def later(fn, *a):
@@ -308,183 +388,186 @@ def rank_program(g, core, T, topo):
                 fn, a = todo.pop(0)
                 fn(*a)
 
-    def ox(fn, *a):
-        k = "ox0_%d" % len(OX)
-        OX.append(k)
-        later(fn, *(a + ([k],)))
+    def first_tile():
+        quant(T.xin, 0, T.xq0, T.xp0, 0, C, ["xin"], xkeys(0))
+        h_products(0)
+        h_tile(0)
 
-    later(fill, T.v0f[:, 0:1], 200.0, ["v0i"])
-    later(fill, T.v0f[:, 1:2], -144.0, ["v0j"])
-    later(fill, T.v0[:, 0:2], -144.0, ["v0k"])
-    later(fill, T.rst[:, 0:1], 1.0, ["rst0"])
-    later(ts, T.cl[:, 2:3], T.bf[:, 1:2], 2.0, T.bf[:, 0:1], A.mult, A.add, ["bf"], ["cl2"])
-    for d in range(3):
-        later(ts, T.cc[:, d:d + 1], T.qf[:, :], 2.0 ** (d + 1), T.cb[:, d:d + 1], A.is_ge, A.mult, ["qf", "cb%d" % d], ["cc%d" % d])
-    later(ts, T.cl[:, 3:4], T.bf[:, 2:3], 4.0, T.cl[:, 2:3], A.mult, A.add, ["bf", "cl2"], ["cl3"])
-    ox(fill, T.ox[:, 0:1], 0.0)
-    ox(fill, T.ox[:, 256:257], 0.0)
-    ox(fill, T.ox[:, 8:16], 0.0)
-    for d in range(4):
-        ox(ts, T.ox[:, 16 * 2 ** d:32 * 2 ** d], T.t16[:, 0:16 * 2 ** d], T.qf[:, 0:1], 2.0 ** (3 - d), A.is_equal, A.mult, ["t16", "qf"])
-    for c, z, m in ((0, "cc", 3), (256, "cb", 4)):
-        for d in range(m):
-            if d == 0:
-                ox(cp, T.ox[:, c + 1:c + 2], T[z][:, 0:1], [z + "0"])
-            else:
-                low = T.bf[:, 0:1] if d == 1 else T.cl[:, d:d + 1]
-                ox(ts, T.ox[:, c + 2 ** d:c + 2 ** (d + 1)], T.t16[:, 0:2 ** d], low, T[z][:, d:d + 1], A.is_equal, A.mult,
-                   ["t16", "bf" if d == 1 else "cl%d" % d, z + "%d" % d])
-    later(ts, T.ini[:, :], T.qf[:, :], 0.0, -256.0, A.is_equal, A.mult, ["qf"], ["ini"])
-    later(ts, T.paru[:, :], T.sei[:, :], 0.5, 0.25, A.mult, A.subtract, ["sei"], ["paru"])
+    def scorer():
+        cp(T.ur[:, :].bitcast(dt.uint32), T.uq[:, 0:128].bitcast(dt.uint32).indirect(T.ls[:, 0:8]), ["uq", "lsu"], ["ur"])
+        act(T.urp[:, :], T.up[:, 0:128].indirect(T.ls[:, 0:8]), ["uq", "lsu"], ["urp"])
+        mm(0, T.ur, T.urp, 0, T.xq0, T.xp0, 0, C, ["ur", "urp"] + xkeys(0))
 
-    LO = {1: 0, 2: 2, 3: 4, 4: 6, 5: 8, 6: 10, 7: 14, 8: 22}
+    later(first_tile)
+    later(tt, T.xm[:, :], T.xf[:, :], T.diag[:, 0:144], A.mult, ["xf", "xfa", "xfb", "xfc", "diag"], ["xm"])
+    later(ts, T.wh[:, 0:16], T.tg[:, 0:16], 1.0, k("w0"), A.is_equal, A.mult, ["tg", "w0"], ["wh0"])
+    later(scan, T.xs[:, :], T.xm[:, :], 144, ["xm"], ["xs"])
+    for d, a in ((1, b(0)), (2, k("a2")), (3, k("a3"))):
+        later(ts, T.wh[:, 8 * 2 ** d:16 * 2 ** d], T.tg[:, 0:8 * 2 ** d], a, k("w%d" % d), A.is_equal, A.mult,
+              ["tg", "bf", "a2", "a3", "w%d" % d], ["wh%d" % d])
+    later(cp, T.ls[:, 16:25], T.xs[:, 15:144:16], ["xs"], ["lsv"])
+    later(quant, T.uin, 0, T.uq, T.up, 0, 128, ["uin"], ["uq"])
+    later(ts, T.xi[:, :], T.bg[:, :], k("al"), k("m2"), A.mult, A.add, ["bg", "al", "m2"], ["xi"])
+    later(scorer)
+    later(ts, T.ls[:, 8:16], T.kg[:, 0:8], k("i7"), None, A.add, None, ["kg", "i7"], ["ls7"])
+    later(ts, T.ls[:, 26:42], T.xi[:, :], 16.0, None, A.mult, None, ["xi"], ["lsx"])
+    later(ts, T.ls[:, 42:50], T.kg[:, 0:8], k("y2"), None, A.add, None, ["kg", "y2"], ["lsy"])
+    later(ts, T.pn[:, 0:19], T.sei[:, 0:19], 0.5, 0.25, A.mult, A.subtract, ["sei", "sej"], ["pn0"])
+    later(ts, T.si[:, 0:19], T.sei[:, 0:19], 1, None, A.bitwise_and, None, ["sei", "sej"], ["si"])
+    later(ts, T.pp[:, 0:36], T.pa[:, :], k("lo2"), None, A.mult, None, PA + ["lo2"], ["p1"])
+    later(ts, T.pp[:, 36:72], T.pb[:, :], k("hi2"), 0.25, A.mult, A.subtract, PA + ["hi2"], ["p2"])
+    later(ts, T.pn[:, 0:19:18], T.sei[:, 0:19:18], 0.5, k("ae"), A.mult, A.add, ["sei", "sej", "ae", "pn0"], ["pn1"])
+    later(ts, T.sm[:, 0:19], T.si[:, 0:19], 2048.0, None, A.subtract, None, ["si"], ["sm"])
+    later(tt, T.pp[:, 72:108], T.pp[:, 0:36], T.pp[:, 36:72], A.add, ["p1", "p2"], ["p3"])
+    later(cp, T.par[:, :], T.pp[:, 72:108], ["p3"], ["par"])
 
-    def child(t, name="ch"):
+    LO = {2: 0, 3: 2, 4: 4, 5: 6, 6: 8, 7: 12}
+    RB = {2: 17, 3: 33, 4: 49, 5: 65, 6: 97, 7: 161}
+
+    def child(t):
         n = max(1, 2 ** t // 16)
-        deps = [name] + ([name + "t"] if t > 1 else []) + (["lo%da" % t, "lo%db" % t] if t > 4 else ["lo%d" % t])
-        return T[name][:, 0:(4 if t > 1 else 2) * C].indirect(T.loff[:, LO[t]:LO[t] + n]), deps
+        return T.cw[:, 0:2 * C].indirect(T.lo[:, LO[t]:LO[t] + n]), ["cw"] + (["lo%da" % t, "lo%db" % t] if t > 5 else ["lo%d" % t])
 
-    def lanes(t):
+    def lanes(t, n1=1, n2=1, n3=1):
         kid, deps = child(t)
-        if t < 5:
-            gm, red = T.gm[:, 16 * t - 16:16 * t], T.red[:, t - 1:t]
-            tt(gm, kid, T.mask2[:, 0:16], A.mult, deps + ["mask2"], ["gm%d" % t])
-            some()
-            op("v", lambda q: q.tensor_reduce(red, gm, AxisListType.X, A.add), ["gm%d" % t], ["red%d" % t])
-            some()
-            if t < 4:
-                ts(T.loff[:, LO[t + 1]:LO[t + 1] + 1], red, T.bc[:, t:t + 1], None, A.add, None, ["red%d" % t, "bc"], ["lo%d" % (t + 1)])
-                some()
-            else:
-                ts(T.loff[:, 8:9], red, T.c2[:, 0:1], None, A.add, None, ["red4", "c2"], ["lo5a"])
-                ts(T.loff[:, 9:10], red, T.c2[:, 1:2], None, A.add, None, ["red4", "c2"], ["lo5b"])
-                ts(T.pv[:, 1:2], red, 0.5, None, A.mult, None, ["red4"], ["pv4"])
-            return
-        n = 2 ** t
-        o, w = n - 32, n // 16
-        tt(T.gl[:, o:o + n], kid, T.mask2[:, 0:n], A.mult, deps + ["mask2"], ["gl%d" % t])
-        some()
-        scan(T.gs[:, o:o + n], T.gl[:, o:o + n], n, ["gl%d" % t], ["gs%d" % t])
-        some()
-        e = T.gs[:, o + 15:o + n:16]
-        if t < 8:
-            b = LO[t + 1]
-            ts(T.loff[:, b:b + w], e, 288.0, None, A.add, None, ["gs%d" % t], ["lo%da" % (t + 1)])
-            ts(T.loff[:, b + w:b + 2 * w], e, 289.0, None, A.add, None, ["gs%d" % t], ["lo%db" % (t + 1)])
-        ts(T.pv[:, w:2 * w], e, 0.5, None, A.mult, None, ["gs%d" % t], ["pv%d" % t])
+        n, o = max(16, 2 ** t), RB[t]
+        tt(T.gm[:, o - 17:o - 17 + n], kid, T.diag[:, 0:n], A.mult, deps + ["diag"], ["gm%d" % t])
+        some(n1)
+        scan(T.rb[:, o:o + n], T.gm[:, o - 17:o - 17 + n], n, ["gm%d" % t], ["rb%d" % t])
+        some(n2)
+        ends = T.rb[:, o + 15:o + n:16]
+        if t < 4:
+            ts(T.lo[:, LO[t + 1]:LO[t + 1] + 1], ends, T.bc[:, t:t + 1], None, A.add, None, ["rb%d" % t, "bc"], ["lo%d" % (t + 1)])
+        elif t == 4:
+            ts(T.lo[:, 6:8], T.c2[:, :], ends, None, A.add, None, ["rb4", "c2"], ["lo5"])
+        elif t < 7:
+            for s in range(2):
+                ts(T.lo[:, LO[t + 1] + s:LO[t + 1] + n // 8:2], ends, float(C + s), None, A.add, None, ["rb%d" % t], ["lo%d%s" % (t + 1, "ab"[s])])
+        some(n3)
 
     def whole(t):
-        kid, deps = child(t, "cw")
-        n = max(16, 2 ** t)
-        act(T.v0[:, 2 ** t:2 ** t + n], kid, deps, ["v0t" if t < 5 else "v0%d" % t])
-        if t < 4:
-            kid, deps = child(t)
-            act(T.v0f[:, 2 ** t:2 ** t + 16], kid, deps, ["v0s"])
+        kid, deps = child(t)
+        act(T.v0[:, 2 ** t:2 ** t + max(16, 2 ** t)], kid, deps, ["v0t" if t < 5 else "v0%d" % t])
 
-    lanes(1)
-    quant(T.xin, 0, T.xq, T.xp, 0, C, ["xin"], ["xq0"])
-    h_products(0)
+    d1 = T.dw[:, 19:20]
+    ts(d1, T.cw[:, 1:2], T.cw[:, 0:1], T.cm[:, 10:11], A.subtract, A.mult, ["cw", "cm3"], ["d1"])
+    act(T.wd[:, :], T.cw[:, 0:2 * C:2], ["cw", "ma"], ["wd"], scale=k("ma"))
+    act(T.wt[:, :], T.cw[:, 1:2 * C:2], ["cw"], ["wt"], scale=0.5)
+    for i in (9, 11):
+        dma("y", lambda q: q.dma_start(T.wd[i:128:16, :], T.wt[i:128:16, :]), ["wd", "wt"], ["wd%d" % i])
+    act(T.v0[:, 2:4], T.cw[:, 0:2], ["cw"], ["v01"])
+    some()
+    ts(T.lo[:, 0:1], T.cw[:, 0:1], d1, T.bc[:, 1:2], A.add, A.add, ["d1", "cw", "bc"], ["lo2"])
+    ts(T.rb[:, 16:17], d1, T.cw[:, 0:1], None, A.add, None, ["d1", "cw"], ["rb1"])
     lanes(2)
-    quant(T.uin, 0, T.uq, T.up, 0, 128, ["uin"], ["uq"])
-    act(T.urp[:, :], T.up[:, 0:128].indirect(T.lu[:, 0:8]), ["uq", "lu"], ["urp"])
     lanes(3)
-    cp(T.ur[:, :].bitcast(dt.uint32), T.uq[:, 0:128].bitcast(dt.uint32).indirect(T.lu[:, 0:8]), ["uq", "lu"], ["ur"])
-    signs(0)
-    h_tile(0)
-    for t in range(1, 4):
-        whole(t)
     lanes(4)
-    whole(4)
-    tau(0)
-    lanes(5)
-    whole(5)
-    lanes(6)
-    whole(6)
+    act(T.ox[:, 0:144], T.wh[:, :].indirect(T.ls[:, 16:25]), ["wh0", "wh1", "wh2", "wh3", "lsv"], ["ox0"])
+    iota(T.ox[:, 0:144:18], [[0, 4], [128, 2]], -64, 0, ["oxa"], ["ox0"])
+    iota(T.ox[:, 1:144:18], [[0, 2], [64, 2], [0, 2]], -32, 0, ["oxb"], ["ox0"])
+    iota(T.ox[:, 2:144:18], [[32, 2], [0, 4]], -16, 0, ["oxc"], ["ox0"])
+    for t in (2, 3, 4):
+        whole(t)
     h_quant(0)
     h_send(0)
-    tt(T.top[:, :], T.v0f[:, 0:16], T.mask2[:, 0:16], A.mult, ["v0i", "v0j", "v0s", "mask2"], ["top"])
-    lanes(7)
-    op("v", lambda q: q.tensor_reduce(T.red[:, 4:5], T.top[:, :], AxisListType.X, A.add), ["top"], ["red5"])
-    some()
-    ts(T.pv[:, 0:1], T.red[:, 4:5], 0.5, None, A.mult, None, ["red5"], ["pv0"])
-    some(2)
-    PV = ["pv0", "pv4", "pv5", "pv6", "pv7"]
-    ts(T.pf[:, 0:16], T.pv[:, 0:16], 144.0, -288.0, A.is_ge, A.mult, PV, ["pf"])
-    some(2)
-    tt(T.pg[:, 0:16], T.pf[:, 0:16], T.pv[:, 0:16], A.add, PV + ["pf"], ["pg"])
-    some(2)
-    ts(T.ol[:, 0:16], T.pg[:, 0:16], 144.0, None, A.add, None, ["pg"], ["ol0"])
-    ts(T.ol[:, 16:17], T.pg[:, 0:1], 144.0, None, A.add, None, ["pg"], ["ol1"])
-    some(99)
+    for d in (4, 3, 2, 1):
+        handed(d)
+    iota(T.now[:, 0:1], [[0, 1]], 128 + 2048 * W[0], 0, ["nw1"], ["nw0"])
+    lanes(5)
+    whole(5)
+    lanes(6, 2, 2)
+    whole(6)
     whole(7)
-    whole(8)
-    key_part(0)
-    key_send(0)
-    V0 = ["v0k", "v0t", "v05", "v06", "v07", "v08"]
-    send(lambda: remote(0, T.vp0[:, :], T.v0[:, :], "va"), V0, eng(0))
-    arrive("va", eng(0), ["vp0"])
-    dma("y", lambda q: q.dma_start(T.dv[:, :], T.v0[0:128:16, 0:512]), V0, ["dv"])
-    later(ts, T.icy[:, :], T.icx[:, :], T.qf[:, 0:1], None, A.add, None, ["icx", "qf"], ["icy"])
-    lanes(8)
-    quant(T.et, 0, T.eq, T.ep, 0, 512, ["et%d" % b for b in range(4)], ["eq"])
-    PV = PV + ["pv8"]
-    ts(T.n1[:, :], T.pv[:, :], 144.0, None, A.is_ge, None, PV, ["n1"])
-    tt(T.n2[:, :], T.icy[:, :], T.pv[:, :], A.subtract, PV + ["icy"], ["n2"])
-    ts(T.mask[:, :], T.t16[:, :], T.qf[:, 0:1], None, A.is_equal, None, ["t16", "qf"], ["mask"])
-    ksk = ["ks0%s" % z for z in ("a", "b", "c0", "c1", "d0", "d1", "e")]
-    tt(T.k9[:, 0:8], T.ks[:, 8:16], T.ks[:, 16:24], A.subtract, ksk, ["kv0x"])
-    tt(T.n3[:, :], T.n1[:, :], T.n2[:, :], A.mult, ["n1", "n2"], ["n3"])
-    tt(T.k9[:, 8:16], T.ks[:, 8:16], T.ks[:, 16:24], A.add, ksk, ["kv0y"])
-    tt(T.n4[:, :], T.n3[:, :], T.pv[:, :], A.add, PV + ["n3"], ["n4"])
-    ts(T.kv[:, 0:16], T.ks[:, 0:16], 256.0, None, A.add, None, ksk, ["kv0a"])
-    ts(T.nu[:, :], T.n4[:, :], 144.0, None, A.add, None, ["n4"], ["nu"])
-    ts(T.kv[:, 16:32], T.k9[:, 0:16], 256.0, None, A.add, None, ["kv0x", "kv0y"], ["kv0b"])
-    cp(T.now[:, 0:800].indirect(T.nu[:, 0:32]), T.ix[:, :], ["nu", "ix"], ["now"])
-    tt(T.nm[:, :], T.now[:, 0:C], T.mask[:, :], A.mult, ["now", "mask"], ["nm"])
-    scan(T.ns[:, :], T.nm[:, :], C, ["nm"], ["ns"])
-    ts(T.no[:, :], T.ns[:, 15:C:16], 256.0, None, A.add, None, ["ns"], ["no"])
-    f_products(0)
-    f_copies(0)
-    f_picks(0)
-    for r in (1, 2):
-        send(lambda: remote(r, T["dl%d" % r][:, :], T.dv[:, :], "vb%d" % r), ["dv"], eng(r))
-        arrive("vb%d" % r, eng(r), ["dl%d" % r])
-        dma("y", lambda q: q.dma_start(T["dt%d" % r][:, :], T["dl%d" % r][:, :]), ["dl%d" % r], ["dt%d" % r])
-    unpack(0)
-    ts(T.gi[:, :], T.pi[:, :], 4, None, A.arith_shift_right, None, ["pi"], ["gi"])
+    lanes(7, 2, 0, 0)
+    RBS = ["rb%d" % t for t in range(8)]
+    act(T.xx[:, :], T.rb[:, 0:289].indirect(T.ls[:, 26:42]), RBS + ["lsx"], ["xx"])
+    act(tau(0), psum(0), ["b0"], ["tau00", "tau01"], F.Sign, bias=2.0 ** -100)
+    tt(T.lm[:, :], T.v0[:, :].indirect(T.ls[:, 8:25]), T.diag[:, 0:272], A.mult,
+       ["v00", "v01", "v0t", "v05", "v06", "v07", "ls7", "lsv", "diag"], ["lm"])
+    act(ta2(0), tau(0), ["tau00", "sp", "bp"], ["ta20"], F.Identity, scale=k("sp"), bias=k("bp"))
+    tt(T.same[:, 1:5], T.rb[:, 16:65:16], T.rb[:, 0:49:16], A.is_equal, RBS, ["sa0"])
+    for s in range(2):
+        tt(T.same[:, 5 + s:19:2], T.rb[:, 80 + 16 * s:289:32], T.rb[:, 64:161:16], A.is_equal, RBS, ["sa%d" % (s + 1)])
+    scan(T.lsc[:, :], T.lm[:, :], 272, ["lm"], ["lsc"])
+    turn(T.yy[:, :], T.xx[:, :], ["xx"], ["yy"])
+    ts(T.lst[:, 0:17], T.lsc[:, 15:272:16], 0.5, 144.0, A.mult, A.add, ["lsc"], ["lst"])
+    act(T.yg[:, :], T.yy[:, :].indirect(T.ls[:, 42:50]), ["yy", "lsy", "ys"], ["yg"], scale=k("ys"))
+    op("v", lambda q: q.tensor_tensor_scan(T.nr[:, 1:5], T.same[:, 1:5], T.same[:, 1:5], 0.0, A.max, A.max), ["sa0"], ["nr4"])
+    ts(T.nn[:, 0:18], T.rb[:, 16:289:16], 400.0, None, A.add, None, RBS, ["n1"])
+    table(0, lambda: tt(T.src[:, 0:128], T.wd[:, :].indirect(T.lst[:, 0:8]), T.yg[:, :], A.add,
+                        ["wd", "wd9", "wd11", "lst", "yg"], ["src0"]))
+
+    act(T.off[:, :], T.off[:, :], ["io"], ["io"], F.Abs)
+    own_signs(0)
+    act(T.be[:, :], T.off[:, :], ["io", "lo"], ["be"], F.Relu, scale=-1.0, bias=k("lo"))
+    act(T.bo[:, :], T.off[:, :], ["io", "bf"], ["bo"], F.Relu, scale=-1.0, bias=b(4))
+
+    ts(T.nr[:, 5:7], T.same[:, 5:7], T.nr[:, 4:5], None, A.max, None, ["sa1", "sa2", "nr4"], ["nr5"])
+    tt(T.nr[:, 1:4], T.nr[:, 1:4], T.k[:, 36:39], A.max, ["nr4", "gq0", "gq1", "gq2"], ["nr3"])
+    some()
+    for s in range(2):
+        tt(T.nr[:, 7 + s:11:2], T.same[:, 7 + s:11:2], T.nr[:, 5:7], A.max, ["sa1", "sa2", "nr5"], ["nr6%d" % s])
+    some(2)
+    for s in range(2):
+        tt(T.nr[:, 11 + s:19:2], T.same[:, 11 + s:19:2], T.nr[:, 7:11], A.max, ["sa1", "sa2", "nr60", "nr61"], ["nr7%d" % s])
+    some(99)
+    for h in range(2):
+        for i in range(4):
+            later(quant, T.bo if h else T.be, 3 - i, T.eq, T.ep, 512 * h + 128 * i, 128, ["bo" if h else "be"], ["eq%d%d" % (h, i)])
+    tt(T.nn[:, 18:36], T.nr[:, 1:19], T.dum[:, :], A.mult, ["nr3", "nr4", "nr5", "nr60", "nr61", "nr70", "nr71", "dum"], ["n2"])
+    some()
+    tt(T.nn[:, 36:54], T.nn[:, 0:18], T.nn[:, 18:36], A.max, ["n1", "n2"], ["n3"])
+    some()
+    ts(T.nu[:, :], T.nn[:, 36:54], 0.5, 56.0, A.mult, A.subtract, ["n3"], ["nu"])
+    some()
+    cp(T.now[:, :].indirect(T.nu[:, 0:18]), T.pk[:, :], ["nu", "nw0", "nw1"] + ["pk%d" % d for d in range(1, 8)], ["now"])
+    some()
+    tt(T.nm[:, :], T.now[:, :].indirect(T.pn[:, 0:19]), T.diag[:, :], A.mult, ["now", "pn0", "pn1", "diag"], ["nm"])
+    some()
+    scan(T.ns[:, :], T.nm[:, :], 304, ["nm"], ["ns"])
+    some()
+    ts(T.dl[:, 0:19], T.ns[:, 15:304:16], 2.0 ** -11, 0.28, A.mult, A.subtract, ["ns"], ["dl"])
+    some()
+    tt(T.dw[:, 0:19], T.dl[:, 0:19], T.sm[:, 0:19], A.mult, ["dl", "sm"], ["dw"])
+    some()
+    tt(T.cd[:, 0:19], T.dw[:, 0:19], T.ns[:, 15:304:16], A.add, ["dw", "ns"], ["cd"])
+    ts(T.cl[:, 0:19], T.cd[:, 0:19], 2.0 ** -7, 0.496, A.mult, A.subtract, ["cd"], ["cl"])
+    ts(T.ni[:, 0:19], T.cd[:, 0:19], 127, None, A.bitwise_and, None, ["cd"], ["ni"])
+    act(T.mask[:, :], T.cm[:, 0:10].indirect(T.cl[:, 0:19]), ["cm0", "cm1", "cm2", "cl"], ["mask"])
+    cp(T.no[:, 0:19], T.ni[:, 0:19], ["ni"], ["no"])
+    f_part(0)
     mapping(0)
-    for r in (1, 2):
-        dma("g", lambda q: q.indirect_dma_start(T["vp%d" % r][:, :], None, T["dt%d" % r][:], IndirectOffsetOnAxis(ap=T.gi[:, 0:1], axis=0),
-                                                bounds_check=7), ["gi", "dt%d" % r], ["vp%d" % r])
     new_state(0)
 
     for r in (1, 2):
-        signs(r)
+        z = "%d" % r
+        for j, (c, n) in enumerate(PART):
+            mm(j, T.ur, T.urp, 0, T["xq" + z], T["xp" + z], c, n, ["ur", "urp", "xq%d%d" % (r, j)])
         h_products(r)
-        tau(r)
+        for j, (c, n) in enumerate(PART):
+            ts(T.tau[:, C * r + c:C * r + c + n], psum(j, n), 0.0, 0.5, A.is_ge, A.subtract, ["b%d" % j], ["tau%d%d" % (r, j)])
         h_tile(r)
-        key_part(r)
-        key_send(r)
+        table(r, lambda: ts(ta2(r), tau(r), k("sp2"), k("bp"), A.mult, A.add, ["tau%d0" % r, "tau%d1" % r, "sp2", "bp"], ["ta2" + z]))
         h_quant(r)
         h_send(r)
-        f_products(r)
-        f_copies(r)
-        f_picks(r)
-        own_list(r)
+        own_signs(r)
+        f_part(r)
         if r == 1:
             quant(T.vin, 0, T.vq, T.vp, 0, 128, ["vin"], ["vq"])
-        unpack(r)
         mapping(r)
-        if r == R - 1:
-            act(T.ims[:, :], T.v2[:, 512 * r:512 * r + 512].indirect(T.no[:, 0:18]), ["v2%d" % r, "no"], ["ims"], F.Identity, bias=144.0)
-            dma("y", lambda q: q.dma_start(T.im[:, :], T.ims[0:128:16, :]), ["ims"], [])
         new_state(r)
 
-    a, b = R * C, R * C + C
-    mm(5, T.vq, T.vp, 0, T.xq, T.xp, a, ["vq", "xq%d" % R])
-    dma("y", lambda q: q.dma_start(T.oc[:, :], T.xq[:, a:b].bitcast(dt.uint8)), ["xq%d" % R], [])
-    for k in range(4):
-        dma("y" if k < 2 else "s", lambda q: q.dma_start(T.osc[4 * k:4 * k + 4, :], T.xp[32 * k:32 * k + 4, a:b]), ["xq%d" % R], [])
-    act(T.ys[:, :], psum(5), ["b5"], ["ys"])
-    dma("s", lambda q: q.dma_start(T.y[:, :], T.ys[:, :]), ["ys"], [])
+    xq, xp = T["xq%d" % R], T["xp%d" % R]
+    for h in range(2):
+        act(T.ims[:, C * h:C * h + C], T.ij[:, :].indirect(mo(R - 1, h)), ["ij", "mo%d" % (R - 1)], ["ims%d" % h], F.Identity,
+            scale=0.5, bias=144.0)
+    for j, (c, n) in enumerate(PART):
+        mm(j, T.vq, T.vp, 0, xq, xp, c, n, ["vq", "xq%d%d" % (R, j)])
+        cp(T.ys[:, c:c + n], psum(j, n), ["b%d" % j], ["ys%d" % j])
+    dma("y", lambda q: q.dma_start(T.oc[:, :], xq[:, :].bitcast(dt.uint8)), xkeys(R), [])
+    for i in range(4):
+        dma("y", lambda q: q.dma_start(T.osc[4 * i:4 * i + 4, :], xp[32 * i:32 * i + 4, :]), xkeys(R), [])
+    dma("y", lambda q: q.dma_start(T.y[:, :], T.ys[:, :]), ["ys0", "ys1"], [])
+    for h in range(2):
+        dma("s", lambda q: q.dma_start(T.im[h:8:2, :], T.ims[0:128:32, C * h:C * h + C]), ["ims%d" % h], [])
     finish()

@@ -12,28 +12,28 @@ def _sb(n, d):
 
 
 SCRATCH = {
-    "xin": _sb(4 * C, BF), "uin": _sb(512, BF), "vin": _sb(512, BF), "sei": _sb(20, I32), "pa": _sb(36, I32), "pb": _sb(36, I32),
+    "xin": _sb(4 * C, BF), "uin": _sb(512, BF), "vin": _sb(512, BF), "sei": _sb(18, I32), "pa": _sb(36, I32),
     "wq": _sb(512, FP8), "wp": _sb(512, U8),
     "uq": _sb(128, FP8), "up": _sb(128, U8), "ur": _sb(128, FP8), "urp": _sb(128, U8),
     "vq": _sb(128, FP8), "vp": _sb(128, U8), "eq": _sb(1024, FP8), "ep": _sb(1024, U8),
     "off": _sb(520, BF), "be": _sb(520, BF), "bo": _sb(520, BF),
     "xt": _sb(R * 4 * C, BF), "ht": _sb(R * 4 * C, BF),
     "pi": _sb(1, I32), "bi": _sb(6, I32), "bf": _sb(5, F32), "k": _sb(40, F32), "bc": _sb(4, F32),
-    "ij": _sb(C, BF), "t16": _sb(304, BF), "diag": _sb(304, BF), "rst": _sb(304, BF), "r18": _sb(144, BF), "eg": _sb(144, BF),
-    "kg": _sb(20, F32), "bg": _sb(16, F32), "tg": _sb(128, BF), "wh": _sb(128, BF), "xf": _sb(144, BF), "xm": _sb(144, BF),
-    "xs": _sb(144, BF), "ls": _sb(56, U16), "xi": _sb(16, I32), "cm": _sb(16, BF), "c2": _sb(2, F32),
+    "ij": _sb(C, BF), "t16": _sb(C, BF), "diag": _sb(C, BF), "rst": _sb(C, BF), "r18": _sb(144, BF), "eg": _sb(144, BF),
+    "kg": _sb(20, F32), "bg": _sb(16, F32), "tg": _sb(128, BF), "wh": _sb(128, BF),
+    "ls": _sb(64, U16), "xi": _sb(16, I32), "cm": _sb(16, BF), "c2": _sb(2, F32),
     "dum": _sb(18, F32), "pk": _sb(C, F32),
     "seu": _sb(18, U16), "cw": _sb(592, BF), "lo": _sb(24, U16), "gm": _sb(272, BF), "rb": _sb(304, BF), "v0": _sb(256, BF),
     "lm": _sb(272, BF), "lsc": _sb(272, BF), "lst": _sb(18, U16), "wd": _sb(C, BF), "wt": _sb(C, BF),
     "xx": _sb(256, BF), "yy": _sb(256, BF), "yg": _sb(128, BF),
     "same": _sb(20, F32), "nr": _sb(20, F32), "nn": _sb(54, F32), "nu": _sb(18, U16),
-    "now": _sb(592, F32), "pn": _sb(20, U16), "nm": _sb(304, F32), "ns": _sb(304, F32), "si": _sb(20, I32), "sm": _sb(20, F32),
-    "dl": _sb(20, I32), "dw": _sb(20, F32), "cd": _sb(20, I32), "ni": _sb(20, I32), "no": _sb(20, U16), "cl": _sb(20, U16),
-    "mask": _sb(304, BF), "pp": _sb(108, F32), "par": _sb(36, U16),
+    "now": _sb(592, F32), "pn": _sb(18, U16), "nm": _sb(C, F32), "ns": _sb(C, F32), "si": _sb(18, I32), "sm": _sb(18, F32),
+    "dl": _sb(18, I32), "dw": _sb(20, F32), "cd": _sb(18, I32), "ni": _sb(18, I32), "no": _sb(18, U16), "cl": _sb(18, U16),
+    "mask": _sb(C, BF), "par": _sb(36, U16),
     "tau": _sb(R * C, BF), "ta2": _sb(R * C, BF), "ox": _sb((R + 1) * 144, BF), "sc": _sb(R * 144, BF), "key": _sb(R * 8, U16),
     "src": _sb((R + 1) * 128, BF), "cum": _sb(R * 128, BF), "tb": _sb(R * 128, BF), "tl": _sb(R * 128, BF), "t1": _sb(R * 128, BF),
-    "gg": _sb(R * 304, BF), "zz": _sb(R * 576, BF), "zs": _sb(R * 576, BF), "mo": _sb(R * 64, U16),
-    "ims": _sb(2 * C, F32), "ys": _sb(C, F32),
+    "gg": _sb(320, BF), "zz": _sb(640, BF), "zs": _sb(640, BF), "mo": _sb(R * 64, U16), "ms": _sb(32, U16),
+    "ims": _sb(C, F32), "ys": _sb(C, F32),
     "ps": ("psum", [128, 4096], F32),
 }
 for _r in range(R + 1):
@@ -86,13 +86,13 @@ def tracker(g, T):
         fn(qs[q]).then_inc(T.sem[s], 1)
         after(reads, writes, (s, total[s]))
 
-    def dma(q, fn, reads, writes):
-        before(q, reads, writes)
+    def dma(q, fn, reads, writes, joins=False):
+        before(q, reads, [] if joins else writes)
+        nd[0] += 0 if joins else 1
         s = "d%d" % nd[0]
-        nd[0] += 1
-        total[s] = 16
+        total[s] = total.get(s, 0) + 16
         fn(qs[q]).then_inc(T.sem[s], 16)
-        after(reads, writes, (s, 16))
+        after(reads, writes, (s, total[s]))
 
     def send(fn, reads, count):
         before("g", reads, [])
@@ -120,13 +120,12 @@ def rank_program(g, core, T, topo):
     op, dma, send, arrive, finish = tracker(g, T)
     mate = [T.cores[rank ^ s] for s in STEP]
 
-    def remote(r, dst, src, sem):
-        d = mate[r]
-        rid, pid = topo.addr(d, core)
-        g.remote_dma(dst, src, T.sem[sem], T.sem.loc, pid, rid, topo.mask(core, d))
-
     def eng(r):
-        return len(topo.engines(core, mate[r]))
+        return topo.engines(core, mate[r])
+
+    def remote(r, dst, src, sem, n):
+        rid, pid = topo.addr(mate[r], core)
+        g.remote_dma(dst, src, T.sem[sem], T.sem.loc, pid, rid, sum(1 << i for i in eng(r)[:n]))
 
     def ts(out, in0, s1, s2, o0, o1, reads, writes):
         if s2 is None:
@@ -165,8 +164,8 @@ def rank_program(g, core, T, topo):
     def quant(src, a, q_, p_, c, n, reads, writes):
         op("v", lambda q: q.quantize_mx(q_[:, c:c + n], p_[:, c:c + n], src[:, a:a + 4 * n]), reads, writes)
 
-    KN = ["q", "ad", "lo", "a2", "a3", "a3b", "w0", "w1", "w2", "w3", "i7", "y1", "y2", "al1", "al", "m1", "m2", "ma",
-          "ys", "sp", "sp2", "bp", "u", "w", "x", "y", "z", "eh", "dq", "lo2", "hi2", "ae"]
+    KN = ["q", "ad", "lo", "a2", "a3", "a3b", "w0", "w1", "w2", "w3", "i7", "y1", "y2", "al1", "al", "m1", "m2", "m3", "ma",
+          "ys", "sp", "sp2", "bp", "u", "w", "x", "y", "z0", "z1", "f0", "f1", "dq", "ae", "g0", "g1", "sp3"]
 
     def k(name):
         i = KN.index(name)
@@ -184,22 +183,25 @@ def rank_program(g, core, T, topo):
     def xkeys(r):
         return ["xq%d%d" % (r, j) for j in range(2)]
 
-    def h_products(r):
+    HB = [[0, 1, 2, 3], [6, 7, 4, 5]]
+
+    def h_products(r, j, c, n, keys, which=range(4)):
+        for i in which:
+            mm(HB[j][i], T.wq, T.wp, 128 * i, T["xq%d" % r], T["xp%d" % r], c, n, ["wq", "wp"] + keys)
+
+    def h_tile(r, j, c, n):
+        a = 4 * C * r + 4 * c
         for i in range(4):
-            mm(4 + i, T.wq, T.wp, 128 * i, T["xq%d" % r], T["xp%d" % r], 0, C, ["wq", "wp"] + xkeys(r))
+            act(T.ht[:, a + i:a + 4 * n:4], psum(HB[j][i], n), ["b%d" % HB[j][i]], ["ht%d%d%d" % (r, j, i)], scale=0.03125)
 
-    def h_tile(r):
-        for i in range(4):
-            act(T.ht[:, 4 * C * r + i:4 * C * (r + 1):4], psum(4 + i), ["b%d" % (4 + i)], ["ht%d%d" % (r, i)], scale=0.03125)
-
-    def h_quant(r):
-        quant(T.ht, 4 * C * r, T["hq%d" % r], T["hp%d" % r], 0, C, ["ht%d%d" % (r, i) for i in range(4)], ["hq%d" % r])
-
-    def h_send(r):
-        n = eng(r)
-        send(lambda: remote(r, T["lq%d" % r][:, :].bitcast(dt.uint8), T["hq%d" % r][:, :].bitcast(dt.uint8), "ha%d" % r), ["hq%d" % r], n)
-        send(lambda: remote(r, T["lp%d" % r][:, :], T["hp%d" % r][:, :], "ha%d" % r), ["hq%d" % r], n)
-        arrive("ha%d" % r, 2 * n, ["lq%d" % r])
+    def h_send(r, j, c, m):
+        n, key = len(eng(r)), "hq%d%d" % (r, j)
+        quant(T.ht, 4 * C * r + 4 * c, T["hq%d" % r], T["hp%d" % r], c, m, ["ht%d%d%d" % (r, j, i) for i in range(4)], [key])
+        send(lambda: remote(r, T["lq%d" % r][:, c:c + m].bitcast(dt.uint8), T["hq%d" % r][:, c:c + m].bitcast(dt.uint8), "ha%d" % r, n),
+             [key], n)
+        if c + m == C:
+            send(lambda: remote(r, T["lp%d" % r][:, :], T["hp%d" % r][:, :], "ha%d" % r, n), ["hq%d0" % r, key], n)
+            arrive("ha%d" % r, (j + 2) * n, ["lq%d" % r])
 
     def tau(r):
         return T.tau[:, C * r:C * r + C]
@@ -215,60 +217,83 @@ def rank_program(g, core, T, topo):
         op("v", lambda q: q.tensor_tensor_scan(T.sc[:, o:o + 144], T.r18[:, :], T.ox[:, o + 144:o + 288], 0.0, A.mult, A.add),
            ["r18", "ox%d" % (r + 1)], ["sc" + z])
         tt(T.src[:, s + 128:s + 256], ta2(r).indirect(T.lst[:, 0:8]), T.src[:, s:s + 128], A.mult,
-           ["ta2" + z, "lst", "src" + z], ["src%d" % (r + 1)])
+           ["ta2%d0" % r, "ta2%d1" % r, "lst", "src" + z], ["src%d" % (r + 1)])
         ts(T.key[:, 8 * r:8 * r + 8], T.sc[:, o + 17:o + 144:18], 2.0 ** (r - 1), 63.5, A.mult, A.add, ["sc" + z], ["key" + z])
         cp(T.tb[:, s:s + 128].indirect(T.key[:, 8 * r:8 * r + 8]), T.src[:, s + 128:s + 256], ["key" + z, "src%d" % (r + 1)], ["tb" + z])
-        n = eng(r)
-        send(lambda: remote(r, T.tl[:, s:s + 128], T.tb[:, s:s + 128], "ka" + z), ["tb" + z], n)
+        n = len(eng(r))
+        send(lambda: remote(r, T.tl[:, s:s + 128], T.tb[:, s:s + 128], "ka" + z, n), ["tb" + z], n)
         arrive("ka" + z, n, ["tl" + z])
 
     def own_signs(r):
         z, s = "%d" % r, 128 * r
         if r == 0:
-            act(T.cum[:, 0:128], ta2(0).indirect(T.lst[:, 0:8]), ["ta20", "lst"], ["cum0"])
+            act(T.cum[:, 0:128], ta2(0).indirect(T.lst[:, 0:8]), ["ta200", "lst"], ["cum0"])
         else:
             tt(T.cum[:, s:s + 128], ta2(r).indirect(T.lst[:, 0:8]), T.cum[:, s - 128:s], A.mult,
-               ["ta2" + z, "lst", "cum%d" % (r - 1)], ["cum" + z])
+               ["ta2%d0" % r, "ta2%d1" % r, "lst", "cum%d" % (r - 1)], ["cum" + z])
 
     def pick(out, a, src, lst, n, reads, writes):
         cp(T[out % "q"][:, a:a + n].bitcast(dt.uint32), T[src % "q"][:, 0:C].bitcast(dt.uint32).indirect(lst), reads, [writes + "q"])
         act(T[out % "p"][:, a:a + n], T[src % "p"][:, 0:C].indirect(lst), reads, [writes + "p"])
 
-    def f_part(r):
-        z = "%d" % r
-        pick("f%s" + z, 0, "x%s" + z, T.par[:, 0:36], 2 * C, ["par"] + xkeys(r), "f" + z)
-        for j, (c, n) in enumerate(PART):
-            for h in range(2):
+    def f_pick(r, h):
+        pick("f%%s%d" % r, C * h, "x%%s%d" % r, T.par[:, 18 * h:18 * h + 18], C, ["par"] + xkeys(r), "f%d%d" % (r, h))
+
+    def f_products(r):
+        for h in range(2):
+            for j, (c, n) in enumerate(PART):
                 for i in range(4):
-                    mm(4 * j + i, T.eq, T.ep, 512 * h + 128 * i, T["fq" + z], T["fp" + z], C * h + c, n,
-                       ["eq%d%d" % (h, i), "f" + z + "q", "f" + z + "p"], h == 0, False)
+                    mm(4 * j + i, T.eq, T.ep, 512 * h + 128 * i, T["fq%d" % r], T["fp%d" % r], C * h + c, n,
+                       ["eq%d%d" % (h, i), "f%d%dq" % (r, h), "f%d%dp" % (r, h)], h == 0, False)
 
-    def mapping(r):
-        z, s, a, c = "%d" % r, 128 * r, 304 * r, 576 * r
-        tt(T.t1[:, s:s + 128], T.tl[:, s:s + 128].indirect(T.key[:, 8 * r:8 * r + 8]), T.cum[:, s:s + 128], A.mult,
-           ["tl" + z, "key" + z, "cum" + z], ["t1" + z])
-        tt(T.gg[:, a:a + 304], T.t1[:, s:s + 128].indirect(T.no[:, 0:19]), T.mask[:, :], A.mult, ["t1" + z, "no", "mask"], ["gg" + z])
-        for h in range(2):
-            turn(T.zz[:, c + C * h:c + C * h + C], T.gg[:, a + 16 * h:a + 16 * h + C], ["gg" + z], ["zz%d%d" % (r, h)])
-        for h in range(2):
-            scan(T.zs[:, c + C * h:c + C * h + C], T.zz[:, c + C * h:c + C * h + C], C, ["zz%d%d" % (r, h)], ["zs%d%d" % (r, h)])
-        ts(T.mo[:, 64 * r:64 * r + 64], T.zs[:, c:c + 576].indirect(T.ls[:, 50:54]), 144.0, None, A.add, None,
-           ["zs%d0" % r, "zs%d1" % r, "lsf"], ["mo" + z])
+    TURN = [(16, 0, 160), (0, 160, 192), (176, 352, 128), (160, 480, 160)]
 
-    def mo(r, h, c=0, n=C):
-        a = 64 * r + 32 * h + c // 16
-        return T.mo[:, a:a + n // 16]
+    def turns(i, more=()):
+        a, c, n = TURN[i]
+        turn(T.zz[:, c:c + n], T.gg[:, a:a + n], ["gg0", "ggy", "ggz"] + (["gg1"] if i > 1 else []) + list(more), ["zz%d" % i])
 
     def new_state(r):
-        z, x = "%d" % r, 4 * C * r
-        for j, (c, n) in enumerate(PART):
-            for h in range(2):
-                pick("p%s" + z, C * h + c, "l%s" + z, mo(r, h, c, n), n, ["mo" + z, "lq" + z], "p%d%d%d" % (r, j, h))
-        for j, (c, n) in enumerate(PART):
-            for h in range(2):
-                for i in range(4):
-                    mm(4 * j + i, T.eq, T.ep, 512 * h + 128 * i, T["pq" + z], T["pp" + z], C * h + c, n,
-                       ["p%d%d%dq" % (r, j, h), "p%d%d%dp" % (r, j, h)], False, h == 1)
+        z, s, x = "%d" % r, 128 * r, 4 * C * r
+        tt(T.t1[:, s:s + 128], T.tl[:, s:s + 128].indirect(T.key[:, 8 * r:8 * r + 8]), T.cum[:, s:s + 128], A.mult,
+           ["tl" + z, "key" + z, "cum" + z], ["t1" + z])
+        for j, (c, n) in enumerate(((0, 192), (192, 96))):
+            tt(T.gg[:, 16 + c:16 + c + n], T.t1[:, s:s + 128].indirect(T.no[:, c // 16:(c + n) // 16]), T.mask[:, c:c + n], A.mult,
+               ["t1" + z, "no", "mask"], ["gg%d" % j])
+
+        def sums(i):
+            a, n = TURN[i][1:]
+            scan(T.zs[:, a:a + n], T.zz[:, a:a + n], n, ["zz%d" % i], ["zs%d" % i])
+
+        def lists(j):
+            ts(T.mo[:, 64 * r + 32 * j:64 * r + 32 * j + 32], T.zs[:, 352 * j:352 + C * j].indirect(T.ls[:, 56 + 2 * j:58 + 2 * j]),
+               4.0 ** r, 144.0, A.mult, A.add, ["zs%d" % (2 * j), "zs%d" % (2 * j + 1), "lsf%d" % j], ["mo%d%d" % (r, j)])
+
+        def picks(j, h):
+            c, n = PART[j]
+            a = 64 * r + 32 * j + 16 * h
+            pick("p%s" + z, C * h + c, "l%s" + z, T.mo[:, a:a + n // 16], n, ["mo%d%d" % (r, j), "lq" + z], "p%d%d%d" % (r, j, h))
+            for i in range(4):
+                mm(4 * j + i, T.eq, T.ep, 512 * h + 128 * i, T["pq" + z], T["pp" + z], C * h + c, n,
+                   ["p%d%d%dq" % (r, j, h), "p%d%d%dp" % (r, j, h)], False, h == 1)
+
+        turns(0)
+        turns(1)
+        sums(0)
+        sums(1)
+        turns(2)
+        turns(3)
+        lists(0)
+        sums(2)
+        sums(3)
+        picks(0, 0)
+        lists(1)
+        picks(0, 1)
+        picks(1, 0)
+        picks(1, 1)
+        if r == R - 1:
+            for j in range(2):
+                ts(T.ms[:, 16 * j:16 * j + 16], T.zs[:, 352 * j:352 + C * j].indirect(T.ls[:, 60 + 2 * j:61 + 2 * j]),
+                   4.0 ** r, 144.0, A.mult, A.add, ["zs%d" % (2 * j), "zs%d" % (2 * j + 1), "lsg%d" % j], ["ms%d" % j])
         for j, (c, n) in enumerate(PART):
             for i in range(4):
                 out, key, bank = T.xt[:, x + 4 * c + i:x + 4 * (c + n):4], "xt%d%d%d" % (r, j, i), 4 * j + i
@@ -280,28 +305,21 @@ def rank_program(g, core, T, topo):
                   ["xq%d%d" % (r + 1, j)])
 
     dma("y", lambda q: q.dma_start(T.sei[:, 0:18], T.se[:, :]), [], ["sei"])
-    dma("s", lambda q: q.dma_start(T.xin[:, :], T.x[:, :]), [], ["xin"])
+    dma("y", lambda q: q.dma_start(T.xin[:, :], T.x[:, :]), [], ["xin"])
     dma("y", lambda q: q.dma_start(T.wq[:, :].bitcast(dt.uint8), T.wc[:, :]), [], ["wq"])
     dma("y", lambda q: q.dma_start(T.wp[:, :], T.ws[:, :]), [], ["wp"])
     dma("y", lambda q: q.dma_start(T.uin[:, :], T.u[:, :]), [], ["uin"])
-    dma("y", lambda q: q.dma_start(T.sei[:, 18:20], T.se[:, 0:2]), [], ["sej"])
-    PA = []
-    for i, (buf, c, p0, p1, s0) in enumerate([("pa", 0, 0, 128, 0), ("pa", 18, 0, 112, 16), ("pa", 18, 112, 128, 0),
-                                              ("pb", 0, 16, 128, 0), ("pb", 0, 0, 16, 112), ("pb", 18, 0, 128, 0)]):
-        dma("y", lambda q: q.dma_start(T[buf][p0:p1, c:c + 18], T.se[s0:s0 + p1 - p0, :]), [], ["pa%d" % i])
-        PA.append("pa%d" % i)
-    dma("y", lambda q: q.dma_start(T.vin[:, :], T.v[:, :]), [], ["vin"])
 
     op("g", lambda q: q.iota(T.pi[:, :], [[0, 1]], 0, 1), [], ["pi"])
     iota(T.ij[:, :], [[2, C]], -C, 0, ["ij"])
-    iota(T.t16[:, :], [[0, 19], [1, 16]], 0, 0, ["t16"])
+    iota(T.t16[:, :], [[0, 18], [1, 16]], 0, 0, ["t16"])
     iota(T.kg[:, :], [[1, 20]], 0, 0, ["kg"])
     iota(T.c2[:, :], [[1, 2]], C, 0, ["c2"])
-    iota(T.xf[:, :], [[1, 8], [8, 18]], -16, 0, ["xf"])
+    iota(T.gg[:, 16:160], [[1, 8], [8, 18]], -16, 0, ["gg0"])
     iota(T.tg[:, :], [[1, 16], [0, 8]], 0, 0, ["tg"])
-    iota(T.xf[:, 0:144:18], [[0, 8]], 1, 0, ["xfa"], ["xf"])
-    iota(T.xf[:, 1:144:18], [[0, 4], [1, 2]], 2, 0, ["xfb"], ["xf"])
-    iota(T.xf[:, 2:144:18], [[0, 2], [1, 4]], 4, 0, ["xfc"], ["xf"])
+    iota(T.gg[:, 16:160:18], [[0, 8]], 1, 0, ["xfa"], ["gg0"])
+    iota(T.gg[:, 17:160:18], [[0, 4], [1, 2]], 2, 0, ["xfb"], ["gg0"])
+    iota(T.gg[:, 18:160:18], [[0, 2], [1, 4]], 4, 0, ["xfc"], ["gg0"])
     iota(T.bg[:, :], [[1, 8], [0, 2]], 0, 0, ["bg"])
     iota(T.eg[:, :], [[0, 8], [1, 18]], 0, 0, ["eg"])
     iota(T.off[:, :], [[1, 520]], -3, -4, ["io"])
@@ -313,69 +331,54 @@ def rank_program(g, core, T, topo):
         c = 16 * (d - 1) if d < 5 else 16 * (n + 2)
         iota(T.pk[:, c:c + 16 * n], [[16 // n, n], [1, 2], [16, 8]], 128 * (d + 1) + 2048 * W[d], 0, ["pk%d" % d])
 
-    for d in (7, 6, 5):
-        handed(d)
-
     fill(T.rb[:, 0:16], -float(C), ["rb0"])
     fill(T.v0[:, 0:2], -float(C), ["v00"])
+    fill(T.gg[:, 0:16], 0.0, ["ggy"])
     ts(T.bi[:, 5:6], T.pi[:, :], 15, None, A.bitwise_and, None, ["pi"], ["qi"])
     BI = ["bi%d" % d for d in range(5)]
     for d in range(5):
         ts(T.bi[:, d:d + 1], T.pi[:, :], d, 1, A.arith_shift_right, A.bitwise_and, ["pi"], [BI[d]])
     cp(k("q"), T.bi[:, 5:6], ["qi"], ["q"])
     cp(T.bf[:, :], T.bi[:, 0:5], BI, ["bf"])
+    fill(T.gg[:, 160:320], 0.0, ["ggz"])
     ts(k("ad"), k("q"), 0.0, 576.0, A.is_equal, A.mult, ["q"], ["ad"])
-    for d in range(3):
-        ts(T.k[:, 36 + d:37 + d], k("q"), 2.0 ** (d + 1), None, A.is_ge, None, ["q"], ["gq%d" % d])
-    ts(T.bc[:, :], T.bf[:, 0:4], float(C), None, A.add, None, ["bf"], ["bc"])
     for i in range(2):
         act(T.cw[:, i:2 * C:2], T.ij[:, :], ["ij"], ["cw%d" % i])
+    ts(k("x"), b(0), b(4), None, A.not_equal, None, ["bf"], ["x"])
+    ts(k("y"), k("q"), b(4), 16.0, A.subtract, A.mult, ["q", "bf"], ["y"])
+    ts(T.bc[:, :], T.bf[:, 0:4], float(C), None, A.add, None, ["bf"], ["bc"])
+    ts(k("y1"), k("q"), b(4), 16.0, A.add, A.mult, ["q", "bf"], ["y1"])
+    for j, n in enumerate((176.0, 144.0)):
+        ts(k("z%d" % j), k("x"), n, k("y"), A.mult, A.add, ["x", "y"], ["z%d" % j])
     ts(k("a2"), b(3), 2.0, b(0), A.mult, A.add, ["bf"], ["a2"])
     ts(k("a3b"), b(3), 2.0, b(2), A.mult, A.add, ["bf"], ["a3b"])
-    ts(k("x"), b(0), b(4), 272.0, A.not_equal, A.mult, ["bf"], ["x"])
-    ts(k("y"), k("q"), b(4), 16.0, A.subtract, A.mult, ["q", "bf"], ["y"])
-    ts(k("eh"), k("ad"), b(4), 0.5, A.mult, A.mult, ["ad", "bf"], ["eh"])
-    ts(k("y1"), k("q"), b(4), 16.0, A.add, A.mult, ["q", "bf"], ["y1"])
-    ts(k("z"), k("x"), k("y"), 15.0, A.add, A.add, ["x", "y"], ["z"])
+    for j, n in enumerate((335.0, 271.0)):
+        ts(k("f%d" % j), k("z%d" % j), 15.0, n, A.add, A.min, ["z%d" % j], ["f%d" % j])
     ts(k("a3"), k("a3b"), 2.0, b(0), A.mult, A.add, ["bf", "a3b"], ["a3"])
-    ts(k("y2"), b(0), -8.0, k("y1"), A.mult, A.add, ["bf", "y1"], ["y2"])
     ts(T.diag[:, :], T.t16[:, :], k("q"), None, A.is_equal, None, ["t16", "q"], ["diag"])
-    ts(T.k[:, 34:35], k("z"), k("eh"), None, A.add, None, ["z", "eh"], ["fl0"])
-    ts(T.k[:, 35:36], k("z"), 256.0, 559.0, A.add, A.min, ["z"], ["fl1"])
     act(T.rst[:, :], T.t16[:, :], ["t16"], ["rst"], F.Sign)
-    for d, s in enumerate((0, 3, 2, 1)):
-        lin("w%d" % d, b(s), 2.0 ** (4 - d), -2.0 ** (3 - d), ["bf"])
-    lin("i7", k("q"), 8.0, 128.0, ["q"])
-    ts(k("ma"), e(8), e(10), 0.5, A.add, A.mult, ["diag"], ["ma"])
-    ts(k("sp"), e(10), e(11), None, A.add, None, ["diag"], ["sp"])
-    ts(k("al1"), e(6), 0.5, e(7), A.mult, A.add, ["diag"], ["al1"])
-    ts(k("m1"), e(7), 4.0, e(6), A.mult, A.add, ["diag"], ["m1"])
     ts(T.ls[:, 0:8], T.kg[:, 0:8], 16.0, None, A.mult, None, ["kg"], ["lsu"])
-    ts(k("u"), e(8), e(9), 0.5, A.add, A.mult, ["diag"], ["u"])
-    ts(k("w"), e(10), e(11), 0.5, A.subtract, A.mult, ["diag"], ["w"])
-    ts(k("al"), e(5), 0.25, k("al1"), A.mult, A.add, ["diag", "al1"], ["al"])
-    ts(k("m2"), k("m1"), k("q"), 0.375, A.add, A.subtract, ["m1", "q"], ["m2"])
+    ts(k("ma"), e(8), e(10), 0.5, A.add, A.mult, ["diag"], ["ma"])
+    ts(T.ls[:, 56:58], T.kg[:, 0:2], 16.0, k("f0"), A.mult, A.add, ["kg", "f0"], ["lsf0"])
 
     ts(T.seu[:, 0:1], T.sei[:, 0:1], k("ad"), None, A.add, None, ["sei", "ad"], ["seu0"])
     cp(T.seu[:, 1:18], T.sei[:, 1:18], ["sei"], ["seu1"])
-    cp(T.ls[:, 50:52], T.k[:, 34:36], ["fl0", "fl1"], ["lse"])
-    ts(T.ls[:, 52:54], T.k[:, 34:36], 16.0, None, A.add, None, ["fl0", "fl1"], ["lsf"])
-    cp(T.cw[:, 0:592].indirect(T.seu[:, 0:18]), T.ij[:, :], ["seu0", "seu1", "ij", "cw0", "cw1", "lse"], ["cw"])
+    ts(k("sp"), e(10), e(11), None, A.add, None, ["diag"], ["sp"])
+    ts(k("m1"), e(7), 4.0, e(6), A.mult, A.add, ["diag"], ["m1"])
+    cp(T.cw[:, 0:592].indirect(T.seu[:, 0:18]), T.ij[:, :], ["seu0", "seu1", "ij", "cw0", "cw1"], ["cw"])
 
     act(T.cm[:, 10:11], b(0), ["bf"], ["cm3"])
-    lin("lo", b(4), -1.0, 1.0, ["bf"])
+    for d, s in enumerate((0, 3, 2, 1)):
+        lin("w%d" % d, b(s), 2.0 ** (4 - d), -2.0 ** (3 - d), ["bf"])
+    lin("al1", e(6), 0.5, e(7), ["diag"])
+    lin("m3", k("q"), 1.0, -0.375, ["q"])
+    lin("i7", k("q"), 8.0, 128.0, ["q"])
+    lin("al", e(5), 0.25, k("al1"), ["diag", "al1"])
+    lin("m2", k("m1"), 1.0, k("m3"), ["m1", "m3"])
+    lin("y2", b(0), -8.0, k("y1"), ["bf", "y1"])
     lin("ys", b(3), -0.5, 0.5, ["bf"])
     lin("bp", k("sp"), -1.0, 1.0, ["sp"])
-    lin("sp2", k("sp"), 2.0, 0.0, ["sp"])
-    lin("dq", k("q"), 2.0, 688.0, ["q"])
     lin("ae", k("ad"), 1.0, -0.25, ["ad"])
-    lin("lo2", b(4), -0.5, 0.5, ["bf"])
-    lin("hi2", b(4), 0.5, 0.0, ["bf"])
-    act(T.cm[:, 0:8], T.diag[:, 0:8], ["diag"], ["cm0"])
-    act(T.cm[:, 8:9], k("w"), ["u", "w"], ["cm1"], F.Identity, bias=k("u"))
-    act(T.cm[:, 9:10], k("w"), ["u", "w"], ["cm2"], F.Identity, scale=-1.0, bias=k("u"))
-    act(T.dum[:, :], T.kg[:, 0:18], ["kg", "dq"], ["dum"], F.Identity, scale=32.0, bias=k("dq"))
-    act(T.r18[:, :], T.eg[:, :], ["eg"], ["r18"], F.Sign)
 
     todo = []
 
@@ -390,36 +393,38 @@ def rank_program(g, core, T, topo):
 
     def first_tile():
         quant(T.xin, 0, T.xq0, T.xp0, 0, C, ["xin"], xkeys(0))
-        h_products(0)
-        h_tile(0)
+        h_products(0, 0, 0, C, xkeys(0))
+        h_tile(0, 0, 0, C)
 
     def scorer():
         cp(T.ur[:, :].bitcast(dt.uint32), T.uq[:, 0:128].bitcast(dt.uint32).indirect(T.ls[:, 0:8]), ["uq", "lsu"], ["ur"])
         act(T.urp[:, :], T.up[:, 0:128].indirect(T.ls[:, 0:8]), ["uq", "lsu"], ["urp"])
-        mm(0, T.ur, T.urp, 0, T.xq0, T.xp0, 0, C, ["ur", "urp"] + xkeys(0))
+        mm(4, T.ur, T.urp, 0, T.xq0, T.xp0, 0, C, ["ur", "urp"] + xkeys(0))
 
     later(first_tile)
-    later(tt, T.xm[:, :], T.xf[:, :], T.diag[:, 0:144], A.mult, ["xf", "xfa", "xfb", "xfc", "diag"], ["xm"])
+    later(turns, 0, ["xfa", "xfb", "xfc"])
+    later(turns, 1, ["xfa", "xfb", "xfc"])
     later(ts, T.wh[:, 0:16], T.tg[:, 0:16], 1.0, k("w0"), A.is_equal, A.mult, ["tg", "w0"], ["wh0"])
-    later(scan, T.xs[:, :], T.xm[:, :], 144, ["xm"], ["xs"])
+    later(cp, T.ls[:, 16:32], T.zz[:, 0:352].indirect(T.ls[:, 56:57]), ["zz0", "zz1", "lsf0"], ["lsv"])
     for d, a in ((1, b(0)), (2, k("a2")), (3, k("a3"))):
         later(ts, T.wh[:, 8 * 2 ** d:16 * 2 ** d], T.tg[:, 0:8 * 2 ** d], a, k("w%d" % d), A.is_equal, A.mult,
               ["tg", "bf", "a2", "a3", "w%d" % d], ["wh%d" % d])
-    later(cp, T.ls[:, 16:25], T.xs[:, 15:144:16], ["xs"], ["lsv"])
     later(quant, T.uin, 0, T.uq, T.up, 0, 128, ["uin"], ["uq"])
     later(ts, T.xi[:, :], T.bg[:, :], k("al"), k("m2"), A.mult, A.add, ["bg", "al", "m2"], ["xi"])
     later(scorer)
     later(ts, T.ls[:, 8:16], T.kg[:, 0:8], k("i7"), None, A.add, None, ["kg", "i7"], ["ls7"])
-    later(ts, T.ls[:, 26:42], T.xi[:, :], 16.0, None, A.mult, None, ["xi"], ["lsx"])
-    later(ts, T.ls[:, 42:50], T.kg[:, 0:8], k("y2"), None, A.add, None, ["kg", "y2"], ["lsy"])
-    later(ts, T.pn[:, 0:19], T.sei[:, 0:19], 0.5, 0.25, A.mult, A.subtract, ["sei", "sej"], ["pn0"])
-    later(ts, T.si[:, 0:19], T.sei[:, 0:19], 1, None, A.bitwise_and, None, ["sei", "sej"], ["si"])
-    later(ts, T.pp[:, 0:36], T.pa[:, :], k("lo2"), None, A.mult, None, PA + ["lo2"], ["p1"])
-    later(ts, T.pp[:, 36:72], T.pb[:, :], k("hi2"), 0.25, A.mult, A.subtract, PA + ["hi2"], ["p2"])
-    later(ts, T.pn[:, 0:19:18], T.sei[:, 0:19:18], 0.5, k("ae"), A.mult, A.add, ["sei", "sej", "ae", "pn0"], ["pn1"])
-    later(ts, T.sm[:, 0:19], T.si[:, 0:19], 2048.0, None, A.subtract, None, ["si"], ["sm"])
-    later(tt, T.pp[:, 72:108], T.pp[:, 0:36], T.pp[:, 36:72], A.add, ["p1", "p2"], ["p3"])
-    later(cp, T.par[:, :], T.pp[:, 72:108], ["p3"], ["par"])
+    later(ts, T.ls[:, 32:48], T.xi[:, :], 16.0, None, A.mult, None, ["xi"], ["lsx"])
+    later(ts, T.ls[:, 48:56], T.kg[:, 0:8], k("y2"), None, A.add, None, ["kg", "y2"], ["lsy"])
+    later(ts, T.pn[:, 1:18], T.sei[:, 1:18], 0.5, 0.25, A.mult, A.subtract, ["sei"], ["pn0"])
+    later(ts, T.si[:, :], T.sei[:, :], 1, None, A.bitwise_and, None, ["sei"], ["si"])
+    later(ts, T.pn[:, 0:1], T.sei[:, 0:1], 0.5, k("ae"), A.mult, A.add, ["sei", "ae"], ["pn1"])
+    later(ts, T.sm[:, :], T.si[:, :], 2048.0, None, A.subtract, None, ["si"], ["sm"])
+    for d in range(3):
+        later(ts, T.k[:, 36 + d:37 + d], k("q"), 2.0 ** (d + 1), None, A.is_ge, None, ["q"], ["gq%d" % d])
+    later(ts, k("u"), e(8), e(9), 0.5, A.add, A.mult, ["diag"], ["u"])
+    later(ts, k("w"), e(10), e(11), 0.5, A.subtract, A.mult, ["diag"], ["w"])
+    later(ts, T.ls[:, 58:60], T.kg[:, 0:2], 16.0, k("f1"), A.mult, A.add, ["kg", "f1"], ["lsf1"])
+    later(ts, T.par[:, :], T.pa[:, :], 0.5, 0.25, A.mult, A.subtract, ["pa"], ["par"])
 
     LO = {2: 0, 3: 2, 4: 4, 5: 6, 6: 8, 7: 12}
     RB = {2: 17, 3: 33, 4: 49, 5: 65, 6: 97, 7: 161}
@@ -455,6 +460,11 @@ def rank_program(g, core, T, topo):
     act(T.wt[:, :], T.cw[:, 1:2 * C:2], ["cw"], ["wt"], scale=0.5)
     for i in (9, 11):
         dma("y", lambda q: q.dma_start(T.wd[i:128:16, :], T.wt[i:128:16, :]), ["wd", "wt"], ["wd%d" % i])
+    for i in range(16):
+        h, p = i // 8, 16 * (i % 8)
+        s0 = p - p % 32 + 16 * h
+        dma("y", lambda q: q.dma_start(T.pa[p:p + 16, 18 * h:18 * h + 18], T.se[s0:s0 + 16, :]), [], ["pa"], i > 0)
+    dma("y", lambda q: q.dma_start(T.vin[:, :], T.v[:, :]), [], ["vin"])
     act(T.v0[:, 2:4], T.cw[:, 0:2], ["cw"], ["v01"])
     some()
     ts(T.lo[:, 0:1], T.cw[:, 0:1], d1, T.bc[:, 1:2], A.add, A.add, ["d1", "cw", "bc"], ["lo2"])
@@ -462,55 +472,67 @@ def rank_program(g, core, T, topo):
     lanes(2)
     lanes(3)
     lanes(4)
+    whole(2)
     act(T.ox[:, 0:144], T.wh[:, :].indirect(T.ls[:, 16:25]), ["wh0", "wh1", "wh2", "wh3", "lsv"], ["ox0"])
     iota(T.ox[:, 0:144:18], [[0, 4], [128, 2]], -64, 0, ["oxa"], ["ox0"])
     iota(T.ox[:, 1:144:18], [[0, 2], [64, 2], [0, 2]], -32, 0, ["oxb"], ["ox0"])
     iota(T.ox[:, 2:144:18], [[32, 2], [0, 4]], -16, 0, ["oxc"], ["ox0"])
-    for t in (2, 3, 4):
-        whole(t)
-    h_quant(0)
-    h_send(0)
-    for d in (4, 3, 2, 1):
-        handed(d)
-    iota(T.now[:, 0:1], [[0, 1]], 128 + 2048 * W[0], 0, ["nw1"], ["nw0"])
+    whole(3)
     lanes(5)
+    whole(4)
     whole(5)
-    lanes(6, 2, 2)
+    lanes(6, 2, 2, 0)
     whole(6)
     whole(7)
-    lanes(7, 2, 0, 0)
+    h_send(0, 0, 0, C)
+    for d in (7, 6, 5):
+        handed(d)
+    lanes(7, 2, 2, 0)
     RBS = ["rb%d" % t for t in range(8)]
-    act(T.xx[:, :], T.rb[:, 0:289].indirect(T.ls[:, 26:42]), RBS + ["lsx"], ["xx"])
-    act(tau(0), psum(0), ["b0"], ["tau00", "tau01"], F.Sign, bias=2.0 ** -100)
+    act(T.xx[:, :], T.rb[:, 0:289].indirect(T.ls[:, 32:48]), RBS + ["lsx"], ["xx"])
+    act(tau(0), psum(4), ["b4"], ["tau00", "tau01"], F.Sign, bias=2.0 ** -100)
+    tt(T.same[:, 1:5], T.rb[:, 16:65:16], T.rb[:, 0:49:16], A.is_equal, RBS, ["sa0"])
     tt(T.lm[:, :], T.v0[:, :].indirect(T.ls[:, 8:25]), T.diag[:, 0:272], A.mult,
        ["v00", "v01", "v0t", "v05", "v06", "v07", "ls7", "lsv", "diag"], ["lm"])
-    act(ta2(0), tau(0), ["tau00", "sp", "bp"], ["ta20"], F.Identity, scale=k("sp"), bias=k("bp"))
-    tt(T.same[:, 1:5], T.rb[:, 16:65:16], T.rb[:, 0:49:16], A.is_equal, RBS, ["sa0"])
+    act(T.r18[:, :], T.eg[:, :], ["eg"], ["r18"], F.Sign)
+    act(ta2(0), tau(0), ["tau00", "sp", "bp"], ["ta200", "ta201"], F.Identity, scale=k("sp"), bias=k("bp"))
+    turn(T.yy[:, :], T.xx[:, :], ["xx"], ["yy"])
+    scan(T.lsc[:, :], T.lm[:, :], 272, ["lm"], ["lsc"])
     for s in range(2):
         tt(T.same[:, 5 + s:19:2], T.rb[:, 80 + 16 * s:289:32], T.rb[:, 64:161:16], A.is_equal, RBS, ["sa%d" % (s + 1)])
-    scan(T.lsc[:, :], T.lm[:, :], 272, ["lm"], ["lsc"])
-    turn(T.yy[:, :], T.xx[:, :], ["xx"], ["yy"])
     ts(T.lst[:, 0:17], T.lsc[:, 15:272:16], 0.5, 144.0, A.mult, A.add, ["lsc"], ["lst"])
-    act(T.yg[:, :], T.yy[:, :].indirect(T.ls[:, 42:50]), ["yy", "lsy", "ys"], ["yg"], scale=k("ys"))
+    act(T.yg[:, :], T.yy[:, :].indirect(T.ls[:, 48:56]), ["yy", "lsy", "ys"], ["yg"], scale=k("ys"))
     op("v", lambda q: q.tensor_tensor_scan(T.nr[:, 1:5], T.same[:, 1:5], T.same[:, 1:5], 0.0, A.max, A.max), ["sa0"], ["nr4"])
     ts(T.nn[:, 0:18], T.rb[:, 16:289:16], 400.0, None, A.add, None, RBS, ["n1"])
     table(0, lambda: tt(T.src[:, 0:128], T.wd[:, :].indirect(T.lst[:, 0:8]), T.yg[:, :], A.add,
                         ["wd", "wd9", "wd11", "lst", "yg"], ["src0"]))
+    for d in (4, 3, 2, 1):
+        handed(d)
+    iota(T.now[:, 0:1], [[0, 1]], 128 + 2048 * W[0], 0, ["nw1"], ["nw0"])
 
+    lin("lo", b(4), -1.0, 1.0, ["bf"])
+    lin("dq", k("q"), 2.0, 688.0, ["q"])
     act(T.off[:, :], T.off[:, :], ["io"], ["io"], F.Abs)
-    own_signs(0)
+    act(T.dum[:, :], T.kg[:, 0:18], ["kg", "dq"], ["dum"], F.Identity, scale=32.0, bias=k("dq"))
     act(T.be[:, :], T.off[:, :], ["io", "lo"], ["be"], F.Relu, scale=-1.0, bias=k("lo"))
     act(T.bo[:, :], T.off[:, :], ["io", "bf"], ["bo"], F.Relu, scale=-1.0, bias=b(4))
+    own_signs(0)
+    lin("sp3", k("bp"), -2.0 ** 80, 0.0, ["bp"])
+    act(T.cm[:, 0:8], T.diag[:, 0:8], ["diag"], ["cm0"])
 
     ts(T.nr[:, 5:7], T.same[:, 5:7], T.nr[:, 4:5], None, A.max, None, ["sa1", "sa2", "nr4"], ["nr5"])
-    tt(T.nr[:, 1:4], T.nr[:, 1:4], T.k[:, 36:39], A.max, ["nr4", "gq0", "gq1", "gq2"], ["nr3"])
-    some()
+    some(2)
     for s in range(2):
         tt(T.nr[:, 7 + s:11:2], T.same[:, 7 + s:11:2], T.nr[:, 5:7], A.max, ["sa1", "sa2", "nr5"], ["nr6%d" % s])
     some(2)
     for s in range(2):
         tt(T.nr[:, 11 + s:19:2], T.same[:, 11 + s:19:2], T.nr[:, 7:11], A.max, ["sa1", "sa2", "nr60", "nr61"], ["nr7%d" % s])
+    tt(T.nr[:, 1:4], T.nr[:, 1:4], T.k[:, 36:39], A.max, ["nr4", "gq0", "gq1", "gq2"], ["nr3"])
     some(99)
+    act(T.cm[:, 8:9], k("w"), ["u", "w"], ["cm1"], F.Identity, bias=k("u"))
+    act(T.cm[:, 9:10], k("w"), ["u", "w"], ["cm2"], F.Identity, scale=-1.0, bias=k("u"))
+    for j in range(2):
+        act(T.k[:, 33 + j:34 + j], b(4), ["bf", "f%d" % j], ["g%d" % j], F.Identity, scale=16.0, bias=k("f%d" % j))
     for h in range(2):
         for i in range(4):
             later(quant, T.bo if h else T.be, 3 - i, T.eq, T.ep, 512 * h + 128 * i, 128, ["bo" if h else "be"], ["eq%d%d" % (h, i)])
@@ -522,52 +544,57 @@ def rank_program(g, core, T, topo):
     some()
     cp(T.now[:, :].indirect(T.nu[:, 0:18]), T.pk[:, :], ["nu", "nw0", "nw1"] + ["pk%d" % d for d in range(1, 8)], ["now"])
     some()
-    tt(T.nm[:, :], T.now[:, :].indirect(T.pn[:, 0:19]), T.diag[:, :], A.mult, ["now", "pn0", "pn1", "diag"], ["nm"])
+    tt(T.nm[:, :], T.now[:, :].indirect(T.pn[:, 0:18]), T.diag[:, :], A.mult, ["now", "pn0", "pn1", "diag"], ["nm"])
     some()
-    scan(T.ns[:, :], T.nm[:, :], 304, ["nm"], ["ns"])
+    scan(T.ns[:, :], T.nm[:, :], C, ["nm"], ["ns"])
     some()
-    ts(T.dl[:, 0:19], T.ns[:, 15:304:16], 2.0 ** -11, 0.28, A.mult, A.subtract, ["ns"], ["dl"])
+    ts(T.dl[:, :], T.ns[:, 15:C:16], 2.0 ** -11, 0.28, A.mult, A.subtract, ["ns"], ["dl"])
     some()
-    tt(T.dw[:, 0:19], T.dl[:, 0:19], T.sm[:, 0:19], A.mult, ["dl", "sm"], ["dw"])
+    tt(T.dw[:, 0:18], T.dl[:, :], T.sm[:, :], A.mult, ["dl", "sm"], ["dw"])
     some()
-    tt(T.cd[:, 0:19], T.dw[:, 0:19], T.ns[:, 15:304:16], A.add, ["dw", "ns"], ["cd"])
-    ts(T.cl[:, 0:19], T.cd[:, 0:19], 2.0 ** -7, 0.496, A.mult, A.subtract, ["cd"], ["cl"])
-    ts(T.ni[:, 0:19], T.cd[:, 0:19], 127, None, A.bitwise_and, None, ["cd"], ["ni"])
-    act(T.mask[:, :], T.cm[:, 0:10].indirect(T.cl[:, 0:19]), ["cm0", "cm1", "cm2", "cl"], ["mask"])
-    cp(T.no[:, 0:19], T.ni[:, 0:19], ["ni"], ["no"])
-    f_part(0)
-    mapping(0)
+    tt(T.cd[:, :], T.dw[:, 0:18], T.ns[:, 15:C:16], A.add, ["dw", "ns"], ["cd"])
+    f_pick(0, 0)
+    ts(T.cl[:, :], T.cd[:, :], 2.0 ** -7, 0.496, A.mult, A.subtract, ["cd"], ["cl"])
+    ts(T.ni[:, :], T.cd[:, :], 127, None, A.bitwise_and, None, ["cd"], ["ni"])
+    act(T.mask[:, :], T.cm[:, 0:10].indirect(T.cl[:, :]), ["cm0", "cm1", "cm2", "cl"], ["mask"])
+    f_pick(0, 1)
+    cp(T.no[:, :], T.ni[:, :], ["ni"], ["no"])
+    f_products(0)
     new_state(0)
 
     for r in (1, 2):
         z = "%d" % r
         for j, (c, n) in enumerate(PART):
-            mm(j, T.ur, T.urp, 0, T["xq" + z], T["xp" + z], c, n, ["ur", "urp", "xq%d%d" % (r, j)])
-        h_products(r)
-        for j, (c, n) in enumerate(PART):
-            ts(T.tau[:, C * r + c:C * r + c + n], psum(j, n), 0.0, 0.5, A.is_ge, A.subtract, ["b%d" % j], ["tau%d%d" % (r, j)])
-        h_tile(r)
-        table(r, lambda: ts(ta2(r), tau(r), k("sp2"), k("bp"), A.mult, A.add, ["tau%d0" % r, "tau%d1" % r, "sp2", "bp"], ["ta2" + z]))
-        h_quant(r)
-        h_send(r)
+            key, a, bank = "xq%d%d" % (r, j), C * r + c, "b%d" % (4 + j)
+            h_products(r, j, c, n, [key], range(0, 2 - 2 * j))
+            mm(4 + j, T.ur, T.urp, 0, T["xq" + z], T["xp" + z], c, n, ["ur", "urp", key])
+            ts(T.tau[:, a:a + n], psum(4 + j, n), 0.0, 0.5, A.is_ge, A.subtract, [bank], ["tau%d%d" % (r, j)])
+            ts(T.ta2[:, a:a + n], psum(4 + j, n), k("sp3"), 0.5, A.is_ge, A.subtract, [bank, "sp3"], ["ta2%d%d" % (r, j)])
+            h_products(r, j, c, n, [key], range(2 - 2 * j, 4))
+            h_tile(r, j, c, n)
+        table(r, lambda: h_send(r, 0, *PART[0]))
+        h_send(r, 1, *PART[1])
         own_signs(r)
-        f_part(r)
+        for h in range(2):
+            f_pick(r, h)
+        f_products(r)
         if r == 1:
             quant(T.vin, 0, T.vq, T.vp, 0, 128, ["vin"], ["vq"])
-        mapping(r)
+            cp(T.ls[:, 60:63:2], T.k[:, 33:35], ["g0", "g1"], ["lsg0", "lsg1"])
         new_state(r)
 
     xq, xp = T["xq%d" % R], T["xp%d" % R]
-    for h in range(2):
-        act(T.ims[:, C * h:C * h + C], T.ij[:, :].indirect(mo(R - 1, h)), ["ij", "mo%d" % (R - 1)], ["ims%d" % h], F.Identity,
-            scale=0.5, bias=144.0)
     for j, (c, n) in enumerate(PART):
         mm(j, T.vq, T.vp, 0, xq, xp, c, n, ["vq", "xq%d%d" % (R, j)])
-        cp(T.ys[:, c:c + n], psum(j, n), ["b%d" % j], ["ys%d" % j])
-    dma("y", lambda q: q.dma_start(T.oc[:, :], xq[:, :].bitcast(dt.uint8)), xkeys(R), [])
+        (cp if j else act)(T.ys[:, c:c + n], psum(j, n), ["b%d" % j], ["ys%d" % j])
+        dma("y", lambda q: q.dma_start(T.oc[:, 4 * c:4 * (c + n)], xq[:, c:c + n].bitcast(dt.uint8)), ["xq%d%d" % (R, j)], [])
+        if j == 0:
+            dma("y", lambda q: q.dma_start(T.y[:, c:c + n], T.ys[:, c:c + n]), ["ys0"], [])
+    for j, (c, n) in enumerate(PART):
+        act(T.ims[:, c:c + n], T.ij[:, :].indirect(T.ms[:, 16 * j:16 * j + n // 16]), ["ij", "ms%d" % j], ["ims%d" % j], F.Identity,
+            scale=0.5, bias=144.0)
     for i in range(4):
         dma("y", lambda q: q.dma_start(T.osc[4 * i:4 * i + 4, :], xp[32 * i:32 * i + 4, :]), xkeys(R), [])
-    dma("y", lambda q: q.dma_start(T.y[:, :], T.ys[:, :]), ["ys0", "ys1"], [])
-    for h in range(2):
-        dma("s", lambda q: q.dma_start(T.im[h:8:2, :], T.ims[0:128:32, C * h:C * h + C]), ["ims%d" % h], [])
+    dma("s", lambda q: q.dma_start(T.y[:, c:c + n], T.ys[:, c:c + n]), ["ys1"], [])
+    dma("y", lambda q: q.dma_start(T.im[:, :], T.ims[0:128:16, :]), ["ims0", "ims1"], [])
     finish()

@@ -16,12 +16,13 @@ SCRATCH = {
     "wq": _sb(512, FP8), "wp": _sb(512, U8),
     "uq": _sb(128, FP8), "up": _sb(128, U8), "ur": _sb(128, FP8), "urp": _sb(128, U8),
     "vq": _sb(128, FP8), "vp": _sb(128, U8), "eq": _sb(1024, FP8), "ep": _sb(1024, U8),
-    "off": _sb(520, BF), "be": _sb(520, BF), "bo": _sb(520, BF),
+    "cq": _sb(512, FP8), "cs": _sb(512, U8), "off": _sb(128, BF), "be": _sb(520, BF), "bo": _sb(520, BF),
+    "fb": _sb(4 * C, BF), "fc": _sb(4 * C, BF), "db": _sb(4 * C, BF), "pu": _sb(18, U16),
     "xt": _sb(R * 4 * C, BF), "ht": _sb(R * 4 * C, BF),
     "pi": _sb(1, I32), "bi": _sb(6, I32), "bf": _sb(5, F32), "k": _sb(40, F32), "bc": _sb(4, F32),
-    "ij": _sb(C, BF), "t16": _sb(C, BF), "diag": _sb(C, BF), "rst": _sb(C, BF), "r18": _sb(144, BF), "eg": _sb(144, BF),
+    "ij": _sb(C, BF), "t16": _sb(C, BF), "diag": _sb(C, BF), "rst": _sb(C, BF), "r18": _sb(144, BF),
     "kg": _sb(20, F32), "bg": _sb(16, F32), "tg": _sb(128, BF), "wh": _sb(128, BF),
-    "ls": _sb(64, U16), "xi": _sb(16, I32), "cm": _sb(16, BF), "c2": _sb(2, F32),
+    "ls": _sb(64, U16), "xi": _sb(16, I32), "cm": _sb(16, BF), "c2": _sb(5, F32),
     "dum": _sb(18, F32), "pk": _sb(C, F32),
     "seu": _sb(18, U16), "cw": _sb(592, BF), "lo": _sb(24, U16), "gm": _sb(272, BF), "rb": _sb(304, BF), "v0": _sb(256, BF),
     "lm": _sb(272, BF), "lsc": _sb(272, BF), "lst": _sb(18, U16), "wd": _sb(C, BF), "wt": _sb(C, BF),
@@ -39,7 +40,7 @@ SCRATCH = {
 for _r in range(R + 1):
     SCRATCH["xq%d" % _r], SCRATCH["xp%d" % _r] = _sb(C, FP8), _sb(C, U8)
 for _r in range(R):
-    for _n, _w in (("h", C), ("l", C), ("f", 2 * C), ("p", 2 * C)):
+    for _n, _w in (("h", C), ("l", C), ("f", 2 * C), ("p", 2 * C))[:4 if _r else 2]:
         SCRATCH["%sq%d" % (_n, _r)], SCRATCH["%sp%d" % (_n, _r)] = _sb(_w, FP8), _sb(_w, U8)
 NDMA = 36
 SEMAPHORES = (["cv", "cs", "ct", "cg", "loc"] + ["ha%d" % r for r in range(R)] + ["ka%d" % r for r in range(R)]
@@ -165,7 +166,7 @@ def rank_program(g, core, T, topo):
         op("v", lambda q: q.quantize_mx(q_[:, c:c + n], p_[:, c:c + n], src[:, a:a + 4 * n]), reads, writes)
 
     KN = ["q", "ad", "lo", "a2", "a3", "a3b", "w0", "w1", "w2", "w3", "i7", "y1", "y2", "al1", "al", "m1", "m2", "m3", "ma",
-          "ys", "sp", "sp2", "bp", "u", "w", "x", "y", "z0", "z1", "f0", "f1", "dq", "ae", "g0", "g1", "sp3"]
+          "ys", "sp", "sp2", "bp", "u", "w", "x", "y", "z0", "z1", "f0", "f1", "dq", "h16", "sp3", "u2"]
 
     def k(name):
         i = KN.index(name)
@@ -209,16 +210,18 @@ def rank_program(g, core, T, topo):
     def ta2(r):
         return T.ta2[:, C * r:C * r + C]
 
-    def table(r, between):
+    def table(r, between, gap=lambda: None):
         z, o, s = "%d" % r, 144 * r, 128 * r
         tt(T.ox[:, o + 144:o + 288], tau(r).indirect(T.lst[:, 8:17]), T.ox[:, o:o + 144], A.mult,
            ["tau%d0" % r, "tau%d1" % r, "lst"] + (["ox0", "oxa", "oxb", "oxc"] if r == 0 else ["ox" + z]), ["ox%d" % (r + 1)])
         between()
         op("v", lambda q: q.tensor_tensor_scan(T.sc[:, o:o + 144], T.r18[:, :], T.ox[:, o + 144:o + 288], 0.0, A.mult, A.add),
            ["r18", "ox%d" % (r + 1)], ["sc" + z])
+        gap()
         tt(T.src[:, s + 128:s + 256], ta2(r).indirect(T.lst[:, 0:8]), T.src[:, s:s + 128], A.mult,
            ["ta2%d0" % r, "ta2%d1" % r, "lst", "src" + z], ["src%d" % (r + 1)])
         ts(T.key[:, 8 * r:8 * r + 8], T.sc[:, o + 17:o + 144:18], 2.0 ** (r - 1), 63.5, A.mult, A.add, ["sc" + z], ["key" + z])
+        gap()
         cp(T.tb[:, s:s + 128].indirect(T.key[:, 8 * r:8 * r + 8]), T.src[:, s + 128:s + 256], ["key" + z, "src%d" % (r + 1)], ["tb" + z])
         n = len(eng(r))
         send(lambda: remote(r, T.tl[:, s:s + 128], T.tb[:, s:s + 128], "ka" + z, n), ["tb" + z], n)
@@ -239,26 +242,32 @@ def rank_program(g, core, T, topo):
     def f_pick(r, h):
         pick("f%%s%d" % r, C * h, "x%%s%d" % r, T.par[:, 18 * h:18 * h + 18], C, ["par"] + xkeys(r), "f%d%d" % (r, h))
 
-    def f_products(r):
-        for h in range(2):
+    def f_products(r, h, which):
+        for i in which:
             for j, (c, n) in enumerate(PART):
-                for i in range(4):
-                    mm(4 * j + i, T.eq, T.ep, 512 * h + 128 * i, T["fq%d" % r], T["fp%d" % r], C * h + c, n,
-                       ["eq%d%d" % (h, i), "f%d%dq" % (r, h), "f%d%dp" % (r, h)], h == 0, False)
+                mm(4 * j + i, T.eq, T.ep, 512 * h + 128 * i, T["fq%d" % r], T["fp%d" % r], C * h + c, n,
+                   ["eq%d%d" % (h, i), "f%d%dq" % (r, h), "f%d%dp" % (r, h)], h == 0, False)
 
+    WIDE = [(0, 192), (192, 96)]
     TURN = [(16, 0, 160), (0, 160, 192), (176, 352, 128), (160, 480, 160)]
 
     def turns(i, more=()):
         a, c, n = TURN[i]
         turn(T.zz[:, c:c + n], T.gg[:, a:a + n], ["gg0", "ggy", "ggz"] + (["gg1"] if i > 1 else []) + list(more), ["zz%d" % i])
 
-    def new_state(r):
+    ORDER = [("g", 0), ("g", 1), ("t", 0), ("t", 1), ("s", 0), ("s", 1), ("t", 2), ("t", 3), ("l", 0), ("s", 2), ("s", 3), ("p", 0, 0),
+             ("l", 1), ("p", 0, 1), ("p", 1, 0), ("p", 1, 1)]
+
+    def new_state(r, between=lambda: None):
         z, s, x = "%d" % r, 128 * r, 4 * C * r
         tt(T.t1[:, s:s + 128], T.tl[:, s:s + 128].indirect(T.key[:, 8 * r:8 * r + 8]), T.cum[:, s:s + 128], A.mult,
            ["tl" + z, "key" + z, "cum" + z], ["t1" + z])
-        for j, (c, n) in enumerate(((0, 192), (192, 96))):
+        between()
+
+        def parts(j):
+            c, n = WIDE[j]
             tt(T.gg[:, 16 + c:16 + c + n], T.t1[:, s:s + 128].indirect(T.no[:, c // 16:(c + n) // 16]), T.mask[:, c:c + n], A.mult,
-               ["t1" + z, "no", "mask"], ["gg%d" % j])
+               ["t1" + z, "no", "mask%d" % j], ["gg%d" % j])
 
         def sums(i):
             a, n = TURN[i][1:]
@@ -276,33 +285,33 @@ def rank_program(g, core, T, topo):
                 mm(4 * j + i, T.eq, T.ep, 512 * h + 128 * i, T["pq" + z], T["pp" + z], C * h + c, n,
                    ["p%d%d%dq" % (r, j, h), "p%d%d%dp" % (r, j, h)], False, h == 1)
 
-        turns(0)
-        turns(1)
-        sums(0)
-        sums(1)
-        turns(2)
-        turns(3)
-        lists(0)
-        sums(2)
-        sums(3)
-        picks(0, 0)
-        lists(1)
-        picks(0, 1)
-        picks(1, 0)
-        picks(1, 1)
-        if r == R - 1:
-            for j in range(2):
-                ts(T.ms[:, 16 * j:16 * j + 16], T.zs[:, 352 * j:352 + C * j].indirect(T.ls[:, 60 + 2 * j:61 + 2 * j]),
-                   4.0 ** r, 144.0, A.mult, A.add, ["zs%d" % (2 * j), "zs%d" % (2 * j + 1), "lsg%d" % j], ["ms%d" % j])
-        for j, (c, n) in enumerate(PART):
-            for i in range(4):
-                out, key, bank = T.xt[:, x + 4 * c + i:x + 4 * (c + n):4], "xt%d%d%d" % (r, j, i), 4 * j + i
-                if i % 2 == j:
-                    ts(out, psum(bank, n), 0.5, None, A.mult, None, ["b%d" % bank], [key])
-                else:
-                    act(out, psum(bank, n), ["b%d" % bank], [key], scale=0.5)
+        def single(j):
+            ts(T.ms[:, 16 * j:16 * j + 16], T.zs[:, 352 * j:352 + C * j].indirect(T.ls[:, 60 + 2 * j:61 + 2 * j]),
+               4.0 ** r, 144.0, A.mult, A.add, ["zs%d" % (2 * j), "zs%d" % (2 * j + 1), "lsg%d" % j], ["ms%d" % j])
+
+        def number(j, i):
+            c, n = PART[j]
+            out, key, bank = T.xt[:, x + 4 * c + i:x + 4 * (c + n):4], "xt%d%d%d" % (r, j, i), 4 * j + i
+            if r == 0:
+                tt(out, T.db[:, C * i:C * i + C].indirect(T.ms[:, 16 * j:16 * j + n // 16]), T.fc[:, C * i + c:C * i + c + n], A.add,
+                   ["db%d" % i, "fc%d" % i, "ms%d" % j], [key])
+            elif i % 2 == j:
+                ts(out, psum(bank, n), 0.5, None, A.mult, None, ["b%d" % bank], [key])
+            else:
+                act(out, psum(bank, n), ["b%d" % bank], [key], scale=0.5)
+
+        def codes(j):
+            c, n = PART[j]
             quant(T.xt, x + 4 * c, T["xq%d" % (r + 1)], T["xp%d" % (r + 1)], c, n, ["xt%d%d%d" % (r, j, i) for i in range(4)],
                   ["xq%d%d" % (r + 1, j)])
+
+        rest = [("n", 0, i) for i in range(4)] + [("c", 0)] + [("n", 1, i) for i in range(4)] + [("c", 1)]
+        if r == 0:
+            order = ORDER[:8] + [("m", 0)] + ORDER[9:11] + rest[:1] + [("m", 1)] + rest[1:4] + rest[5:6] + rest[4:5] + rest[6:]
+        else:
+            order = ORDER + ([("m", 0), ("m", 1)] if r == R - 1 else []) + rest
+        for fn, *a in order:
+            {"g": parts, "t": turns, "s": sums, "l": lists, "p": picks, "m": single, "n": number, "c": codes}[fn](*a)
 
     dma("y", lambda q: q.dma_start(T.sei[:, 0:18], T.se[:, :]), [], ["sei"])
     dma("y", lambda q: q.dma_start(T.xin[:, :], T.x[:, :]), [], ["xin"])
@@ -314,23 +323,27 @@ def rank_program(g, core, T, topo):
     iota(T.ij[:, :], [[2, C]], -C, 0, ["ij"])
     iota(T.t16[:, :], [[0, 18], [1, 16]], 0, 0, ["t16"])
     iota(T.kg[:, :], [[1, 20]], 0, 0, ["kg"])
-    iota(T.c2[:, :], [[1, 2]], C, 0, ["c2"])
+    iota(T.c2[:, 0:2], [[1, 2]], C, 0, ["c2"])
     iota(T.gg[:, 16:160], [[1, 8], [8, 18]], -16, 0, ["gg0"])
     iota(T.tg[:, :], [[1, 16], [0, 8]], 0, 0, ["tg"])
     iota(T.gg[:, 16:160:18], [[0, 8]], 1, 0, ["xfa"], ["gg0"])
     iota(T.gg[:, 17:160:18], [[0, 4], [1, 2]], 2, 0, ["xfb"], ["gg0"])
     iota(T.gg[:, 18:160:18], [[0, 2], [1, 4]], 4, 0, ["xfc"], ["gg0"])
     iota(T.bg[:, :], [[1, 8], [0, 2]], 0, 0, ["bg"])
-    iota(T.eg[:, :], [[0, 8], [1, 18]], 0, 0, ["eg"])
-    iota(T.off[:, :], [[1, 520]], -3, -4, ["io"])
-    iota(T.now[:, :], [[0, 592]], 0, 0, ["nw0"])
+    iota(T.off[:, :], [[1, 128]], 0, -1, ["io"])
+    iota(T.c2[:, 2:4], [[2, 2]], 2, 0, ["c3"])
+    iota(T.c2[:, 4:5], [[0, 1]], 8, 0, ["c4"])
+    iota(T.now[:, 1:296], [[0, 295]], 0, 0, ["nw0"])
     W = [16, 32, 64, 1, 8, 4, 2, 128]
-
-    def handed(d):
+    iota(T.now[:, 0:1], [[0, 1]], 128 + 2048 * W[0], 0, ["nw1"])
+    for d in range(1, 8):
         n = max(1, 2 ** (d - 4))
         c = 16 * (d - 1) if d < 5 else 16 * (n + 2)
         iota(T.pk[:, c:c + 16 * n], [[16 // n, n], [1, 2], [16, 8]], 128 * (d + 1) + 2048 * W[d], 0, ["pk%d" % d])
 
+    fill(T.bo[:, 0:130], 0.0, ["bo0"])
+    for i in range(1, 4):
+        act(T.bo[:, 130 * i:130 * i + 130], T.bo[:, 0:130], ["bo0"], ["bo%d" % i])
     fill(T.rb[:, 0:16], -float(C), ["rb0"])
     fill(T.v0[:, 0:2], -float(C), ["v00"])
     fill(T.gg[:, 0:16], 0.0, ["ggy"])
@@ -378,7 +391,7 @@ def rank_program(g, core, T, topo):
     lin("y2", b(0), -8.0, k("y1"), ["bf", "y1"])
     lin("ys", b(3), -0.5, 0.5, ["bf"])
     lin("bp", k("sp"), -1.0, 1.0, ["sp"])
-    lin("ae", k("ad"), 1.0, -0.25, ["ad"])
+    lin("h16", b(4), 16.0, 0.0, ["bf"])
 
     todo = []
 
@@ -391,17 +404,11 @@ def rank_program(g, core, T, topo):
                 fn, a = todo.pop(0)
                 fn(*a)
 
-    def first_tile():
-        quant(T.xin, 0, T.xq0, T.xp0, 0, C, ["xin"], xkeys(0))
-        h_products(0, 0, 0, C, xkeys(0))
-        h_tile(0, 0, 0, C)
-
     def scorer():
         cp(T.ur[:, :].bitcast(dt.uint32), T.uq[:, 0:128].bitcast(dt.uint32).indirect(T.ls[:, 0:8]), ["uq", "lsu"], ["ur"])
         act(T.urp[:, :], T.up[:, 0:128].indirect(T.ls[:, 0:8]), ["uq", "lsu"], ["urp"])
         mm(4, T.ur, T.urp, 0, T.xq0, T.xp0, 0, C, ["ur", "urp"] + xkeys(0))
 
-    later(first_tile)
     later(turns, 0, ["xfa", "xfb", "xfc"])
     later(turns, 1, ["xfa", "xfb", "xfc"])
     later(ts, T.wh[:, 0:16], T.tg[:, 0:16], 1.0, k("w0"), A.is_equal, A.mult, ["tg", "w0"], ["wh0"])
@@ -415,16 +422,11 @@ def rank_program(g, core, T, topo):
     later(ts, T.ls[:, 8:16], T.kg[:, 0:8], k("i7"), None, A.add, None, ["kg", "i7"], ["ls7"])
     later(ts, T.ls[:, 32:48], T.xi[:, :], 16.0, None, A.mult, None, ["xi"], ["lsx"])
     later(ts, T.ls[:, 48:56], T.kg[:, 0:8], k("y2"), None, A.add, None, ["kg", "y2"], ["lsy"])
-    later(ts, T.pn[:, 1:18], T.sei[:, 1:18], 0.5, 0.25, A.mult, A.subtract, ["sei"], ["pn0"])
+    later(ts, T.pn[:, :], T.seu[:, :], 0.5, 0.25, A.mult, A.subtract, ["seu0", "seu1"], ["pn"])
     later(ts, T.si[:, :], T.sei[:, :], 1, None, A.bitwise_and, None, ["sei"], ["si"])
-    later(ts, T.pn[:, 0:1], T.sei[:, 0:1], 0.5, k("ae"), A.mult, A.add, ["sei", "ae"], ["pn1"])
+    later(ts, T.k[:, 36:39], T.c2[:, 2:5], k("q"), None, A.is_le, None, ["q", "c3", "c4"], ["gq"])
     later(ts, T.sm[:, :], T.si[:, :], 2048.0, None, A.subtract, None, ["si"], ["sm"])
-    for d in range(3):
-        later(ts, T.k[:, 36 + d:37 + d], k("q"), 2.0 ** (d + 1), None, A.is_ge, None, ["q"], ["gq%d" % d])
-    later(ts, k("u"), e(8), e(9), 0.5, A.add, A.mult, ["diag"], ["u"])
-    later(ts, k("w"), e(10), e(11), 0.5, A.subtract, A.mult, ["diag"], ["w"])
-    later(ts, T.ls[:, 58:60], T.kg[:, 0:2], 16.0, k("f1"), A.mult, A.add, ["kg", "f1"], ["lsf1"])
-    later(ts, T.par[:, :], T.pa[:, :], 0.5, 0.25, A.mult, A.subtract, ["pa"], ["par"])
+    later(ts, T.pu[:, :], T.sei[:, :], 0.5, 0.25, A.mult, A.subtract, ["sei"], ["pu"])
 
     LO = {2: 0, 3: 2, 4: 4, 5: 6, 6: 8, 7: 12}
     RB = {2: 17, 3: 33, 4: 49, 5: 65, 6: 97, 7: 161}
@@ -444,7 +446,7 @@ def rank_program(g, core, T, topo):
         if t < 4:
             ts(T.lo[:, LO[t + 1]:LO[t + 1] + 1], ends, T.bc[:, t:t + 1], None, A.add, None, ["rb%d" % t, "bc"], ["lo%d" % (t + 1)])
         elif t == 4:
-            ts(T.lo[:, 6:8], T.c2[:, :], ends, None, A.add, None, ["rb4", "c2"], ["lo5"])
+            ts(T.lo[:, 6:8], T.c2[:, 0:2], ends, None, A.add, None, ["rb4", "c2"], ["lo5"])
         elif t < 7:
             for s in range(2):
                 ts(T.lo[:, LO[t + 1] + s:LO[t + 1] + n // 8:2], ends, float(C + s), None, A.add, None, ["rb%d" % t], ["lo%d%s" % (t + 1, "ab"[s])])
@@ -455,6 +457,7 @@ def rank_program(g, core, T, topo):
         act(T.v0[:, 2 ** t:2 ** t + max(16, 2 ** t)], kid, deps, ["v0t" if t < 5 else "v0%d" % t])
 
     d1 = T.dw[:, 19:20]
+    quant(T.xin, 0, T.xq0, T.xp0, 0, C, ["xin"], xkeys(0))
     ts(d1, T.cw[:, 1:2], T.cw[:, 0:1], T.cm[:, 10:11], A.subtract, A.mult, ["cw", "cm3"], ["d1"])
     act(T.wd[:, :], T.cw[:, 0:2 * C:2], ["cw", "ma"], ["wd"], scale=k("ma"))
     act(T.wt[:, :], T.cw[:, 1:2 * C:2], ["cw"], ["wt"], scale=0.5)
@@ -466,7 +469,9 @@ def rank_program(g, core, T, topo):
         dma("y", lambda q: q.dma_start(T.pa[p:p + 16, 18 * h:18 * h + 18], T.se[s0:s0 + 16, :]), [], ["pa"], i > 0)
     dma("y", lambda q: q.dma_start(T.vin[:, :], T.v[:, :]), [], ["vin"])
     act(T.v0[:, 2:4], T.cw[:, 0:2], ["cw"], ["v01"])
-    some()
+    h_products(0, 0, 0, C, xkeys(0))
+    h_tile(0, 0, 0, C)
+    some(2)
     ts(T.lo[:, 0:1], T.cw[:, 0:1], d1, T.bc[:, 1:2], A.add, A.add, ["d1", "cw", "bc"], ["lo2"])
     ts(T.rb[:, 16:17], d1, T.cw[:, 0:1], None, A.add, None, ["d1", "cw"], ["rb1"])
     lanes(2)
@@ -478,74 +483,94 @@ def rank_program(g, core, T, topo):
     iota(T.ox[:, 1:144:18], [[0, 2], [64, 2], [0, 2]], -32, 0, ["oxb"], ["ox0"])
     iota(T.ox[:, 2:144:18], [[32, 2], [0, 4]], -16, 0, ["oxc"], ["ox0"])
     whole(3)
+    act(T.off[:, :], T.off[:, :], ["io"], ["io"], F.Abs)
     lanes(5)
     whole(4)
+    act(T.bo[:, 3:515:4], T.off[:, :], ["io", "bo1", "bo2", "bo3"], ["bo", "bo0"], F.Relu, scale=-1.0, bias=1.0)
     whole(5)
     lanes(6, 2, 2, 0)
     whole(6)
     whole(7)
     h_send(0, 0, 0, C)
-    for d in (7, 6, 5):
-        handed(d)
-    lanes(7, 2, 2, 0)
+
+    def whole_tile(i):
+        quant(T.bo, 3 - i, T.cq, T.cs, 128 * i, 128, ["bo"], ["cq%d" % i])
+
+    later(whole_tile, 0)
+    lanes(7, 99, 0, 0)
     RBS = ["rb%d" % t for t in range(8)]
-    act(T.xx[:, :], T.rb[:, 0:289].indirect(T.ls[:, 32:48]), RBS + ["lsx"], ["xx"])
     act(tau(0), psum(4), ["b4"], ["tau00", "tau01"], F.Sign, bias=2.0 ** -100)
-    tt(T.same[:, 1:5], T.rb[:, 16:65:16], T.rb[:, 0:49:16], A.is_equal, RBS, ["sa0"])
+    lin("dq", k("q"), 2.0, 720.0, ["q"])
+    act(T.xx[:, :], T.rb[:, 0:289].indirect(T.ls[:, 32:48]), RBS + ["lsx"], ["xx"])
+    act(T.dum[:, :], T.kg[:, 0:18], ["kg", "dq"], ["dum"], F.Identity, scale=32.0, bias=k("dq"))
+    act(T.nn[:, 0:18], T.rb[:, 16:289:16], RBS, ["n1"], F.Identity, bias=400.0)
+
+    def pair(fn):
+        later(lambda: [fn(s) for s in range(2)])
+
+    later(tt, T.same[:, 1:5], T.rb[:, 16:65:16], T.rb[:, 0:49:16], A.is_equal, RBS, ["sa0"])
+    pair(lambda s: tt(T.same[:, 5 + s:19:2], T.rb[:, 80 + 16 * s:289:32], T.rb[:, 64:161:16], A.is_equal, RBS, ["sa%d" % (s + 1)]))
+    later(op, "v", lambda q: q.tensor_tensor_scan(T.nr[:, 1:5], T.same[:, 1:5], T.same[:, 1:5], 0.0, A.max, A.max), ["sa0"], ["nr4"])
+    later(ts, T.nr[:, 5:7], T.same[:, 5:7], T.nr[:, 4:5], None, A.max, None, ["sa1", "sa2", "nr4"], ["nr5"])
+    later(tt, T.nr[:, 1:4], T.nr[:, 1:4], T.k[:, 36:39], A.max, ["nr4", "gq"], ["nr3"])
+    pair(lambda s: tt(T.nr[:, 7 + s:11:2], T.same[:, 7 + s:11:2], T.nr[:, 5:7], A.max, ["sa1", "sa2", "nr5"], ["nr6%d" % s]))
+    pair(lambda s: tt(T.nr[:, 11 + s:19:2], T.same[:, 11 + s:19:2], T.nr[:, 7:11], A.max, ["sa1", "sa2", "nr60", "nr61"], ["nr7%d" % s]))
+    later(tt, T.nn[:, 18:36], T.nr[:, 1:19], T.dum[:, :], A.mult, ["nr3", "nr4", "nr5", "nr60", "nr61", "nr70", "nr71", "dum"], ["n2"])
+    later(tt, T.nn[:, 36:54], T.nn[:, 0:18], T.nn[:, 18:36], A.max, ["n1", "n2"], ["n3"])
+    later(ts, T.nu[:, :], T.nn[:, 36:54], 0.5, 56.0, A.mult, A.subtract, ["n3"], ["nu"])
+
+    whole_tile(1)
+    some()
     tt(T.lm[:, :], T.v0[:, :].indirect(T.ls[:, 8:25]), T.diag[:, 0:272], A.mult,
        ["v00", "v01", "v0t", "v05", "v06", "v07", "ls7", "lsv", "diag"], ["lm"])
-    act(T.r18[:, :], T.eg[:, :], ["eg"], ["r18"], F.Sign)
-    act(ta2(0), tau(0), ["tau00", "sp", "bp"], ["ta200", "ta201"], F.Identity, scale=k("sp"), bias=k("bp"))
-    turn(T.yy[:, :], T.xx[:, :], ["xx"], ["yy"])
+    some(2)
     scan(T.lsc[:, :], T.lm[:, :], 272, ["lm"], ["lsc"])
-    for s in range(2):
-        tt(T.same[:, 5 + s:19:2], T.rb[:, 80 + 16 * s:289:32], T.rb[:, 64:161:16], A.is_equal, RBS, ["sa%d" % (s + 1)])
-    ts(T.lst[:, 0:17], T.lsc[:, 15:272:16], 0.5, 144.0, A.mult, A.add, ["lsc"], ["lst"])
+    turn(T.yy[:, :], T.xx[:, :], ["xx"], ["yy"])
+    act(T.r18[:, :], T.gg[:, 16:160], ["gg0", "xfa", "xfb", "xfc"], ["r18"], F.Sign, bias=-1.0)
     act(T.yg[:, :], T.yy[:, :].indirect(T.ls[:, 48:56]), ["yy", "lsy", "ys"], ["yg"], scale=k("ys"))
-    op("v", lambda q: q.tensor_tensor_scan(T.nr[:, 1:5], T.same[:, 1:5], T.same[:, 1:5], 0.0, A.max, A.max), ["sa0"], ["nr4"])
-    ts(T.nn[:, 0:18], T.rb[:, 16:289:16], 400.0, None, A.add, None, RBS, ["n1"])
-    table(0, lambda: tt(T.src[:, 0:128], T.wd[:, :].indirect(T.lst[:, 0:8]), T.yg[:, :], A.add,
-                        ["wd", "wd9", "wd11", "lst", "yg"], ["src0"]))
-    for d in (4, 3, 2, 1):
-        handed(d)
-    iota(T.now[:, 0:1], [[0, 1]], 128 + 2048 * W[0], 0, ["nw1"], ["nw0"])
-
-    lin("lo", b(4), -1.0, 1.0, ["bf"])
-    lin("dq", k("q"), 2.0, 688.0, ["q"])
-    act(T.off[:, :], T.off[:, :], ["io"], ["io"], F.Abs)
-    act(T.dum[:, :], T.kg[:, 0:18], ["kg", "dq"], ["dum"], F.Identity, scale=32.0, bias=k("dq"))
-    act(T.be[:, :], T.off[:, :], ["io", "lo"], ["be"], F.Relu, scale=-1.0, bias=k("lo"))
-    act(T.bo[:, :], T.off[:, :], ["io", "bf"], ["bo"], F.Relu, scale=-1.0, bias=b(4))
-    own_signs(0)
-    lin("sp3", k("bp"), -2.0 ** 80, 0.0, ["bp"])
-    act(T.cm[:, 0:8], T.diag[:, 0:8], ["diag"], ["cm0"])
-
-    ts(T.nr[:, 5:7], T.same[:, 5:7], T.nr[:, 4:5], None, A.max, None, ["sa1", "sa2", "nr4"], ["nr5"])
-    some(2)
-    for s in range(2):
-        tt(T.nr[:, 7 + s:11:2], T.same[:, 7 + s:11:2], T.nr[:, 5:7], A.max, ["sa1", "sa2", "nr5"], ["nr6%d" % s])
-    some(2)
-    for s in range(2):
-        tt(T.nr[:, 11 + s:19:2], T.same[:, 11 + s:19:2], T.nr[:, 7:11], A.max, ["sa1", "sa2", "nr60", "nr61"], ["nr7%d" % s])
-    tt(T.nr[:, 1:4], T.nr[:, 1:4], T.k[:, 36:39], A.max, ["nr4", "gq0", "gq1", "gq2"], ["nr3"])
+    act(ta2(0), tau(0), ["tau00", "sp", "bp"], ["ta200", "ta201"], F.Identity, scale=k("sp"), bias=k("bp"))
+    ts(T.lst[:, 0:17], T.lsc[:, 15:272:16], 0.5, 144.0, A.mult, A.add, ["lsc"], ["lst"])
+    some()
+    whole_tile(2)
+    table(0, lambda: (some(2), tt(T.src[:, 0:128], T.wd[:, :].indirect(T.lst[:, 0:8]), T.yg[:, :], A.add,
+                                  ["wd", "wd9", "wd11", "lst", "yg"], ["src0"]), some()), some)
     some(99)
-    act(T.cm[:, 8:9], k("w"), ["u", "w"], ["cm1"], F.Identity, bias=k("u"))
-    act(T.cm[:, 9:10], k("w"), ["u", "w"], ["cm2"], F.Identity, scale=-1.0, bias=k("u"))
-    for j in range(2):
-        act(T.k[:, 33 + j:34 + j], b(4), ["bf", "f%d" % j], ["g%d" % j], F.Identity, scale=16.0, bias=k("f%d" % j))
-    for h in range(2):
+    whole_tile(3)
+
+    def unpack(name, q_, p_, bank, keys, which):
+        for i in which:
+            mm(bank + i, T.cq, T.cs, 128 * i, q_, p_, 0, C, ["cq%d" % i] + keys)
+            act(T[name][:, C * i:C * i + C], psum(bank + i), ["b%d" % (bank + i)], [name + "%d" % i], scale=0.5)
+
+    def parents(i):
+        act(T.fc[:, C * i:C * i + C], T.fb[:, C * i:C * i + C].indirect(T.pu[:, :]), ["fb%d" % i, "pu"], ["fc%d" % i])
+
+    iota(T.be[:, :], [[0, 520]], 0, 0, ["bez"])
+    lin("lo", b(4), -1.0, 1.0, ["bf"])
+    lin("u", e(8), 1.0, e(9), ["diag"])
+    lin("w", e(11), -1.0, e(10), ["diag"])
+    own_signs(0)
+    lin("u2", k("u"), 0.5, 0.0, ["u"])
+    unpack("fb", T.xq0, T.xp0, 4, xkeys(0), range(3))
+    act(T.cm[:, 8:9], k("w"), ["u2", "w"], ["cm1"], F.Identity, scale=0.5, bias=k("u2"))
+    act(T.cm[:, 9:10], k("w"), ["u2", "w"], ["cm2"], F.Identity, scale=-0.5, bias=k("u2"))
+    act(T.cm[:, 0:8], T.diag[:, 0:8], ["diag"], ["cm0"])
+    unpack("fb", T.xq0, T.xp0, 4, xkeys(0), [3])
+    act(T.bo[:, 3:515:4], T.off[:, :], ["io", "bf"], ["bo"], F.Relu, scale=-1.0, bias=b(4))
+    parents(0)
+    parents(1)
+    act(T.be[:, 3:515:4], T.off[:, :], ["io", "lo", "bez"], ["be"], F.Relu, scale=-1.0, bias=k("lo"))
+    unpack("db", T.lq0, T.lp0, 0, ["lq0"], range(2))
+    later(ts, T.ls[:, 60:63:2], T.k[:, 29:31], k("h16"), None, A.add, None, ["f0", "f1", "h16"], ["lsg0", "lsg1"])
+    later(ts, T.ls[:, 58:60], T.kg[:, 0:2], 16.0, k("f1"), A.mult, A.add, ["kg", "f1"], ["lsf1"])
+    later(ts, T.par[:, :], T.pa[:, :], 0.5, 0.25, A.mult, A.subtract, ["pa"], ["par"])
+    for h in (1, 0):
         for i in range(4):
             later(quant, T.bo if h else T.be, 3 - i, T.eq, T.ep, 512 * h + 128 * i, 128, ["bo" if h else "be"], ["eq%d%d" % (h, i)])
-    tt(T.nn[:, 18:36], T.nr[:, 1:19], T.dum[:, :], A.mult, ["nr3", "nr4", "nr5", "nr60", "nr61", "nr70", "nr71", "dum"], ["n2"])
-    some()
-    tt(T.nn[:, 36:54], T.nn[:, 0:18], T.nn[:, 18:36], A.max, ["n1", "n2"], ["n3"])
-    some()
-    ts(T.nu[:, :], T.nn[:, 36:54], 0.5, 56.0, A.mult, A.subtract, ["n3"], ["nu"])
-    some()
     cp(T.now[:, :].indirect(T.nu[:, 0:18]), T.pk[:, :], ["nu", "nw0", "nw1"] + ["pk%d" % d for d in range(1, 8)], ["now"])
-    some()
-    tt(T.nm[:, :], T.now[:, :].indirect(T.pn[:, 0:18]), T.diag[:, :], A.mult, ["now", "pn0", "pn1", "diag"], ["nm"])
-    some()
+    some(2)
+    tt(T.nm[:, :], T.now[:, 0:296].indirect(T.pn[:, 0:18]), T.diag[:, :], A.mult, ["now", "pn", "diag"], ["nm"])
+    some(2)
     scan(T.ns[:, :], T.nm[:, :], C, ["nm"], ["ns"])
     some()
     ts(T.dl[:, :], T.ns[:, 15:C:16], 2.0 ** -11, 0.28, A.mult, A.subtract, ["ns"], ["dl"])
@@ -553,14 +578,16 @@ def rank_program(g, core, T, topo):
     tt(T.dw[:, 0:18], T.dl[:, :], T.sm[:, :], A.mult, ["dl", "sm"], ["dw"])
     some()
     tt(T.cd[:, :], T.dw[:, 0:18], T.ns[:, 15:C:16], A.add, ["dw", "ns"], ["cd"])
-    f_pick(0, 0)
+    some()
     ts(T.cl[:, :], T.cd[:, :], 2.0 ** -7, 0.496, A.mult, A.subtract, ["cd"], ["cl"])
     ts(T.ni[:, :], T.cd[:, :], 127, None, A.bitwise_and, None, ["cd"], ["ni"])
-    act(T.mask[:, :], T.cm[:, 0:10].indirect(T.cl[:, :]), ["cm0", "cm1", "cm2", "cl"], ["mask"])
-    f_pick(0, 1)
-    cp(T.no[:, :], T.ni[:, :], ["ni"], ["no"])
-    f_products(0)
-    new_state(0)
+    for j, (c, n) in enumerate(WIDE):
+        act(T.mask[:, c:c + n], T.cm[:, 0:10].indirect(T.cl[:, c // 16:(c + n) // 16]), ["cm0", "cm1", "cm2", "cl"], ["mask%d" % j])
+    parents(2)
+    unpack("db", T.lq0, T.lp0, 0, ["lq0"], range(2, 4))
+    parents(3)
+    lin("sp3", k("bp"), -2.0 ** 80, 0.0, ["bp"])
+    new_state(0, lambda: (cp(T.no[:, :], T.ni[:, :], ["ni"], ["no"]), some()))
 
     for r in (1, 2):
         z = "%d" % r
@@ -577,10 +604,10 @@ def rank_program(g, core, T, topo):
         own_signs(r)
         for h in range(2):
             f_pick(r, h)
-        f_products(r)
-        if r == 1:
+            some(99)
+            f_products(r, h, range(4))
+        if r == 2:
             quant(T.vin, 0, T.vq, T.vp, 0, 128, ["vin"], ["vq"])
-            cp(T.ls[:, 60:63:2], T.k[:, 33:35], ["g0", "g1"], ["lsg0", "lsg1"])
         new_state(r)
 
     xq, xp = T["xq%d" % R], T["xp%d" % R]

from concourse.mybir import dt, AluOpType, ActivationFunctionType

N, C, R = 8, 288, 3
STEP = [2, 4, 1]
PART = [(0, 160), (160, 128)]
A, F = AluOpType, ActivationFunctionType
BF, F32, I32, U16, FP8, U8 = "bfloat16", "float32", "int32", "uint16", "float8_e4m3fn_x4", "uint8"


def _sb(n, d):
    return ("sbuf", [128, n], d)


SCRATCH = {
    "xin": _sb(4 * C, BF), "uin": _sb(512, BF), "vin": _sb(512, BF), "sei": _sb(18, I32), "pa": _sb(36, I32),
    "wq": _sb(512, FP8), "wp": _sb(512, U8),
    "uq": _sb(128, FP8), "up": _sb(128, U8), "ur": _sb(128, FP8), "urp": _sb(128, U8),
    "vq": _sb(128, FP8), "vp": _sb(128, U8), "eq": _sb(1024, FP8), "ep": _sb(1024, U8),
    "cq": _sb(512, FP8), "cs": _sb(512, U8), "off": _sb(128, BF), "be": _sb(520, BF), "bo": _sb(520, BF),
    "fb": _sb(4 * C, BF), "fc": _sb(4 * C, BF), "db": _sb(4 * C, BF), "pu": _sb(18, U16),
    "xt": _sb(R * 4 * C, BF), "ht": _sb(R * 4 * C, BF),
    "pi": _sb(1, I32), "bi": _sb(6, I32), "bf": _sb(5, F32), "k": _sb(40, F32), "bc": _sb(4, F32),
    "ij": _sb(C, BF), "t16": _sb(C, BF), "diag": _sb(C, BF), "rst": _sb(C, BF), "r18": _sb(144, BF),
    "kg": _sb(20, F32), "bg": _sb(16, F32), "tg": _sb(128, BF), "wh": _sb(128, BF),
    "ls": _sb(64, U16), "xi": _sb(16, I32), "cm": _sb(16, BF), "c2": _sb(5, F32),
    "dum": _sb(18, F32), "pk": _sb(C, F32),
    "seu": _sb(18, U16), "cw": _sb(592, BF), "lo": _sb(24, U16), "gm": _sb(272, BF), "rb": _sb(304, BF), "v0": _sb(256, BF),
    "lm": _sb(272, BF), "lsc": _sb(272, BF), "lst": _sb(18, U16), "wd": _sb(C, BF), "wt": _sb(C, BF),
    "xx": _sb(256, BF), "yy": _sb(256, BF), "yg": _sb(128, BF),
    "same": _sb(20, F32), "nr": _sb(20, F32), "nn": _sb(54, F32), "nu": _sb(18, U16),
    "now": _sb(592, F32), "pn": _sb(18, U16), "nm": _sb(C, F32), "ns": _sb(C, F32), "si": _sb(18, I32), "sm": _sb(18, F32),
    "dl": _sb(18, I32), "dw": _sb(20, F32), "cd": _sb(18, I32), "ni": _sb(18, I32), "no": _sb(18, U16), "cl": _sb(18, U16),
    "mask": _sb(C, BF), "par": _sb(36, U16),
    "tau": _sb(R * C, BF), "ta2": _sb(R * C, BF), "ox": _sb((R + 1) * 144, BF), "sc": _sb(R * 144, BF), "key": _sb(R * 8, U16),
    "src": _sb((R + 1) * 128, BF), "cum": _sb(R * 128, BF), "tb": _sb(R * 128, BF), "tl": _sb(R * 128, BF), "t1": _sb(R * 128, BF),
    "gg": _sb(320, BF), "zz": _sb(640, BF), "zs": _sb(640, BF), "mo": _sb(R * 64, U16), "ms": _sb(32, U16),
    "ims": _sb(C, F32), "ys": _sb(C, F32),
    "ps": ("psum", [128, 4096], F32),
}
for _r in range(R + 1):
    SCRATCH["xq%d" % _r], SCRATCH["xp%d" % _r] = _sb(C, FP8), _sb(C, U8)
for _r in range(R):
    for _n, _w in (("h", C), ("l", C), ("f", 2 * C), ("p", 2 * C))[:4 if _r else 2]:
        SCRATCH["%sq%d" % (_n, _r)], SCRATCH["%sp%d" % (_n, _r)] = _sb(_w, FP8), _sb(_w, U8)
NDMA = 36
SEMAPHORES = (["cv", "cs", "ct", "cg", "loc"] + ["ha%d" % r for r in range(R)] + ["ka%d" % r for r in range(R)]
              + ["d%d" % i for i in range(NDMA)])


def tracker(g, T):
    qs = {"v": g.vector, "s": g.scalar, "t": g.tensor, "g": g, "y": g.sync}
    own = {"v": "cv", "s": "cs", "t": "ct", "g": "cg"}
    total, waited = {}, {q: {} for q in qs}
    wrote, read = {}, {}
    nd = [0]

    def wait(q, sem, val):
        if waited[q].get(sem, 0) < val:
            qs[q].wait_ge(T.sem[sem], val)
            waited[q][sem] = val

    def before(q, reads, writes):
        need = {}
        for k in list(reads) + list(writes):
            if k in wrote:
                s, v = wrote[k]
                need[s] = max(need.get(s, 0), v)
        for k in writes:
            for s, v in read.get(k, []):
                need[s] = max(need.get(s, 0), v)
        for s in sorted(need):
            wait(q, s, need[s])

    def after(reads, writes, mark):
        for k in writes:
            wrote[k] = mark
            read[k] = []
        for k in reads:
            assert k in wrote, k
            if k not in writes:
                read.setdefault(k, []).append(mark)

    def op(q, fn, reads, writes, adds=False):
        before(q, reads, [] if adds else writes)
        s = own[q]
        total[s] = total.get(s, 0) + 1
        fn(qs[q]).then_inc(T.sem[s], 1)
        after(reads, writes, (s, total[s]))

    def dma(q, fn, reads, writes, joins=False):
        before(q, reads, [] if joins else writes)
        nd[0] += 0 if joins else 1
        s = "d%d" % nd[0]
        total[s] = total.get(s, 0) + 16
        fn(qs[q]).then_inc(T.sem[s], 16)
        after(reads, writes, (s, total[s]))

    def send(fn, reads, count):
        before("g", reads, [])
        fn()
        total["loc"] = total.get("loc", 0) + count

    def arrive(sem, val, keys):
        total[sem] = val
        for k in keys:
            wrote[k] = (sem, val)
            read[k] = []

    def finish():
        for s in sorted(total):
            if max(waited[q].get(s, 0) for q in qs) < total[s]:
                wait("g", s, total[s])

    return op, dma, send, arrive, finish


def rank_program(g, core, T, topo):
    rank = T.rank_of(core)
    if rank is None:
        return
    op, dma, send, arrive, finish = tracker(g, T)
    mate = [T.cores[rank ^ s] for s in STEP]

    def eng(r):
        return topo.engines(core, mate[r])

    def remote(r, dst, src, sem, n):
        rid, pid = topo.addr(mate[r], core)
        g.remote_dma(dst, src, T.sem[sem], T.sem.loc, pid, rid, sum(1 << i for i in eng(r)[:n]))

    def ts(out, in0, s1, s2, o0, o1, reads, writes):
        if s2 is None:
            op("v", lambda q: q.tensor_scalar(out, in0, s1, None, o0), reads, writes)
        else:
            op("v", lambda q: q.tensor_scalar(out, in0, s1, s2, o0, o1), reads, writes)

    def tt(out, a, b, o, reads, writes):
        op("v", lambda q: q.tensor_tensor(out, a, b, o), reads, writes)

    def cp(out, in_, reads, writes):
        op("v", lambda q: q.tensor_copy(out, in_), reads, writes)

    def fill(ap, c, writes):
        op("v", lambda q: q.memset(ap, c), [], writes)

    def act(out, in_, reads, writes, func=F.Copy, **kw):
        op("s", lambda q: q.activation(out, in_, func, **kw), reads, writes)

    def iota(out, pattern, base, cm, writes, reads=()):
        op("g", lambda q: q.iota(out, pattern, base, cm, allow_small_or_imprecise_dtypes=True), list(reads), writes)

    def scan(out, d1, n, reads, writes):
        op("v", lambda q: q.tensor_tensor_scan(out, T.rst[:, 0:n], d1, 0.0, A.mult, A.add), ["rst"] + reads, writes)

    def turn(out, in_, reads, writes):
        op("v", lambda q: q.transpose(out, in_), reads, writes)

    def mm(bank, w, wp, a, x, xp, b, n, reads, start=True, stop=True):
        op("t", lambda q: q.matmul_mx(T.ps[:, 512 * bank:512 * bank + n], w[:, a:a + 128], wp[:, a:a + 128],
                                      x[:, b:b + n], xp[:, b:b + n], start, stop), reads, ["b%d" % bank], not start)

    def psum(bank, n=C):
        return T.ps[:, 512 * bank:512 * bank + n]

    def quant(src, a, q_, p_, c, n, reads, writes):
        op("v", lambda q: q.quantize_mx(q_[:, c:c + n], p_[:, c:c + n], src[:, a:a + 4 * n]), reads, writes)

    KN = ["q", "ad", "lo", "a2", "a3", "a3b", "w0", "w1", "w2", "w3", "i7", "y1", "y2", "al1", "al", "m1", "m2", "m3", "ma",
          "ys", "sp", "sp2", "bp", "u", "w", "x", "y", "z0", "z1", "f0", "f1", "dq", "h16", "sp3", "u2"]

    def k(name):
        i = KN.index(name)
        return T.k[:, i:i + 1]

    def b(d):
        return T.bf[:, d:d + 1]

    def e(i):
        return T.diag[:, i:i + 1]

    def lin(name, in_, scale, bias, reads):
        act(k(name), in_, reads, [name], F.Identity, scale=scale, bias=bias)

    def xkeys(r):
        return ["xq%d%d" % (r, j) for j in range(2)]

    HB = [[0, 1, 2, 3], [6, 7, 4, 5]]

    def h_products(r, j, c, n, keys, which=range(4)):
        for i in which:
            mm(HB[j][i], T.wq, T.wp, 128 * i, T["xq%d" % r], T["xp%d" % r], c, n, ["wq", "wp"] + keys)

    def h_tile(r, j, c, n):
        a = 4 * C * r + 4 * c
        for i in range(4):
            act(T.ht[:, a + i:a + 4 * n:4], psum(HB[j][i], n), ["b%d" % HB[j][i]], ["ht%d%d%d" % (r, j, i)], scale=0.03125)

    def h_send(r, j, c, m):
        n, key = len(eng(r)), "hq%d%d" % (r, j)
        quant(T.ht, 4 * C * r + 4 * c, T["hq%d" % r], T["hp%d" % r], c, m, ["ht%d%d%d" % (r, j, i) for i in range(4)], [key])
        send(lambda: remote(r, T["lq%d" % r][:, c:c + m].bitcast(dt.uint8), T["hq%d" % r][:, c:c + m].bitcast(dt.uint8), "ha%d" % r, n),
             [key], n)
        if c + m == C:
            send(lambda: remote(r, T["lp%d" % r][:, :], T["hp%d" % r][:, :], "ha%d" % r, n), ["hq%d0" % r, key], n)
            arrive("ha%d" % r, (j + 2) * n, ["lq%d" % r])

    def tau(r):
        return T.tau[:, C * r:C * r + C]

    def ta2(r):
        return T.ta2[:, C * r:C * r + C]

    def table(r, between, gap=lambda: None):
        z, o, s = "%d" % r, 144 * r, 128 * r
        tt(T.ox[:, o + 144:o + 288], tau(r).indirect(T.lst[:, 8:17]), T.ox[:, o:o + 144], A.mult,
           ["tau%d0" % r, "tau%d1" % r, "lst"] + (["ox0", "oxa", "oxb", "oxc"] if r == 0 else ["ox" + z]), ["ox%d" % (r + 1)])
        between()
        op("v", lambda q: q.tensor_tensor_scan(T.sc[:, o:o + 144], T.r18[:, :], T.ox[:, o + 144:o + 288], 0.0, A.mult, A.add),
           ["r18", "ox%d" % (r + 1)], ["sc" + z])
        gap()
        tt(T.src[:, s + 128:s + 256], ta2(r).indirect(T.lst[:, 0:8]), T.src[:, s:s + 128], A.mult,
           ["ta2%d0" % r, "ta2%d1" % r, "lst", "src" + z], ["src%d" % (r + 1)])
        ts(T.key[:, 8 * r:8 * r + 8], T.sc[:, o + 17:o + 144:18], 2.0 ** (r - 1), 63.5, A.mult, A.add, ["sc" + z], ["key" + z])
        gap()
        cp(T.tb[:, s:s + 128].indirect(T.key[:, 8 * r:8 * r + 8]), T.src[:, s + 128:s + 256], ["key" + z, "src%d" % (r + 1)], ["tb" + z])
        n = len(eng(r))
        send(lambda: remote(r, T.tl[:, s:s + 128], T.tb[:, s:s + 128], "ka" + z, n), ["tb" + z], n)
        arrive("ka" + z, n, ["tl" + z])

    def own_signs(r):
        z, s = "%d" % r, 128 * r
        if r == 0:
            act(T.cum[:, 0:128], ta2(0).indirect(T.lst[:, 0:8]), ["ta200", "lst"], ["cum0"])
        else:
            tt(T.cum[:, s:s + 128], ta2(r).indirect(T.lst[:, 0:8]), T.cum[:, s - 128:s], A.mult,
               ["ta2%d0" % r, "ta2%d1" % r, "lst", "cum%d" % (r - 1)], ["cum" + z])

    def pick(out, a, src, lst, n, reads, writes):
        cp(T[out % "q"][:, a:a + n].bitcast(dt.uint32), T[src % "q"][:, 0:C].bitcast(dt.uint32).indirect(lst), reads, [writes + "q"])
        act(T[out % "p"][:, a:a + n], T[src % "p"][:, 0:C].indirect(lst), reads, [writes + "p"])

    def f_pick(r, h):
        pick("f%%s%d" % r, C * h, "x%%s%d" % r, T.par[:, 18 * h:18 * h + 18], C, ["par"] + xkeys(r), "f%d%d" % (r, h))

    def f_products(r, h, which):
        for i in which:
            for j, (c, n) in enumerate(PART):
                mm(4 * j + i, T.eq, T.ep, 512 * h + 128 * i, T["fq%d" % r], T["fp%d" % r], C * h + c, n,
                   ["eq%d%d" % (h, i), "f%d%dq" % (r, h), "f%d%dp" % (r, h)], h == 0, False)

    WIDE = [(0, 192), (192, 96)]
    TURN = [(16, 0, 160), (0, 160, 192), (176, 352, 128), (160, 480, 160)]

    def turns(i, more=()):
        a, c, n = TURN[i]
        turn(T.zz[:, c:c + n], T.gg[:, a:a + n], ["gg0", "ggy", "ggz"] + (["gg1"] if i > 1 else []) + list(more), ["zz%d" % i])

    ORDER = [("g", 0), ("g", 1), ("t", 0), ("t", 1), ("s", 0), ("s", 1), ("t", 2), ("t", 3), ("l", 0), ("s", 2), ("s", 3), ("p", 0, 0),
             ("l", 1), ("p", 0, 1), ("p", 1, 0), ("p", 1, 1)]

    def new_state(r, between=lambda: None):
        z, s, x = "%d" % r, 128 * r, 4 * C * r
        tt(T.t1[:, s:s + 128], T.tl[:, s:s + 128].indirect(T.key[:, 8 * r:8 * r + 8]), T.cum[:, s:s + 128], A.mult,
           ["tl" + z, "key" + z, "cum" + z], ["t1" + z])
        between()

        def parts(j):
            c, n = WIDE[j]
            tt(T.gg[:, 16 + c:16 + c + n], T.t1[:, s:s + 128].indirect(T.no[:, c // 16:(c + n) // 16]), T.mask[:, c:c + n], A.mult,
               ["t1" + z, "no", "mask%d" % j], ["gg%d" % j])

        def sums(i):
            a, n = TURN[i][1:]
            scan(T.zs[:, a:a + n], T.zz[:, a:a + n], n, ["zz%d" % i], ["zs%d" % i])

        def lists(j):
            ts(T.mo[:, 64 * r + 32 * j:64 * r + 32 * j + 32], T.zs[:, 352 * j:352 + C * j].indirect(T.ls[:, 56 + 2 * j:58 + 2 * j]),
               4.0 ** r, 144.0, A.mult, A.add, ["zs%d" % (2 * j), "zs%d" % (2 * j + 1), "lsf%d" % j], ["mo%d%d" % (r, j)])

        def picks(j, h):
            c, n = PART[j]
            a = 64 * r + 32 * j + 16 * h
            pick("p%s" + z, C * h + c, "l%s" + z, T.mo[:, a:a + n // 16], n, ["mo%d%d" % (r, j), "lq" + z], "p%d%d%d" % (r, j, h))
            for i in range(4):
                mm(4 * j + i, T.eq, T.ep, 512 * h + 128 * i, T["pq" + z], T["pp" + z], C * h + c, n,
                   ["p%d%d%dq" % (r, j, h), "p%d%d%dp" % (r, j, h)], False, h == 1)

        def single(j):
            ts(T.ms[:, 16 * j:16 * j + 16], T.zs[:, 352 * j:352 + C * j].indirect(T.ls[:, 60 + 2 * j:61 + 2 * j]),
               4.0 ** r, 144.0, A.mult, A.add, ["zs%d" % (2 * j), "zs%d" % (2 * j + 1), "lsg%d" % j], ["ms%d" % j])

        def number(j, i):
            c, n = PART[j]
            out, key, bank = T.xt[:, x + 4 * c + i:x + 4 * (c + n):4], "xt%d%d%d" % (r, j, i), 4 * j + i
            if r == 0:
                tt(out, T.db[:, C * i:C * i + C].indirect(T.ms[:, 16 * j:16 * j + n // 16]), T.fc[:, C * i + c:C * i + c + n], A.add,
                   ["db%d" % i, "fc%d" % i, "ms%d" % j], [key])
            elif i % 2 == j:
                ts(out, psum(bank, n), 0.5, None, A.mult, None, ["b%d" % bank], [key])
            else:
                act(out, psum(bank, n), ["b%d" % bank], [key], scale=0.5)

        def codes(j):
            c, n = PART[j]
            quant(T.xt, x + 4 * c, T["xq%d" % (r + 1)], T["xp%d" % (r + 1)], c, n, ["xt%d%d%d" % (r, j, i) for i in range(4)],
                  ["xq%d%d" % (r + 1, j)])

        rest = [("n", 0, i) for i in range(4)] + [("c", 0)] + [("n", 1, i) for i in range(4)] + [("c", 1)]
        if r == 0:
            order = ORDER[:8] + [("m", 0)] + ORDER[9:11] + rest[:1] + [("m", 1)] + rest[1:4] + rest[5:6] + rest[4:5] + rest[6:]
        else:
            order = ORDER + ([("m", 0), ("m", 1)] if r == R - 1 else []) + rest
        for fn, *a in order:
            {"g": parts, "t": turns, "s": sums, "l": lists, "p": picks, "m": single, "n": number, "c": codes}[fn](*a)

    dma("y", lambda q: q.dma_start(T.sei[:, 0:18], T.se[:, :]), [], ["sei"])
    dma("y", lambda q: q.dma_start(T.xin[:, :], T.x[:, :]), [], ["xin"])
    dma("y", lambda q: q.dma_start(T.wq[:, :].bitcast(dt.uint8), T.wc[:, :]), [], ["wq"])
    dma("y", lambda q: q.dma_start(T.wp[:, :], T.ws[:, :]), [], ["wp"])
    dma("y", lambda q: q.dma_start(T.uin[:, :], T.u[:, :]), [], ["uin"])

    op("g", lambda q: q.iota(T.pi[:, :], [[0, 1]], 0, 1), [], ["pi"])
    iota(T.ij[:, :], [[2, C]], -C, 0, ["ij"])
    iota(T.t16[:, :], [[0, 18], [1, 16]], 0, 0, ["t16"])
    iota(T.kg[:, :], [[1, 20]], 0, 0, ["kg"])
    iota(T.c2[:, 0:2], [[1, 2]], C, 0, ["c2"])
    iota(T.gg[:, 16:160], [[1, 8], [8, 18]], -16, 0, ["gg0"])
    iota(T.tg[:, :], [[1, 16], [0, 8]], 0, 0, ["tg"])
    iota(T.gg[:, 16:160:18], [[0, 8]], 1, 0, ["xfa"], ["gg0"])
    iota(T.gg[:, 17:160:18], [[0, 4], [1, 2]], 2, 0, ["xfb"], ["gg0"])
    iota(T.gg[:, 18:160:18], [[0, 2], [1, 4]], 4, 0, ["xfc"], ["gg0"])
    iota(T.bg[:, :], [[1, 8], [0, 2]], 0, 0, ["bg"])
    iota(T.off[:, :], [[1, 128]], 0, -1, ["io"])
    iota(T.c2[:, 2:4], [[2, 2]], 2, 0, ["c3"])
    iota(T.c2[:, 4:5], [[0, 1]], 8, 0, ["c4"])
    iota(T.now[:, 1:296], [[0, 295]], 0, 0, ["nw0"])
    W = [16, 32, 64, 1, 8, 4, 2, 128]
    iota(T.now[:, 0:1], [[0, 1]], 128 + 2048 * W[0], 0, ["nw1"])
    for d in range(1, 8):
        n = max(1, 2 ** (d - 4))
        c = 16 * (d - 1) if d < 5 else 16 * (n + 2)
        iota(T.pk[:, c:c + 16 * n], [[16 // n, n], [1, 2], [16, 8]], 128 * (d + 1) + 2048 * W[d], 0, ["pk%d" % d])

    fill(T.bo[:, 0:130], 0.0, ["bo0"])
    for i in range(1, 4):
        act(T.bo[:, 130 * i:130 * i + 130], T.bo[:, 0:130], ["bo0"], ["bo%d" % i])
    fill(T.rb[:, 0:16], -float(C), ["rb0"])
    fill(T.v0[:, 0:2], -float(C), ["v00"])
    fill(T.gg[:, 0:16], 0.0, ["ggy"])
    ts(T.bi[:, 5:6], T.pi[:, :], 15, None, A.bitwise_and, None, ["pi"], ["qi"])
    BI = ["bi%d" % d for d in range(5)]
    for d in range(5):
        ts(T.bi[:, d:d + 1], T.pi[:, :], d, 1, A.arith_shift_right, A.bitwise_and, ["pi"], [BI[d]])
    cp(k("q"), T.bi[:, 5:6], ["qi"], ["q"])
    cp(T.bf[:, :], T.bi[:, 0:5], BI, ["bf"])
    fill(T.gg[:, 160:320], 0.0, ["ggz"])
    ts(k("ad"), k("q"), 0.0, 576.0, A.is_equal, A.mult, ["q"], ["ad"])
    for i in range(2):
        act(T.cw[:, i:2 * C:2], T.ij[:, :], ["ij"], ["cw%d" % i])
    ts(k("x"), b(0), b(4), None, A.not_equal, None, ["bf"], ["x"])
    ts(k("y"), k("q"), b(4), 16.0, A.subtract, A.mult, ["q", "bf"], ["y"])
    ts(T.bc[:, :], T.bf[:, 0:4], float(C), None, A.add, None, ["bf"], ["bc"])
    ts(k("y1"), k("q"), b(4), 16.0, A.add, A.mult, ["q", "bf"], ["y1"])
    for j, n in enumerate((176.0, 144.0)):
        ts(k("z%d" % j), k("x"), n, k("y"), A.mult, A.add, ["x", "y"], ["z%d" % j])
    ts(k("a2"), b(3), 2.0, b(0), A.mult, A.add, ["bf"], ["a2"])
    ts(k("a3b"), b(3), 2.0, b(2), A.mult, A.add, ["bf"], ["a3b"])
    for j, n in enumerate((335.0, 271.0)):
        ts(k("f%d" % j), k("z%d" % j), 15.0, n, A.add, A.min, ["z%d" % j], ["f%d" % j])
    ts(k("a3"), k("a3b"), 2.0, b(0), A.mult, A.add, ["bf", "a3b"], ["a3"])
    ts(T.diag[:, :], T.t16[:, :], k("q"), None, A.is_equal, None, ["t16", "q"], ["diag"])
    act(T.rst[:, :], T.t16[:, :], ["t16"], ["rst"], F.Sign)
    ts(T.ls[:, 0:8], T.kg[:, 0:8], 16.0, None, A.mult, None, ["kg"], ["lsu"])
    ts(k("ma"), e(8), e(10), 0.5, A.add, A.mult, ["diag"], ["ma"])
    ts(T.ls[:, 56:58], T.kg[:, 0:2], 16.0, k("f0"), A.mult, A.add, ["kg", "f0"], ["lsf0"])

    ts(T.seu[:, 0:1], T.sei[:, 0:1], k("ad"), None, A.add, None, ["sei", "ad"], ["seu0"])
    cp(T.seu[:, 1:18], T.sei[:, 1:18], ["sei"], ["seu1"])
    ts(k("sp"), e(10), e(11), None, A.add, None, ["diag"], ["sp"])
    ts(k("m1"), e(7), 4.0, e(6), A.mult, A.add, ["diag"], ["m1"])
    cp(T.cw[:, 0:592].indirect(T.seu[:, 0:18]), T.ij[:, :], ["seu0", "seu1", "ij", "cw0", "cw1"], ["cw"])

    act(T.cm[:, 10:11], b(0), ["bf"], ["cm3"])
    for d, s in enumerate((0, 3, 2, 1)):
        lin("w%d" % d, b(s), 2.0 ** (4 - d), -2.0 ** (3 - d), ["bf"])
    lin("al1", e(6), 0.5, e(7), ["diag"])
    lin("m3", k("q"), 1.0, -0.375, ["q"])
    lin("i7", k("q"), 8.0, 128.0, ["q"])
    lin("al", e(5), 0.25, k("al1"), ["diag", "al1"])
    lin("m2", k("m1"), 1.0, k("m3"), ["m1", "m3"])
    lin("y2", b(0), -8.0, k("y1"), ["bf", "y1"])
    lin("ys", b(3), -0.5, 0.5, ["bf"])
    lin("bp", k("sp"), -1.0, 1.0, ["sp"])
    lin("h16", b(4), 16.0, 0.0, ["bf"])

    todo = []

    def later(fn, *a):
        todo.append((fn, a))

    def some(n=1):
        for i in range(n):
            if todo:
                fn, a = todo.pop(0)
                fn(*a)

    def scorer():
        cp(T.ur[:, :].bitcast(dt.uint32), T.uq[:, 0:128].bitcast(dt.uint32).indirect(T.ls[:, 0:8]), ["uq", "lsu"], ["ur"])
        act(T.urp[:, :], T.up[:, 0:128].indirect(T.ls[:, 0:8]), ["uq", "lsu"], ["urp"])
        mm(4, T.ur, T.urp, 0, T.xq0, T.xp0, 0, C, ["ur", "urp"] + xkeys(0))

    later(turns, 0, ["xfa", "xfb", "xfc"])
    later(turns, 1, ["xfa", "xfb", "xfc"])
    later(ts, T.wh[:, 0:16], T.tg[:, 0:16], 1.0, k("w0"), A.is_equal, A.mult, ["tg", "w0"], ["wh0"])
    later(cp, T.ls[:, 16:32], T.zz[:, 0:352].indirect(T.ls[:, 56:57]), ["zz0", "zz1", "lsf0"], ["lsv"])
    for d, a in ((1, b(0)), (2, k("a2")), (3, k("a3"))):
        later(ts, T.wh[:, 8 * 2 ** d:16 * 2 ** d], T.tg[:, 0:8 * 2 ** d], a, k("w%d" % d), A.is_equal, A.mult,
              ["tg", "bf", "a2", "a3", "w%d" % d], ["wh%d" % d])
    later(quant, T.uin, 0, T.uq, T.up, 0, 128, ["uin"], ["uq"])
    later(ts, T.xi[:, :], T.bg[:, :], k("al"), k("m2"), A.mult, A.add, ["bg", "al", "m2"], ["xi"])
    later(scorer)
    later(ts, T.ls[:, 8:16], T.kg[:, 0:8], k("i7"), None, A.add, None, ["kg", "i7"], ["ls7"])
    later(ts, T.ls[:, 32:48], T.xi[:, :], 16.0, None, A.mult, None, ["xi"], ["lsx"])
    later(ts, T.ls[:, 48:56], T.kg[:, 0:8], k("y2"), None, A.add, None, ["kg", "y2"], ["lsy"])
    later(ts, T.pn[:, :], T.seu[:, :], 0.5, 0.25, A.mult, A.subtract, ["seu0", "seu1"], ["pn"])
    later(ts, T.si[:, :], T.sei[:, :], 1, None, A.bitwise_and, None, ["sei"], ["si"])
    later(ts, T.k[:, 36:39], T.c2[:, 2:5], k("q"), None, A.is_le, None, ["q", "c3", "c4"], ["gq"])
    later(ts, T.sm[:, :], T.si[:, :], 2048.0, None, A.subtract, None, ["si"], ["sm"])
    later(ts, T.pu[:, :], T.sei[:, :], 0.5, 0.25, A.mult, A.subtract, ["sei"], ["pu"])

    LO = {2: 0, 3: 2, 4: 4, 5: 6, 6: 8, 7: 12}
    RB = {2: 17, 3: 33, 4: 49, 5: 65, 6: 97, 7: 161}

    def child(t):
        n = max(1, 2 ** t // 16)
        return T.cw[:, 0:2 * C].indirect(T.lo[:, LO[t]:LO[t] + n]), ["cw"] + (["lo%da" % t, "lo%db" % t] if t > 5 else ["lo%d" % t])

    def lanes(t, n1=1, n2=1, n3=1):
        kid, deps = child(t)
        n, o = max(16, 2 ** t), RB[t]
        tt(T.gm[:, o - 17:o - 17 + n], kid, T.diag[:, 0:n], A.mult, deps + ["diag"], ["gm%d" % t])
        some(n1)
        scan(T.rb[:, o:o + n], T.gm[:, o - 17:o - 17 + n], n, ["gm%d" % t], ["rb%d" % t])
        some(n2)
        ends = T.rb[:, o + 15:o + n:16]
        if t < 4:
            ts(T.lo[:, LO[t + 1]:LO[t + 1] + 1], ends, T.bc[:, t:t + 1], None, A.add, None, ["rb%d" % t, "bc"], ["lo%d" % (t + 1)])
        elif t == 4:
            ts(T.lo[:, 6:8], T.c2[:, 0:2], ends, None, A.add, None, ["rb4", "c2"], ["lo5"])
        elif t < 7:
            for s in range(2):
                ts(T.lo[:, LO[t + 1] + s:LO[t + 1] + n // 8:2], ends, float(C + s), None, A.add, None, ["rb%d" % t], ["lo%d%s" % (t + 1, "ab"[s])])
        some(n3)

    def whole(t):
        kid, deps = child(t)
        act(T.v0[:, 2 ** t:2 ** t + max(16, 2 ** t)], kid, deps, ["v0t" if t < 5 else "v0%d" % t])

    d1 = T.dw[:, 19:20]
    quant(T.xin, 0, T.xq0, T.xp0, 0, C, ["xin"], xkeys(0))
    ts(d1, T.cw[:, 1:2], T.cw[:, 0:1], T.cm[:, 10:11], A.subtract, A.mult, ["cw", "cm3"], ["d1"])
    act(T.wd[:, :], T.cw[:, 0:2 * C:2], ["cw", "ma"], ["wd"], scale=k("ma"))
    act(T.wt[:, :], T.cw[:, 1:2 * C:2], ["cw"], ["wt"], scale=0.5)
    for i in (9, 11):
        dma("y", lambda q: q.dma_start(T.wd[i:128:16, :], T.wt[i:128:16, :]), ["wd", "wt"], ["wd%d" % i])
    for i in range(16):
        h, p = i // 8, 16 * (i % 8)
        s0 = p - p % 32 + 16 * h
        dma("y", lambda q: q.dma_start(T.pa[p:p + 16, 18 * h:18 * h + 18], T.se[s0:s0 + 16, :]), [], ["pa"], i > 0)
    dma("y", lambda q: q.dma_start(T.vin[:, :], T.v[:, :]), [], ["vin"])
    act(T.v0[:, 2:4], T.cw[:, 0:2], ["cw"], ["v01"])
    h_products(0, 0, 0, C, xkeys(0))
    h_tile(0, 0, 0, C)
    some(2)
    ts(T.lo[:, 0:1], T.cw[:, 0:1], d1, T.bc[:, 1:2], A.add, A.add, ["d1", "cw", "bc"], ["lo2"])
    ts(T.rb[:, 16:17], d1, T.cw[:, 0:1], None, A.add, None, ["d1", "cw"], ["rb1"])
    lanes(2)
    lanes(3)
    lanes(4)
    whole(2)
    act(T.ox[:, 0:144], T.wh[:, :].indirect(T.ls[:, 16:25]), ["wh0", "wh1", "wh2", "wh3", "lsv"], ["ox0"])
    iota(T.ox[:, 0:144:18], [[0, 4], [128, 2]], -64, 0, ["oxa"], ["ox0"])
    iota(T.ox[:, 1:144:18], [[0, 2], [64, 2], [0, 2]], -32, 0, ["oxb"], ["ox0"])
    iota(T.ox[:, 2:144:18], [[32, 2], [0, 4]], -16, 0, ["oxc"], ["ox0"])
    whole(3)
    act(T.off[:, :], T.off[:, :], ["io"], ["io"], F.Abs)
    lanes(5)
    whole(4)
    act(T.bo[:, 3:515:4], T.off[:, :], ["io", "bo1", "bo2", "bo3"], ["bo", "bo0"], F.Relu, scale=-1.0, bias=1.0)
    whole(5)
    lanes(6, 2, 2, 0)
    whole(6)
    whole(7)
    h_send(0, 0, 0, C)

    def whole_tile(i):
        quant(T.bo, 3 - i, T.cq, T.cs, 128 * i, 128, ["bo"], ["cq%d" % i])

    later(whole_tile, 0)
    lanes(7, 99, 0, 0)
    RBS = ["rb%d" % t for t in range(8)]
    act(tau(0), psum(4), ["b4"], ["tau00", "tau01"], F.Sign, bias=2.0 ** -100)
    lin("dq", k("q"), 2.0, 720.0, ["q"])
    act(T.xx[:, :], T.rb[:, 0:289].indirect(T.ls[:, 32:48]), RBS + ["lsx"], ["xx"])
    act(T.dum[:, :], T.kg[:, 0:18], ["kg", "dq"], ["dum"], F.Identity, scale=32.0, bias=k("dq"))
    act(T.nn[:, 0:18], T.rb[:, 16:289:16], RBS, ["n1"], F.Identity, bias=400.0)

    def pair(fn):
        later(lambda: [fn(s) for s in range(2)])

    later(tt, T.same[:, 1:5], T.rb[:, 16:65:16], T.rb[:, 0:49:16], A.is_equal, RBS, ["sa0"])
    pair(lambda s: tt(T.same[:, 5 + s:19:2], T.rb[:, 80 + 16 * s:289:32], T.rb[:, 64:161:16], A.is_equal, RBS, ["sa%d" % (s + 1)]))
    later(op, "v", lambda q: q.tensor_tensor_scan(T.nr[:, 1:5], T.same[:, 1:5], T.same[:, 1:5], 0.0, A.max, A.max), ["sa0"], ["nr4"])
    later(ts, T.nr[:, 5:7], T.same[:, 5:7], T.nr[:, 4:5], None, A.max, None, ["sa1", "sa2", "nr4"], ["nr5"])
    later(tt, T.nr[:, 1:4], T.nr[:, 1:4], T.k[:, 36:39], A.max, ["nr4", "gq"], ["nr3"])
    pair(lambda s: tt(T.nr[:, 7 + s:11:2], T.same[:, 7 + s:11:2], T.nr[:, 5:7], A.max, ["sa1", "sa2", "nr5"], ["nr6%d" % s]))
    pair(lambda s: tt(T.nr[:, 11 + s:19:2], T.same[:, 11 + s:19:2], T.nr[:, 7:11], A.max, ["sa1", "sa2", "nr60", "nr61"], ["nr7%d" % s]))
    later(tt, T.nn[:, 18:36], T.nr[:, 1:19], T.dum[:, :], A.mult, ["nr3", "nr4", "nr5", "nr60", "nr61", "nr70", "nr71", "dum"], ["n2"])
    later(tt, T.nn[:, 36:54], T.nn[:, 0:18], T.nn[:, 18:36], A.max, ["n1", "n2"], ["n3"])
    later(ts, T.nu[:, :], T.nn[:, 36:54], 0.5, 56.0, A.mult, A.subtract, ["n3"], ["nu"])

    whole_tile(1)
    some()
    tt(T.lm[:, :], T.v0[:, :].indirect(T.ls[:, 8:25]), T.diag[:, 0:272], A.mult,
       ["v00", "v01", "v0t", "v05", "v06", "v07", "ls7", "lsv", "diag"], ["lm"])
    some(2)
    scan(T.lsc[:, :], T.lm[:, :], 272, ["lm"], ["lsc"])
    turn(T.yy[:, :], T.xx[:, :], ["xx"], ["yy"])
    act(T.r18[:, :], T.gg[:, 16:160], ["gg0", "xfa", "xfb", "xfc"], ["r18"], F.Sign, bias=-1.0)
    act(T.yg[:, :], T.yy[:, :].indirect(T.ls[:, 48:56]), ["yy", "lsy", "ys"], ["yg"], scale=k("ys"))
    act(ta2(0), tau(0), ["tau00", "sp", "bp"], ["ta200", "ta201"], F.Identity, scale=k("sp"), bias=k("bp"))
    ts(T.lst[:, 0:17], T.lsc[:, 15:272:16], 0.5, 144.0, A.mult, A.add, ["lsc"], ["lst"])
    some()
    whole_tile(2)
    table(0, lambda: (some(2), tt(T.src[:, 0:128], T.wd[:, :].indirect(T.lst[:, 0:8]), T.yg[:, :], A.add,
                                  ["wd", "wd9", "wd11", "lst", "yg"], ["src0"]), some()), some)
    some(99)
    whole_tile(3)

    def unpack(name, q_, p_, bank, keys, which):
        for i in which:
            mm(bank + i, T.cq, T.cs, 128 * i, q_, p_, 0, C, ["cq%d" % i] + keys)
            act(T[name][:, C * i:C * i + C], psum(bank + i), ["b%d" % (bank + i)], [name + "%d" % i], scale=0.5)

    def parents(i):
        act(T.fc[:, C * i:C * i + C], T.fb[:, C * i:C * i + C].indirect(T.pu[:, :]), ["fb%d" % i, "pu"], ["fc%d" % i])

    iota(T.be[:, :], [[0, 520]], 0, 0, ["bez"])
    lin("lo", b(4), -1.0, 1.0, ["bf"])
    lin("u", e(8), 1.0, e(9), ["diag"])
    lin("w", e(11), -1.0, e(10), ["diag"])
    own_signs(0)
    lin("u2", k("u"), 0.5, 0.0, ["u"])
    unpack("fb", T.xq0, T.xp0, 4, xkeys(0), range(3))
    act(T.cm[:, 8:9], k("w"), ["u2", "w"], ["cm1"], F.Identity, scale=0.5, bias=k("u2"))
    act(T.cm[:, 9:10], k("w"), ["u2", "w"], ["cm2"], F.Identity, scale=-0.5, bias=k("u2"))
    act(T.cm[:, 0:8], T.diag[:, 0:8], ["diag"], ["cm0"])
    unpack("fb", T.xq0, T.xp0, 4, xkeys(0), [3])
    act(T.bo[:, 3:515:4], T.off[:, :], ["io", "bf"], ["bo"], F.Relu, scale=-1.0, bias=b(4))
    parents(0)
    parents(1)
    act(T.be[:, 3:515:4], T.off[:, :], ["io", "lo", "bez"], ["be"], F.Relu, scale=-1.0, bias=k("lo"))
    unpack("db", T.lq0, T.lp0, 0, ["lq0"], range(2))
    later(ts, T.ls[:, 60:63:2], T.k[:, 29:31], k("h16"), None, A.add, None, ["f0", "f1", "h16"], ["lsg0", "lsg1"])
    later(ts, T.ls[:, 58:60], T.kg[:, 0:2], 16.0, k("f1"), A.mult, A.add, ["kg", "f1"], ["lsf1"])
    later(ts, T.par[:, :], T.pa[:, :], 0.5, 0.25, A.mult, A.subtract, ["pa"], ["par"])
    for h in (1, 0):
        for i in range(4):
            later(quant, T.bo if h else T.be, 3 - i, T.eq, T.ep, 512 * h + 128 * i, 128, ["bo" if h else "be"], ["eq%d%d" % (h, i)])
    cp(T.now[:, :].indirect(T.nu[:, 0:18]), T.pk[:, :], ["nu", "nw0", "nw1"] + ["pk%d" % d for d in range(1, 8)], ["now"])
    some(2)
    tt(T.nm[:, :], T.now[:, 0:296].indirect(T.pn[:, 0:18]), T.diag[:, :], A.mult, ["now", "pn", "diag"], ["nm"])
    some(2)
    scan(T.ns[:, :], T.nm[:, :], C, ["nm"], ["ns"])
    some()
    ts(T.dl[:, :], T.ns[:, 15:C:16], 2.0 ** -11, 0.28, A.mult, A.subtract, ["ns"], ["dl"])
    some()
    tt(T.dw[:, 0:18], T.dl[:, :], T.sm[:, :], A.mult, ["dl", "sm"], ["dw"])
    some()
    tt(T.cd[:, :], T.dw[:, 0:18], T.ns[:, 15:C:16], A.add, ["dw", "ns"], ["cd"])
    some()
    ts(T.cl[:, :], T.cd[:, :], 2.0 ** -7, 0.496, A.mult, A.subtract, ["cd"], ["cl"])
    ts(T.ni[:, :], T.cd[:, :], 127, None, A.bitwise_and, None, ["cd"], ["ni"])
    for j, (c, n) in enumerate(WIDE):
        act(T.mask[:, c:c + n], T.cm[:, 0:10].indirect(T.cl[:, c // 16:(c + n) // 16]), ["cm0", "cm1", "cm2", "cl"], ["mask%d" % j])
    parents(2)
    unpack("db", T.lq0, T.lp0, 0, ["lq0"], range(2, 4))
    parents(3)
    lin("sp3", k("bp"), -2.0 ** 80, 0.0, ["bp"])
    new_state(0, lambda: (cp(T.no[:, :], T.ni[:, :], ["ni"], ["no"]), some()))

    for r in (1, 2):
        z = "%d" % r
        for j, (c, n) in enumerate(PART):
            key, a, bank = "xq%d%d" % (r, j), C * r + c, "b%d" % (4 + j)
            h_products(r, j, c, n, [key], range(0, 2 - 2 * j))
            mm(4 + j, T.ur, T.urp, 0, T["xq" + z], T["xp" + z], c, n, ["ur", "urp", key])
            ts(T.tau[:, a:a + n], psum(4 + j, n), 0.0, 0.5, A.is_ge, A.subtract, [bank], ["tau%d%d" % (r, j)])
            ts(T.ta2[:, a:a + n], psum(4 + j, n), k("sp3"), 0.5, A.is_ge, A.subtract, [bank, "sp3"], ["ta2%d%d" % (r, j)])
            h_products(r, j, c, n, [key], range(2 - 2 * j, 4))
            h_tile(r, j, c, n)
        table(r, lambda: h_send(r, 0, *PART[0]))
        h_send(r, 1, *PART[1])
        own_signs(r)
        for h in range(2):
            f_pick(r, h)
            some(99)
            f_products(r, h, range(4))
        if r == 2:
            quant(T.vin, 0, T.vq, T.vp, 0, 128, ["vin"], ["vq"])
        new_state(r)

    xq, xp = T["xq%d" % R], T["xp%d" % R]
    for j, (c, n) in enumerate(PART):
        mm(j, T.vq, T.vp, 0, xq, xp, c, n, ["vq", "xq%d%d" % (R, j)])
        (cp if j else act)(T.ys[:, c:c + n], psum(j, n), ["b%d" % j], ["ys%d" % j])
        dma("y", lambda q: q.dma_start(T.oc[:, 4 * c:4 * (c + n)], xq[:, c:c + n].bitcast(dt.uint8)), ["xq%d%d" % (R, j)], [])
        if j == 0:
            dma("y", lambda q: q.dma_start(T.y[:, c:c + n], T.ys[:, c:c + n]), ["ys0"], [])
    for j, (c, n) in enumerate(PART):
        act(T.ims[:, c:c + n], T.ij[:, :].indirect(T.ms[:, 16 * j:16 * j + n // 16]), ["ij", "ms%d" % j], ["ims%d" % j], F.Identity,
            scale=0.5, bias=144.0)
    for i in range(4):
        dma("y", lambda q: q.dma_start(T.osc[4 * i:4 * i + 4, :], xp[32 * i:32 * i + 4, :]), xkeys(R), [])
    dma("s", lambda q: q.dma_start(T.y[:, c:c + n], T.ys[:, c:c + n]), ["ys1"], [])
    dma("y", lambda q: q.dma_start(T.im[:, :], T.ims[0:128:16, :]), ["ims0", "ims1"], [])
    finish()
